import numpy as np
import ml_dtypes


def mxq(x, axis, fmt="e4m3"):
    dtype, down = {"e4m3": (ml_dtypes.float8_e4m3fn, 7), "e5m2": (ml_dtypes.float8_e5m2, 14)}[fmt]
    v = np.moveaxis(np.asarray(x, np.float32).astype(ml_dtypes.bfloat16).astype(np.float64), axis, -1)
    blocks = v.reshape(v.shape[:-1] + (-1, 32))
    amax = np.abs(blocks).max(-1, keepdims=True)
    byte = np.maximum(np.where(amax > 0, np.frexp(amax)[1] - 1 + 127, 0) - down, 1)
    scale = np.exp2(byte - 127.0)
    codes = (blocks / scale).astype(np.float32).astype(dtype).astype(np.float64)
    return np.moveaxis((codes * scale).reshape(v.shape), -1, axis)


WIDE = False


def mx_kscale(k):
    if not WIDE:
        return np.ones(k)
    levels = np.array([10, -10, 5, -5, 0])
    if k % 512:
        return np.exp2(np.random.permutation(np.resize(levels, k // 32))).repeat(32)
    a = np.empty((k // 512, 16))
    for p in range(k // 512):
        a[p, :8] = np.random.permutation(np.resize(levels, 8))
        for g in range(8):
            far = levels[np.abs(levels - a[p, g]) >= 10]
            a[p, g + 8] = far[np.random.randint(len(far))]
    return np.exp2(a.ravel()).repeat(32)


def f64(x):
    return np.asarray(x).astype(np.float64)


def striped(idx):
    return np.tile(idx.reshape(-1, 16).T, (8, 1)).astype(np.uint16)


def unstriped(offs):
    return offs[:16].T.reshape(-1).astype(np.int64)


E2M1 = np.array([0.0, 0.5, 1.0, 1.5, 2.0, 3.0, 4.0, 6.0, -0.0, -0.5, -1.0, -1.5, -2.0, -3.0, -4.0, -6.0])


def pack_weight(w, fmt):
    k, n = w.shape
    w = f64(np.asarray(w, np.float32).astype(ml_dtypes.bfloat16)).reshape(k // 32, 32, n)
    amax = np.abs(w).max(1)
    if fmt == "e4m3":
        byte = np.frexp(amax)[1] - 1 + 127 - 7
    else:
        mant, ex = np.frexp(amax / 6.0)
        byte = np.where(mant > 0.5, ex, ex - 1) + 127
    byte = np.clip(np.where(amax > 0, byte, 1), 1, 254)
    scaled = (w * np.exp2(127.0 - byte)[:, None, :]).reshape(k, n).astype(np.float32)
    by_word = np.ascontiguousarray(scaled.reshape(k // 512, 128, 4, n).transpose(0, 1, 3, 2))
    if fmt == "e4m3":
        words = by_word.astype(ml_dtypes.float8_e4m3fn).view(np.uint8)
    else:
        c = by_word.astype(ml_dtypes.float4_e2m1fn).view(np.uint8) & 0xF
        words = (c[..., 0::2] | (c[..., 1::2] << 4)).reshape(k // 512, 128, 2 * n)
    return np.ascontiguousarray(words), np.ascontiguousarray(byte.astype(np.uint8).reshape(k // 512, 16, n))


def unpack_weight(words, scales, fmt):
    g, _, n = scales.shape
    words = np.ascontiguousarray(words).reshape(g, 128, n, -1)
    if fmt == "e4m3":
        vals = words.view(ml_dtypes.float8_e4m3fn).astype(np.float64)
    else:
        nib = np.empty((g, 128, n, 4), np.uint8)
        nib[..., 0::2] = words & 0xF
        nib[..., 1::2] = words >> 4
        vals = E2M1[nib]
    vals = vals * np.repeat(np.exp2(scales.astype(np.float64) - 127.0), 8, axis=1)[..., None]
    return vals.transpose(0, 1, 3, 2).reshape(g * 512, n)


def gelu(v):
    return 0.5 * v * (1.0 + np.tanh(np.sqrt(2.0 / np.pi) * (v + 0.044715 * v**3)))


K, T, T2, S, S2, N = 512, 2048, 4096, 1024, 1536, 512

def setup_inputs():
    n = np.random.standard_normal
    s = mx_kscale(K)[:, None]
    u = mx_kscale(S)[:, None]
    tab_words, tab_scales = pack_weight(n((K, T)) * s, "e4m3")
    tab2_words, tab2_scales = pack_weight(n((K, T2)) / np.sqrt(K) / s, "e4m3")
    wb_words, wb_scales = pack_weight(0.8 * n((S, N)) / np.sqrt(S) / u, "e2m1")
    wd = (0.5 * n((S, N)) / np.sqrt(S) / u).astype(np.float32)
    return {
        "tab_words": tab_words, "tab_scales": tab_scales,
        "tab2_words": tab2_words, "tab2_scales": tab2_scales,
        "offs": striped(np.random.permutation(T)[:S]),
        "offs2": striped(np.random.permutation(T2)[:S2]),
        "wt": (np.exp(0.3 * n(S)) * u[:, 0]).astype(np.float32),
        "wb_words": wb_words, "wb_scales": wb_scales,
        "wd": wd,
        "b": (0.5 * n(N)).astype(np.float32),
    }

def reference(tab_words, tab_scales, tab2_words, tab2_scales, offs, offs2, wt, wb_words, wb_scales, wd, b):
    v = unpack_weight(tab_words, tab_scales, "e4m3")[:, unstriped(offs)]
    v2 = unpack_weight(tab2_words, tab2_scales, "e4m3")[:, unstriped(offs2)]
    A = v.T @ v2
    z = f64(wt)[:, None] * np.sqrt(np.abs(A))
    zq = mxq(z, 0, "e4m3")
    wb = unpack_weight(wb_words, wb_scales, "e2m1")
    wdq = mxq(f64(wd), 0, "e4m3")
    y = wb.T @ zq + wdq.T @ zq
    return np.tanh(y + f64(b)[:, None])

@@ -1,0 +1,264 @@
+from contextlib import ExitStack
+
+import concourse.mybir as mybir
+
+K, T, T2, S, S2, N = 512, 2048, 4096, 1024, 1536, 512
+FLOPS = 2 * K * S * S2 + 2 * 2 * S * N * S2
+
+F32 = mybir.dt.float32
+BF16 = mybir.dt.bfloat16
+I32 = mybir.dt.int32
+U32 = mybir.dt.uint32
+U16 = mybir.dt.uint16
+U8 = mybir.dt.uint8
+FP8X4 = mybir.dt.float8_e4m3fn_x4
+FP4X4 = mybir.dt.float4_e2m1fn_x4
+ACT = mybir.ActivationFunctionType
+ALU = mybir.AluOpType
+
+P = 128
+PACK = 4
+PASS = P * PACK
+PASSES = S // PASS
+CHUNK = 512
+CHUNKS = S2 // CHUNK
+NBLOCKS = N // P
+LIST_ROWS = 16
+QUAD = 32
+LINE = 4
+
+
+def load_scale_rows(queue, plane, rows):
+    for r in range(PACK):
+        queue.dma_start(out=plane[r:P:QUAD].bitcast(I32), in_=rows[r :: PACK].bitcast(I32))
+
+
+def tile_list_visual_word_hash_kernel(
+    tc, tab_words, tab_scales, tab2_words, tab2_scales, offs, offs2, wt, wb_words, wb_scales, wd, b, out
+):
+    nc = tc.nc
+    with ExitStack() as ctx:
+        held = ctx.enter_context(tc.tile_pool(name="held", bufs=1))
+        ring = ctx.enter_context(tc.tile_pool(name="ring", bufs=2))
+        psum = ctx.enter_context(tc.psum_pool(name="psum", bufs=1))
+
+        def bank(number, shape):
+            return psum.tile(shape, F32, name="bank%d" % number)
+
+        word_list = held.tile([P, S // LIST_ROWS], U16, name="word_list")
+        image_list = held.tile([P, S2 // LIST_ROWS], U16, name="image_list")
+        nc.sync.dma_start(word_list[:], offs)
+        nc.sync.dma_start(image_list[:], offs2)
+
+        t1_words = held.tile([P, T], U32, name="t1_words", align_bytes=64)
+        t2_words = held.tile([P, T2], U32, name="t2_words", align_bytes=64)
+        nc.sync.dma_start(out=t1_words[:].bitcast(I32), in_=tab_words[0].rearrange("p t i -> p (t i)").bitcast(I32))
+        nc.sync.dma_start(out=t2_words[:].bitcast(I32), in_=tab2_words[0].rearrange("p t i -> p (t i)").bitcast(I32))
+
+        t1_scales = held.tile([P, T], U8, name="t1_scales", align_bytes=64)
+        t2_scales = held.tile([P, T2], U8, name="t2_scales", align_bytes=64)
+        nc.vector.memset(t1_scales[:].bitcast(I32), 0)
+        load_scale_rows(nc.scalar, t1_scales, tab_scales[0])
+        nc.vector.memset(t2_scales[:].bitcast(I32), 0)
+        load_scale_rows(nc.scalar, t2_scales, tab2_scales[0])
+
+        weight = held.tile([P, PASSES, PACK], F32, name="weight")
+        weight_sq = held.tile([P, PASSES, PACK], F32, name="weight_sq")
+        nc.gpsimd.dma_start(out=weight[:], in_=wt.rearrange("(a p t) -> p a t", p=P, t=PACK))
+        nc.gpsimd.tensor_tensor(out=weight_sq[:], in0=weight[:], in1=weight[:], op=ALU.mult)
+
+        zero = held.tile([P, 1], F32, name="zero")
+        no_bias = held.tile([P, 1], F32, name="no_bias")
+        nc.vector.memset(zero[:], 0.0)
+        nc.scalar.activation(out=no_bias[:], in_=zero[:], func=ACT.Sqrt)
+
+        wd_raw = [held.tile([P, PACK, N], F32, name="wd_raw%d" % a) for a in range(PASSES)]
+        for a in range(PASSES):
+            nc.sync.dma_start(out=wd_raw[a][:], in_=wd[a * PASS : (a + 1) * PASS].rearrange("(p t) n -> p t n", t=PACK))
+        wb_codes = held.tile([P, PASSES, 2 * N], U8, name="wb_codes", align_bytes=64)
+        wb_plane = held.tile([P, PASSES, N], U8, name="wb_plane", align_bytes=64)
+        nc.sync.dma_start(out=wb_codes[:].bitcast(I32), in_=wb_words.rearrange("a p c -> p a c").bitcast(I32))
+        nc.vector.memset(wb_plane[:].bitcast(I32), 0)
+        load_scale_rows(nc.sync, wb_plane, wb_scales.rearrange("a q c -> q a c"))
+        bias = held.tile([P, NBLOCKS], F32, name="bias")
+        with nc.allow_non_contiguous_dma(reason="one bias value a partition and block of outputs"):
+            nc.sync.dma_start(out=bias[:], in_=b.rearrange("(q p) -> p q", p=P))
+
+        v_codes = held.tile([P, S], U32, name="v_codes", align_bytes=64)
+        v_scales_listed = held.tile([P, S], U8, name="v_scales_listed", align_bytes=64)
+        v_scales = held.tile([P, S], U8, name="v_scales", align_bytes=64)
+        u_codes = held.tile([P, S2], U32, name="u_codes", align_bytes=64)
+        u_scales = held.tile([P, S2], U8, name="u_scales", align_bytes=64)
+        wd_codes = held.tile([P, PASSES, N], U32, name="wd_codes", align_bytes=64)
+        wd_plane = held.tile([P, PASSES, N], U8, name="wd_plane", align_bytes=64)
+        z_codes = held.tile([P, PASSES, S2], U32, name="z_codes", align_bytes=64)
+        z_plane = held.tile([P, PASSES, S2], U8, name="z_plane", align_bytes=64)
+
+        def entries(lst, first, count):
+            return lst[:, first // LIST_ROWS : (first + count) // LIST_ROWS]
+
+        def gather_word_scales(a):
+            cols = slice(a * PASS, (a + 1) * PASS)
+            nc.vector.tensor_copy(v_scales_listed[:, cols], t1_scales[:].indirect(entries(word_list, a * PASS, PASS)))
+
+        def reorder_word_scales(a):
+            cols = slice(a * PASS, (a + 1) * PASS)
+            nc.vector.tensor_copy(
+                out=v_scales[:, cols].rearrange("p (t m) -> p t m", t=PACK),
+                in_=v_scales_listed[:, cols].rearrange("p (m t) -> p t m", t=PACK),
+            )
+
+        def gather_word_codes(a):
+            cols = slice(a * PASS, (a + 1) * PASS)
+            nc.vector.tensor_copy(
+                v_codes[:, cols].rearrange("p (t m) -> p m t", t=PACK),
+                t1_words[:].indirect(entries(word_list, a * PASS, PASS)),
+            )
+
+        def gather_image_scales(c):
+            cols = slice(c * CHUNK, (c + 1) * CHUNK)
+            nc.vector.tensor_copy(u_scales[:, cols], t2_scales[:].indirect(entries(image_list, c * CHUNK, CHUNK)))
+
+        def gather_image_codes(c):
+            cols = slice(c * CHUNK, (c + 1) * CHUNK)
+            nc.vector.tensor_copy(u_codes[:, cols], t2_words[:].indirect(entries(image_list, c * CHUNK, CHUNK)))
+
+        def response(dst, a, t, first, width):
+            words = slice(a * PASS + t * P, a * PASS + (t + 1) * P)
+            images = slice(first, first + width)
+            nc.tensor.matmul_mx(
+                out=dst,
+                lhsT=v_codes[:, words].bitcast(FP8X4),
+                lhsT_scale=v_scales[:, words],
+                rhs=u_codes[:, images].bitcast(FP8X4),
+                rhs_scale=u_scales[:, images],
+                start=True,
+                stop=True,
+            )
+
+        def quantize_z(z, a, c):
+            cols = slice(c * CHUNK, (c + 1) * CHUNK)
+            nc.vector.quantize_mx(out=z_codes[:, a, cols].bitcast(FP8X4), scales=z_plane[:, a, cols], in_=z[:])
+
+        def scalar_unit(a, c, banks, magnitude):
+            by_slot = magnitude.rearrange("p (t j) -> p t j", t=PACK)
+            for t in range(PACK):
+                acc = bank(banks[t % len(banks)], [P, CHUNK])
+                response(acc[:], a, t, c * CHUNK, CHUNK)
+                nc.scalar.activation(
+                    out=by_slot[:, t, :], in_=acc[:], func=ACT.Abs, bias=no_bias[:], scale=weight_sq[:, a, t : t + 1]
+                )
+            z = ring.tile([P, PACK * CHUNK], BF16, name="z", align_bytes=64, bufs=3)
+            nc.scalar.activation(
+                out=z[:].rearrange("p (g i t) -> p g t i", i=LINE, t=PACK),
+                in_=magnitude.rearrange("p (t g i) -> p g t i", i=LINE, t=PACK),
+                func=ACT.Sqrt,
+            )
+            return z
+
+        def vector_magnitudes(a, c, banks, magnitude):
+            signed = ring.tile([P, CHUNK, PACK], F32, name="signed")
+            blocks = CHUNK // P
+            for jb in range(blocks):
+                acc = bank(banks[jb % len(banks)], [P, PACK, P])
+                for t in range(PACK):
+                    response(acc[:, t, :], a, t, c * CHUNK + jb * P, P)
+                nc.vector.tensor_tensor(
+                    out=signed[:, jb * P : (jb + 1) * P, :],
+                    in0=acc[:].rearrange("p t j -> p j t"),
+                    in1=weight_sq[:, a, :].unsqueeze(1).to_broadcast([P, P, PACK]),
+                    op=ALU.mult,
+                )
+            flat = signed[:].rearrange("p j t -> p (j t)")
+            half = PACK * CHUNK // 2
+            for h in range(2):
+                cols = slice(h * half, (h + 1) * half)
+                nc.vector.scalar_tensor_tensor(
+                    out=magnitude[:, cols], in0=flat[:, cols], scalar=-1.0, in1=flat[:, cols], op0=ALU.mult, op1=ALU.max
+                )
+
+        def root(magnitude):
+            z = ring.tile([P, PACK * CHUNK], BF16, name="z", align_bytes=64, bufs=3)
+            nc.scalar.activation(out=z[:], in_=magnitude, func=ACT.Sqrt)
+            return z
+
+        def quantize_update(a):
+            grouped = ring.tile([P, N * PACK], BF16, name="grouped", align_bytes=64)
+            nc.vector.tensor_copy(
+                out=grouped[:].rearrange("p (g i t) -> p g t i", i=LINE, t=PACK),
+                in_=wd_raw[a][:].rearrange("p t (g i) -> p g t i", i=LINE),
+            )
+            return grouped
+
+        def project(c, nb, number):
+            acc = bank(number, [P, CHUNK])
+            images = slice(c * CHUNK, (c + 1) * CHUNK)
+            outs = slice(nb * P, (nb + 1) * P)
+            for a in range(PASSES):
+                nc.tensor.matmul_mx(
+                    out=acc[:],
+                    lhsT=wb_codes[:, a, 2 * nb * P : 2 * (nb + 1) * P].bitcast(FP4X4),
+                    lhsT_scale=wb_plane[:, a, outs],
+                    rhs=z_codes[:, a, images].bitcast(FP8X4),
+                    rhs_scale=z_plane[:, a, images],
+                    start=(a == 0),
+                    stop=False,
+                )
+                nc.tensor.matmul_mx(
+                    out=acc[:],
+                    lhsT=wd_codes[:, a, outs].bitcast(FP8X4),
+                    lhsT_scale=wd_plane[:, a, outs],
+                    rhs=z_codes[:, a, images].bitcast(FP8X4),
+                    rhs_scale=z_plane[:, a, images],
+                    start=False,
+                    stop=(a == PASSES - 1),
+                )
+            return acc
+
+        gather_word_scales(0)
+        gather_word_codes(0)
+        reorder_word_scales(0)
+        gather_image_scales(0)
+        gather_image_codes(0)
+        gather_word_scales(1)
+        gather_word_codes(1)
+        reorder_word_scales(1)
+        gather_image_scales(1)
+        gather_image_codes(1)
+
+        unit = PACK * CHUNK
+        late = held.tile([P, 3 * unit], F32, name="late")
+        early = [ring.tile([P, unit], F32, name="early") for k in range(2)]
+        z00 = scalar_unit(0, 0, [4, 5, 6, 7], early[0][:])
+        gather_image_scales(2)
+        gather_image_codes(2)
+        g0 = quantize_update(0)
+        g1 = quantize_update(1)
+        nc.vector.quantize_mx(out=wd_codes[:, 0, :].bitcast(FP8X4), scales=wd_plane[:, 0, :], in_=g0[:])
+        quantize_z(z00, 0, 0)
+        nc.vector.quantize_mx(out=wd_codes[:, 1, :].bitcast(FP8X4), scales=wd_plane[:, 1, :], in_=g1[:])
+        z10 = scalar_unit(1, 0, [4, 5, 6, 7], early[1][:])
+        quantize_z(z10, 1, 0)
+        third = ring.tile([P, unit], F32, name="early")
+        z01 = scalar_unit(0, 1, [0, 1], third[:])
+        vector_magnitudes(0, 2, [2, 3], late[:, unit : 2 * unit])
+        quantize_z(z01, 0, 1)
+        y = {}
+        for nb in range(NBLOCKS):
+            y[0, nb] = project(0, nb, 4 + nb)
+        z11 = scalar_unit(1, 1, [0, 1], late[:, 0:unit])
+        vector_magnitudes(1, 2, [2, 3], late[:, 2 * unit : 3 * unit])
+        quantize_z(z11, 1, 1)
+        for a in range(PASSES):
+            quantize_z(root(late[:, (1 + a) * unit : (2 + a) * unit]), a, 2)
+        for nb in range(NBLOCKS):
+            y[1, nb] = project(1, nb, nb)
+
+        staged = held.tile([P, CHUNKS * NBLOCKS * CHUNK], F32, name="late")
+        for c in range(CHUNKS):
+            for nb in range(NBLOCKS):
+                if c == CHUNKS - 1:
+                    y[c, nb] = project(c, nb, 4 + nb)
+                piece = staged[:, (c * NBLOCKS + nb) * CHUNK : (c * NBLOCKS + nb + 1) * CHUNK]
+                nc.scalar.activation(out=piece, in_=y[c, nb][:], func=ACT.Tanh, bias=bias[:, nb : nb + 1])
+                nc.sync.dma_start(out=out[nb * P : (nb + 1) * P, c * CHUNK : (c + 1) * CHUNK], in_=piece)

@@ -50,17 +50,16 @@ def tile_list_visual_word_hash_kernel(
         nc.sync.dma_start(word_list[:], offs)
         nc.sync.dma_start(image_list[:], offs2)
 
-        t1_words = held.tile([P, T], U32, name="t1_words", align_bytes=64)
-        t2_words = held.tile([P, T2], U32, name="t2_words", align_bytes=64)
-        nc.sync.dma_start(out=t1_words[:].bitcast(I32), in_=tab_words[0].rearrange("p t i -> p (t i)").bitcast(I32))
-        nc.sync.dma_start(out=t2_words[:].bitcast(I32), in_=tab2_words[0].rearrange("p t i -> p (t i)").bitcast(I32))
-
         t1_scales = held.tile([P, T], U8, name="t1_scales", align_bytes=64)
         t2_scales = held.tile([P, T2], U8, name="t2_scales", align_bytes=64)
+        t1_words = held.tile([P, T], U32, name="t1_words", align_bytes=64)
+        t2_words = held.tile([P, T2], U32, name="t2_words", align_bytes=64)
         nc.vector.memset(t1_scales[:].bitcast(I32), 0)
-        load_scale_rows(nc.scalar, t1_scales, tab_scales[0])
+        load_scale_rows(nc.sync, t1_scales, tab_scales[0])
+        nc.sync.dma_start(out=t1_words[:].bitcast(I32), in_=tab_words[0].rearrange("p t i -> p (t i)").bitcast(I32))
         nc.vector.memset(t2_scales[:].bitcast(I32), 0)
-        load_scale_rows(nc.scalar, t2_scales, tab2_scales[0])
+        load_scale_rows(nc.sync, t2_scales, tab2_scales[0])
+        nc.sync.dma_start(out=t2_words[:].bitcast(I32), in_=tab2_words[0].rearrange("p t i -> p (t i)").bitcast(I32))
 
         weight = held.tile([P, PASSES, PACK], F32, name="weight")
         weight_sq = held.tile([P, PASSES, PACK], F32, name="weight_sq")
@@ -72,23 +71,11 @@ def tile_list_visual_word_hash_kernel(
         nc.vector.memset(zero[:], 0.0)
         nc.scalar.activation(out=no_bias[:], in_=zero[:], func=ACT.Sqrt)
 
-        wd_raw = [held.tile([P, PACK, N], F32, name="wd_raw%d" % a) for a in range(PASSES)]
-        for a in range(PASSES):
-            nc.sync.dma_start(out=wd_raw[a][:], in_=wd[a * PASS : (a + 1) * PASS].rearrange("(p t) n -> p t n", t=PACK))
-        wb_codes = held.tile([P, PASSES, 2 * N], U8, name="wb_codes", align_bytes=64)
-        wb_plane = held.tile([P, PASSES, N], U8, name="wb_plane", align_bytes=64)
-        nc.sync.dma_start(out=wb_codes[:].bitcast(I32), in_=wb_words.rearrange("a p c -> p a c").bitcast(I32))
-        nc.vector.memset(wb_plane[:].bitcast(I32), 0)
-        load_scale_rows(nc.sync, wb_plane, wb_scales.rearrange("a q c -> q a c"))
-        bias = held.tile([P, NBLOCKS], F32, name="bias")
-        with nc.allow_non_contiguous_dma(reason="one bias value a partition and block of outputs"):
-            nc.sync.dma_start(out=bias[:], in_=b.rearrange("(q p) -> p q", p=P))
-
         v_codes = held.tile([P, S], U32, name="v_codes", align_bytes=64)
-        v_scales_listed = held.tile([P, S], U8, name="v_scales_listed", align_bytes=64)
+        listed = [held.tile([P, PASS], U8, name="listed%d" % a) for a in range(PASSES)]
         v_scales = held.tile([P, S], U8, name="v_scales", align_bytes=64)
         u_codes = held.tile([P, S2], U32, name="u_codes", align_bytes=64)
-        u_scales = held.tile([P, S2], U8, name="u_scales", align_bytes=64)
+        u_scales = {0: held.tile([P, CHUNK], U8, name="u_scales_first", align_bytes=64)[:]}
         wd_codes = held.tile([P, PASSES, N], U32, name="wd_codes", align_bytes=64)
         wd_plane = held.tile([P, PASSES, N], U8, name="wd_plane", align_bytes=64)
         z_codes = held.tile([P, PASSES, S2], U32, name="z_codes", align_bytes=64)
@@ -98,14 +85,13 @@ def tile_list_visual_word_hash_kernel(
             return lst[:, first // LIST_ROWS : (first + count) // LIST_ROWS]
 
         def gather_word_scales(a):
-            cols = slice(a * PASS, (a + 1) * PASS)
-            nc.vector.tensor_copy(v_scales_listed[:, cols], t1_scales[:].indirect(entries(word_list, a * PASS, PASS)))
+            nc.vector.tensor_copy(listed[a][:], t1_scales[:].indirect(entries(word_list, a * PASS, PASS)))
 
         def reorder_word_scales(a):
             cols = slice(a * PASS, (a + 1) * PASS)
             nc.vector.tensor_copy(
                 out=v_scales[:, cols].rearrange("p (t m) -> p t m", t=PACK),
-                in_=v_scales_listed[:, cols].rearrange("p (m t) -> p t m", t=PACK),
+                in_=listed[a][:].rearrange("p (m t) -> p t m", t=PACK),
             )
 
         def gather_word_codes(a):
@@ -116,8 +102,7 @@ def tile_list_visual_word_hash_kernel(
             )
 
         def gather_image_scales(c):
-            cols = slice(c * CHUNK, (c + 1) * CHUNK)
-            nc.vector.tensor_copy(u_scales[:, cols], t2_scales[:].indirect(entries(image_list, c * CHUNK, CHUNK)))
+            nc.vector.tensor_copy(u_scales[c], t2_scales[:].indirect(entries(image_list, c * CHUNK, CHUNK)))
 
         def gather_image_codes(c):
             cols = slice(c * CHUNK, (c + 1) * CHUNK)
@@ -131,7 +116,7 @@ def tile_list_visual_word_hash_kernel(
                 lhsT=v_codes[:, words].bitcast(FP8X4),
                 lhsT_scale=v_scales[:, words],
                 rhs=u_codes[:, images].bitcast(FP8X4),
-                rhs_scale=u_scales[:, images],
+                rhs_scale=u_scales[first // CHUNK][:, first % CHUNK : first % CHUNK + width],
                 start=True,
                 stop=True,
             )
@@ -140,14 +125,18 @@ def tile_list_visual_word_hash_kernel(
             cols = slice(c * CHUNK, (c + 1) * CHUNK)
             nc.vector.quantize_mx(out=z_codes[:, a, cols].bitcast(FP8X4), scales=z_plane[:, a, cols], in_=z[:])
 
-        def scalar_unit(a, c, banks, magnitude):
-            by_slot = magnitude.rearrange("p (t j) -> p t j", t=PACK)
-            for t in range(PACK):
-                acc = bank(banks[t % len(banks)], [P, CHUNK])
-                response(acc[:], a, t, c * CHUNK, CHUNK)
-                nc.scalar.activation(
-                    out=by_slot[:, t, :], in_=acc[:], func=ACT.Abs, bias=no_bias[:], scale=weight_sq[:, a, t : t + 1]
-                )
+        def scalar_magnitude(a, c, t, number, magnitude):
+            acc = bank(number, [P, CHUNK])
+            response(acc[:], a, t, c * CHUNK, CHUNK)
+            nc.scalar.activation(
+                out=magnitude[:, t * CHUNK : (t + 1) * CHUNK],
+                in_=acc[:],
+                func=ACT.Abs,
+                bias=no_bias[:],
+                scale=weight_sq[:, a, t : t + 1],
+            )
+
+        def interleaving_root(magnitude):
             z = ring.tile([P, PACK * CHUNK], BF16, name="z", align_bytes=64, bufs=3)
             nc.scalar.activation(
                 out=z[:].rearrange("p (g i t) -> p g t i", i=LINE, t=PACK),
@@ -156,37 +145,25 @@ def tile_list_visual_word_hash_kernel(
             )
             return z
 
-        def vector_magnitudes(a, c, banks, magnitude):
-            signed = ring.tile([P, CHUNK, PACK], F32, name="signed")
-            blocks = CHUNK // P
-            for jb in range(blocks):
-                acc = bank(banks[jb % len(banks)], [P, PACK, P])
-                for t in range(PACK):
-                    response(acc[:, t, :], a, t, c * CHUNK + jb * P, P)
-                nc.vector.tensor_tensor(
-                    out=signed[:, jb * P : (jb + 1) * P, :],
-                    in0=acc[:].rearrange("p t j -> p j t"),
-                    in1=weight_sq[:, a, :].unsqueeze(1).to_broadcast([P, P, PACK]),
-                    op=ALU.mult,
-                )
-            flat = signed[:].rearrange("p j t -> p (j t)")
-            half = PACK * CHUNK // 2
-            for h in range(2):
-                cols = slice(h * half, (h + 1) * half)
-                nc.vector.scalar_tensor_tensor(
-                    out=magnitude[:, cols], in0=flat[:, cols], scalar=-1.0, in1=flat[:, cols], op0=ALU.mult, op1=ALU.max
-                )
+        def vector_weighted(a, c, jb, number, signed):
+            acc = bank(number, [P, PACK, P])
+            for t in range(PACK):
+                response(acc[:, t, :], a, t, c * CHUNK + jb * P, P)
+            nc.vector.tensor_tensor(
+                out=signed[:, jb * PACK * P : (jb + 1) * PACK * P].rearrange("p (j t) -> p j t", t=PACK),
+                in0=acc[:].rearrange("p t j -> p j t"),
+                in1=weight_sq[:, a, :].unsqueeze(1).to_broadcast([P, P, PACK]),
+                op=ALU.mult,
+            )
 
-        def root(magnitude):
-            z = ring.tile([P, PACK * CHUNK], BF16, name="z", align_bytes=64, bufs=3)
-            nc.scalar.activation(out=z[:], in_=magnitude, func=ACT.Sqrt)
-            return z
+        def vector_magnitude(signed, magnitude):
+            nc.vector.scalar_tensor_tensor(out=magnitude, in0=signed, scalar=-1.0, in1=signed, op0=ALU.mult, op1=ALU.max)
 
         def quantize_update(a):
             grouped = ring.tile([P, N * PACK], BF16, name="grouped", align_bytes=64)
             nc.vector.tensor_copy(
                 out=grouped[:].rearrange("p (g i t) -> p g t i", i=LINE, t=PACK),
-                in_=wd_raw[a][:].rearrange("p t (g i) -> p g t i", i=LINE),
+                in_=wd_raw[:, a].rearrange("p t (g i) -> p g t i", i=LINE),
             )
             return grouped
 
@@ -215,42 +192,88 @@ def tile_list_visual_word_hash_kernel(
                 )
             return acc
 
-        gather_word_scales(0)
+        for a in range(PASSES):
+            gather_word_scales(a)
+        for a in range(PASSES):
+            reorder_word_scales(a)
         gather_word_codes(0)
-        reorder_word_scales(0)
         gather_image_scales(0)
         gather_image_codes(0)
-        gather_word_scales(1)
         gather_word_codes(1)
-        reorder_word_scales(1)
-        gather_image_scales(1)
-        gather_image_codes(1)
+        wd_raw = held.tile([P, PASSES, PACK, N], F32, name="wd_raw")
+        for a in range(PASSES):
+            nc.sync.dma_start(out=wd_raw[:, a], in_=wd[a * PASS : (a + 1) * PASS].rearrange("(p t) n -> p t n", t=PACK))
+        wb_codes = held.tile([P, PASSES, 2 * N], U8, name="wb_codes", align_bytes=64)
+        wb_plane = held.tile([P, PASSES, N], U8, name="wb_plane", align_bytes=64)
+        nc.sync.dma_start(out=wb_codes[:].bitcast(I32), in_=wb_words.rearrange("a p c -> p a c").bitcast(I32))
+        nc.vector.memset(wb_plane[:].bitcast(I32), 0)
+        load_scale_rows(nc.sync, wb_plane, wb_scales.rearrange("a q c -> q a c"))
+        bias = held.tile([P, NBLOCKS], F32, name="bias")
+        with nc.allow_non_contiguous_dma(reason="one bias value a partition and block of outputs"):
+            nc.sync.dma_start(out=bias[:], in_=b.rearrange("(q p) -> p q", p=P))
+
+        for c in range(1, CHUNKS):
+            gather_image_codes(c)
 
         unit = PACK * CHUNK
+        half = unit // 2
         late = held.tile([P, 3 * unit], F32, name="late")
-        early = [ring.tile([P, unit], F32, name="early") for k in range(2)]
-        z00 = scalar_unit(0, 0, [4, 5, 6, 7], early[0][:])
-        gather_image_scales(2)
-        gather_image_codes(2)
-        g0 = quantize_update(0)
-        g1 = quantize_update(1)
-        nc.vector.quantize_mx(out=wd_codes[:, 0, :].bitcast(FP8X4), scales=wd_plane[:, 0, :], in_=g0[:])
-        quantize_z(z00, 0, 0)
-        nc.vector.quantize_mx(out=wd_codes[:, 1, :].bitcast(FP8X4), scales=wd_plane[:, 1, :], in_=g1[:])
-        z10 = scalar_unit(1, 0, [4, 5, 6, 7], early[1][:])
-        quantize_z(z10, 1, 0)
-        third = ring.tile([P, unit], F32, name="early")
-        z01 = scalar_unit(0, 1, [0, 1], third[:])
-        vector_magnitudes(0, 2, [2, 3], late[:, unit : 2 * unit])
-        quantize_z(z01, 0, 1)
+        scalar_units = [(0, 0, [4, 5, 6, 7]), (1, 0, [4, 5, 6, 7]), (0, 1, [0, 1, 7, 0]), (1, 1, [1, 7, 0, 1])]
+        first = held.tile([P, unit], F32, name="first", align_bytes=64)
+        magnitudes = [first[:]] + [ring.tile([P, unit], F32, name="early")[:] for k in range(2)] + [late[:, 0:unit]]
+        last = CHUNKS - 1
+        signed = [ring.tile([P, unit], F32, name="signed") for a in range(PASSES)]
+
+        def vector_unit(a):
+            for h in range(2):
+                for jb in range(2 * h, 2 * h + 2):
+                    vector_weighted(a, last, jb, 2 + jb % 2, signed[a])
+            for h in range(2):
+                vector_magnitude(
+                    signed[a][:, h * half : (h + 1) * half], late[:, (1 + a) * unit + h * half : (1 + a) * unit + (h + 1) * half]
+                )
+
+        z_last = [ring.tile([P, unit], BF16, name="z_last", align_bytes=64) for a in range(PASSES)]
+
+        def plain_root(a, h):
+            nc.scalar.activation(
+                out=z_last[a][:, h * half : (h + 1) * half],
+                in_=late[:, (1 + a) * unit + h * half : (1 + a) * unit + (h + 1) * half],
+                func=ACT.Sqrt,
+            )
+
+        a, c, banks = scalar_units[0]
+        scalar_magnitude(a, c, 0, banks[0], magnitudes[0])
+        for k, (a, c, banks) in enumerate(scalar_units):
+            for t in range(1, PACK):
+                scalar_magnitude(a, c, t, banks[t], magnitudes[k])
+            if k + 1 < len(scalar_units):
+                a_next, c_next, banks_next = scalar_units[k + 1]
+                scalar_magnitude(a_next, c_next, 0, banks_next[0], magnitudes[k + 1])
+            else:
+                plain_root(0, 0)
+            z = interleaving_root(magnitudes[k])
+            if k == 0:
+                later_scales = held.tile([P, (CHUNKS - 1) * CHUNK], U8, name="first", align_bytes=64)
+                for later in range(1, CHUNKS):
+                    u_scales[later] = later_scales[:, (later - 1) * CHUNK : later * CHUNK]
+                    gather_image_scales(later)
+                grouped = [quantize_update(half_k) for half_k in range(PASSES)]
+                for half_k in range(PASSES):
+                    nc.vector.quantize_mx(
+                        out=wd_codes[:, half_k, :].bitcast(FP8X4), scales=wd_plane[:, half_k, :], in_=grouped[half_k][:]
+                    )
+            if k in (1, 2):
+                vector_unit(k - 1)
+            quantize_z(z, a, c)
+        plain_root(0, 1)
+        quantize_z(z_last[0], 0, last)
+        for h in range(2):
+            plain_root(1, h)
+        quantize_z(z_last[1], 1, last)
         y = {}
         for nb in range(NBLOCKS):
             y[0, nb] = project(0, nb, 4 + nb)
-        z11 = scalar_unit(1, 1, [0, 1], late[:, 0:unit])
-        vector_magnitudes(1, 2, [2, 3], late[:, 2 * unit : 3 * unit])
-        quantize_z(z11, 1, 1)
-        for a in range(PASSES):
-            quantize_z(root(late[:, (1 + a) * unit : (2 + a) * unit]), a, 2)
         for nb in range(NBLOCKS):
             y[1, nb] = project(1, nb, nb)
 

@@ -25,12 +25,21 @@ CHUNKS = S2 // CHUNK
 NBLOCKS = N // P
 LIST_ROWS = 16
 QUAD = 32
-LINE = 4
+RUN = 4
+WORD_PLANE = 4
+UNIT = PACK * CHUNK
+HALF = UNIT // 2
+HALVES = [slice(0, HALF), slice(HALF, UNIT)]
+VECTOR_BANKS = [2, 3]
 
 
-def load_scale_rows(queue, plane, rows):
+def load_scale_rows(nc, plane, rows, start=0):
     for r in range(PACK):
-        queue.dma_start(out=plane[r:P:QUAD].bitcast(I32), in_=rows[r :: PACK].bitcast(I32))
+        nc.sync.dma_start(out=plane[start + r : P : QUAD].bitcast(I32), in_=rows[r::PACK].bitcast(I32))
+
+
+def entries(list_tile, first, count):
+    return list_tile[:, first // LIST_ROWS : (first + count) // LIST_ROWS]
 
 
 def tile_list_visual_word_hash_kernel(
@@ -50,16 +59,16 @@ def tile_list_visual_word_hash_kernel(
         nc.sync.dma_start(word_list[:], offs)
         nc.sync.dma_start(image_list[:], offs2)
 
-        t1_scales = held.tile([P, T], U8, name="t1_scales", align_bytes=64)
-        t2_scales = held.tile([P, T2], U8, name="t2_scales", align_bytes=64)
-        t1_words = held.tile([P, T], U32, name="t1_words", align_bytes=64)
-        t2_words = held.tile([P, T2], U32, name="t2_words", align_bytes=64)
-        nc.vector.memset(t1_scales[:].bitcast(I32), 0)
-        load_scale_rows(nc.sync, t1_scales, tab_scales[0])
-        nc.sync.dma_start(out=t1_words[:].bitcast(I32), in_=tab_words[0].rearrange("p t i -> p (t i)").bitcast(I32))
-        nc.vector.memset(t2_scales[:].bitcast(I32), 0)
-        load_scale_rows(nc.sync, t2_scales, tab2_scales[0])
-        nc.sync.dma_start(out=t2_words[:].bitcast(I32), in_=tab2_words[0].rearrange("p t i -> p (t i)").bitcast(I32))
+        word_table_plane = held.tile([P, T], U8, name="word_table_plane", align_bytes=64)
+        image_table_plane = held.tile([P, T2], U8, name="image_table_plane", align_bytes=64)
+        word_table = held.tile([P, T], U32, name="word_table", align_bytes=64)
+        image_table = held.tile([P, T2], U32, name="image_table", align_bytes=64)
+        nc.vector.memset(word_table_plane[:].bitcast(I32), 0)
+        load_scale_rows(nc, word_table_plane, tab_scales[0], WORD_PLANE)
+        nc.sync.dma_start(out=word_table[:].bitcast(I32), in_=tab_words[0].rearrange("p c t -> p (c t)").bitcast(I32))
+        nc.vector.memset(image_table_plane[:].bitcast(I32), 0)
+        load_scale_rows(nc, image_table_plane, tab2_scales[0])
+        nc.sync.dma_start(out=image_table[:].bitcast(I32), in_=tab2_words[0].rearrange("p c t -> p (c t)").bitcast(I32))
 
         weight = held.tile([P, PASSES, PACK], F32, name="weight")
         weight_sq = held.tile([P, PASSES, PACK], F32, name="weight_sq")
@@ -71,111 +80,117 @@ def tile_list_visual_word_hash_kernel(
         nc.vector.memset(zero[:], 0.0)
         nc.scalar.activation(out=no_bias[:], in_=zero[:], func=ACT.Sqrt)
 
-        v_codes = held.tile([P, S], U32, name="v_codes", align_bytes=64)
-        listed = [held.tile([P, PASS], U8, name="listed%d" % a) for a in range(PASSES)]
-        v_scales = held.tile([P, S], U8, name="v_scales", align_bytes=64)
-        u_codes = held.tile([P, S2], U32, name="u_codes", align_bytes=64)
-        u_scales = {0: held.tile([P, CHUNK], U8, name="u_scales_first", align_bytes=64)[:]}
+        word_codes = held.tile([P, S], U32, name="word_codes", align_bytes=64)
+        listed_plane = [held.tile([P, PASS], U8, name="listed_plane%d" % a) for a in range(PASSES)]
+        word_plane = held.tile([P, S], U8, name="word_plane", align_bytes=64)
+        image_codes = held.tile([P, S2], U32, name="image_codes", align_bytes=64)
+        image_plane = {c: held.tile([P, CHUNK], U8, name="image_plane%d" % c, align_bytes=64) for c in range(CHUNKS - 1)}
         wd_codes = held.tile([P, PASSES, N], U32, name="wd_codes", align_bytes=64)
         wd_plane = held.tile([P, PASSES, N], U8, name="wd_plane", align_bytes=64)
         z_codes = held.tile([P, PASSES, S2], U32, name="z_codes", align_bytes=64)
         z_plane = held.tile([P, PASSES, S2], U8, name="z_plane", align_bytes=64)
 
-        def entries(lst, first, count):
-            return lst[:, first // LIST_ROWS : (first + count) // LIST_ROWS]
-
         def gather_word_scales(a):
-            nc.vector.tensor_copy(listed[a][:], t1_scales[:].indirect(entries(word_list, a * PASS, PASS)))
+            nc.vector.tensor_copy(listed_plane[a][:], word_table_plane[:].indirect(entries(word_list, a * PASS, PASS)))
 
         def reorder_word_scales(a):
-            cols = slice(a * PASS, (a + 1) * PASS)
             nc.vector.tensor_copy(
-                out=v_scales[:, cols].rearrange("p (t m) -> p t m", t=PACK),
-                in_=listed[a][:].rearrange("p (m t) -> p t m", t=PACK),
+                out=word_plane[:, a * PASS : (a + 1) * PASS].rearrange("p (t m) -> p t m", t=PACK),
+                in_=listed_plane[a][:].rearrange("p (m t) -> p t m", t=PACK),
             )
 
         def gather_word_codes(a):
-            cols = slice(a * PASS, (a + 1) * PASS)
             nc.vector.tensor_copy(
-                v_codes[:, cols].rearrange("p (t m) -> p m t", t=PACK),
-                t1_words[:].indirect(entries(word_list, a * PASS, PASS)),
+                word_codes[:, a * PASS : (a + 1) * PASS].rearrange("p (t m) -> p m t", t=PACK),
+                word_table[:].indirect(entries(word_list, a * PASS, PASS)),
             )
 
         def gather_image_scales(c):
-            nc.vector.tensor_copy(u_scales[c], t2_scales[:].indirect(entries(image_list, c * CHUNK, CHUNK)))
+            nc.vector.tensor_copy(image_plane[c][:], image_table_plane[:].indirect(entries(image_list, c * CHUNK, CHUNK)))
 
         def gather_image_codes(c):
-            cols = slice(c * CHUNK, (c + 1) * CHUNK)
-            nc.vector.tensor_copy(u_codes[:, cols], t2_words[:].indirect(entries(image_list, c * CHUNK, CHUNK)))
+            nc.vector.tensor_copy(
+                image_codes[:, c * CHUNK : (c + 1) * CHUNK], image_table[:].indirect(entries(image_list, c * CHUNK, CHUNK))
+            )
 
-        def response(dst, a, t, first, width):
+        def response(acc, a, t, c, first, width):
             words = slice(a * PASS + t * P, a * PASS + (t + 1) * P)
-            images = slice(first, first + width)
             nc.tensor.matmul_mx(
-                out=dst,
-                lhsT=v_codes[:, words].bitcast(FP8X4),
-                lhsT_scale=v_scales[:, words],
-                rhs=u_codes[:, images].bitcast(FP8X4),
-                rhs_scale=u_scales[first // CHUNK][:, first % CHUNK : first % CHUNK + width],
+                out=acc,
+                lhsT=word_codes[:, words].bitcast(FP8X4),
+                lhsT_scale=word_plane[WORD_PLANE:P, words],
+                rhs=image_codes[:, c * CHUNK + first : c * CHUNK + first + width].bitcast(FP8X4),
+                rhs_scale=image_plane[c][:, first : first + width],
                 start=True,
                 stop=True,
             )
 
-        def quantize_z(z, a, c):
-            cols = slice(c * CHUNK, (c + 1) * CHUNK)
-            nc.vector.quantize_mx(out=z_codes[:, a, cols].bitcast(FP8X4), scales=z_plane[:, a, cols], in_=z[:])
-
-        def scalar_magnitude(a, c, t, number, magnitude):
+        def scalar_magnitude(a, c, t, number):
             acc = bank(number, [P, CHUNK])
-            response(acc[:], a, t, c * CHUNK, CHUNK)
+            response(acc[:], a, t, c, 0, CHUNK)
             nc.scalar.activation(
-                out=magnitude[:, t * CHUNK : (t + 1) * CHUNK],
+                out=magnitude[a, c][:, t * CHUNK : (t + 1) * CHUNK],
                 in_=acc[:],
                 func=ACT.Abs,
                 bias=no_bias[:],
                 scale=weight_sq[:, a, t : t + 1],
             )
 
-        def interleaving_root(magnitude):
-            z = ring.tile([P, PACK * CHUNK], BF16, name="z", align_bytes=64, bufs=3)
+        def interleaving_root(a, c):
             nc.scalar.activation(
-                out=z[:].rearrange("p (g i t) -> p g t i", i=LINE, t=PACK),
-                in_=magnitude.rearrange("p (t g i) -> p g t i", i=LINE, t=PACK),
+                out=z[a, c][:].rearrange("p (g i t) -> p g t i", i=RUN, t=PACK),
+                in_=magnitude[a, c].rearrange("p (t g i) -> p g t i", i=RUN, t=PACK),
                 func=ACT.Sqrt,
             )
-            return z
 
-        def vector_weighted(a, c, jb, number, signed):
-            acc = bank(number, [P, PACK, P])
-            for t in range(PACK):
-                response(acc[:, t, :], a, t, c * CHUNK + jb * P, P)
-            nc.vector.tensor_tensor(
-                out=signed[:, jb * PACK * P : (jb + 1) * PACK * P].rearrange("p (j t) -> p j t", t=PACK),
-                in0=acc[:].rearrange("p t j -> p j t"),
-                in1=weight_sq[:, a, :].unsqueeze(1).to_broadcast([P, P, PACK]),
-                op=ALU.mult,
+        def vector_weighted(a, c, h):
+            signed = ring.tile([P, HALF], F32, name="signed", bufs=3)
+            for block, number in enumerate(VECTOR_BANKS):
+                acc = bank(number, [P, PACK, P])
+                for t in range(PACK):
+                    response(acc[:, t, :], a, t, c, h * CHUNK // 2 + block * P, P)
+                nc.vector.tensor_tensor(
+                    out=signed[:, block * PACK * P : (block + 1) * PACK * P].rearrange("p (j t) -> p j t", t=PACK),
+                    in0=acc[:].rearrange("p t j -> p j t"),
+                    in1=weight_sq[:, a, :].unsqueeze(1).to_broadcast([P, P, PACK]),
+                    op=ALU.mult,
+                )
+            return signed
+
+        def vector_magnitude(a, c, h, signed):
+            nc.vector.scalar_tensor_tensor(
+                out=magnitude[a, c][:, HALVES[h]], in0=signed[:], scalar=-1.0, in1=signed[:], op0=ALU.mult, op1=ALU.max
             )
 
-        def vector_magnitude(signed, magnitude):
-            nc.vector.scalar_tensor_tensor(out=magnitude, in0=signed, scalar=-1.0, in1=signed, op0=ALU.mult, op1=ALU.max)
+        def plain_root(a, c, h):
+            nc.scalar.activation(out=z[a, c][:, HALVES[h]], in_=magnitude[a, c][:, HALVES[h]], func=ACT.Sqrt)
 
-        def quantize_update(a):
-            grouped = ring.tile([P, N * PACK], BF16, name="grouped", align_bytes=64)
+        def quantize_z(a, c):
+            images = slice(c * CHUNK, (c + 1) * CHUNK)
+            nc.vector.quantize_mx(out=z_codes[:, a, images].bitcast(FP8X4), scales=z_plane[:, a, images], in_=z[a, c][:])
+
+        def round_update(a):
+            grouped = ring.tile([P, N, PACK], BF16, name="grouped", align_bytes=64)
             nc.vector.tensor_copy(
-                out=grouped[:].rearrange("p (g i t) -> p g t i", i=LINE, t=PACK),
-                in_=wd_raw[:, a].rearrange("p t (g i) -> p g t i", i=LINE),
+                out=grouped[:].rearrange("p (g i) t -> p g t i", i=RUN),
+                in_=wd_raw[:, a].rearrange("p t (g i) -> p g t i", i=RUN),
             )
             return grouped
+
+        def quantize_update(a, grouped):
+            nc.vector.quantize_mx(
+                out=wd_codes[:, a, :].bitcast(FP8X4), scales=wd_plane[:, a, :], in_=grouped[:].rearrange("p n t -> p (n t)")
+            )
 
         def project(c, nb, number):
             acc = bank(number, [P, CHUNK])
             images = slice(c * CHUNK, (c + 1) * CHUNK)
-            outs = slice(nb * P, (nb + 1) * P)
+            rows = slice(nb * P, (nb + 1) * P)
             for a in range(PASSES):
                 nc.tensor.matmul_mx(
                     out=acc[:],
                     lhsT=wb_codes[:, a, 2 * nb * P : 2 * (nb + 1) * P].bitcast(FP4X4),
-                    lhsT_scale=wb_plane[:, a, outs],
+                    lhsT_scale=wb_plane[:, a, rows],
                     rhs=z_codes[:, a, images].bitcast(FP8X4),
                     rhs_scale=z_plane[:, a, images],
                     start=(a == 0),
@@ -183,8 +198,8 @@ def tile_list_visual_word_hash_kernel(
                 )
                 nc.tensor.matmul_mx(
                     out=acc[:],
-                    lhsT=wd_codes[:, a, outs].bitcast(FP8X4),
-                    lhsT_scale=wd_plane[:, a, outs],
+                    lhsT=wd_codes[:, a, rows].bitcast(FP8X4),
+                    lhsT_scale=wd_plane[:, a, rows],
                     rhs=z_codes[:, a, images].bitcast(FP8X4),
                     rhs_scale=z_plane[:, a, images],
                     start=False,
@@ -200,6 +215,7 @@ def tile_list_visual_word_hash_kernel(
         gather_image_scales(0)
         gather_image_codes(0)
         gather_word_codes(1)
+
         wd_raw = held.tile([P, PASSES, PACK, N], F32, name="wd_raw")
         for a in range(PASSES):
             nc.sync.dma_start(out=wd_raw[:, a], in_=wd[a * PASS : (a + 1) * PASS].rearrange("(p t) n -> p t n", t=PACK))
@@ -207,81 +223,77 @@ def tile_list_visual_word_hash_kernel(
         wb_plane = held.tile([P, PASSES, N], U8, name="wb_plane", align_bytes=64)
         nc.sync.dma_start(out=wb_codes[:].bitcast(I32), in_=wb_words.rearrange("a p c -> p a c").bitcast(I32))
         nc.vector.memset(wb_plane[:].bitcast(I32), 0)
-        load_scale_rows(nc.sync, wb_plane, wb_scales.rearrange("a q c -> q a c"))
+        load_scale_rows(nc, wb_plane, wb_scales.rearrange("a q c -> q a c"))
         bias = held.tile([P, NBLOCKS], F32, name="bias")
-        with nc.allow_non_contiguous_dma(reason="one bias value a partition and block of outputs"):
-            nc.sync.dma_start(out=bias[:], in_=b.rearrange("(q p) -> p q", p=P))
+        with nc.allow_non_contiguous_dma(reason="one bias value a partition and block of output rows"):
+            nc.sync.dma_start(out=bias[:], in_=b.rearrange("(nb p) -> p nb", p=P))
 
-        for c in range(1, CHUNKS):
-            gather_image_codes(c)
+        gather_image_scales(1)
+        gather_image_codes(1)
 
-        unit = PACK * CHUNK
-        half = unit // 2
-        late = held.tile([P, 3 * unit], F32, name="late")
-        scalar_units = [(0, 0, [4, 5, 6, 7]), (1, 0, [4, 5, 6, 7]), (0, 1, [0, 1, 7, 0]), (1, 1, [1, 7, 0, 1])]
-        first = held.tile([P, unit], F32, name="first", align_bytes=64)
-        magnitudes = [first[:]] + [ring.tile([P, unit], F32, name="early")[:] for k in range(2)] + [late[:, 0:unit]]
-        last = CHUNKS - 1
-        signed = [ring.tile([P, unit], F32, name="signed") for a in range(PASSES)]
+        late = held.tile([P, 3 * UNIT], F32, name="late_then_results")
+        first_unit = held.tile([P, UNIT], F32, name="first_unit_then_plane", align_bytes=64)
+        z = {
+            (a, c): held.tile([P, UNIT], BF16, name="z%d%d" % (a, c), align_bytes=64)
+            for a in range(PASSES)
+            for c in range(CHUNKS)
+        }
+        magnitude = {
+            (0, 0): first_unit[:],
+            (1, 0): held.tile([P, UNIT], F32, name="magnitude10")[:],
+            (0, 1): held.tile([P, UNIT], F32, name="magnitude01")[:],
+            (1, 1): late[:, 0:UNIT],
+            (0, 2): late[:, UNIT : 2 * UNIT],
+            (1, 2): late[:, 2 * UNIT : 3 * UNIT],
+        }
 
-        def vector_unit(a):
-            for h in range(2):
-                for jb in range(2 * h, 2 * h + 2):
-                    vector_weighted(a, last, jb, 2 + jb % 2, signed[a])
-            for h in range(2):
-                vector_magnitude(
-                    signed[a][:, h * half : (h + 1) * half], late[:, (1 + a) * unit + h * half : (1 + a) * unit + (h + 1) * half]
-                )
+        for t in range(PACK):
+            scalar_magnitude(0, 0, t, 4 + t)
+        scalar_magnitude(1, 0, 0, 4)
+        interleaving_root(0, 0)
 
-        z_last = [ring.tile([P, unit], BF16, name="z_last", align_bytes=64) for a in range(PASSES)]
+        image_plane[2] = held.tile([P, CHUNK], U8, name="first_unit_then_plane", align_bytes=64)
+        signed = [vector_weighted(0, 1, h) for h in range(2)]
+        vector_magnitude(0, 1, 0, signed[0])
+        gather_image_codes(2)
+        vector_magnitude(0, 1, 1, signed[1])
+        gather_image_scales(2)
 
-        def plain_root(a, h):
-            nc.scalar.activation(
-                out=z_last[a][:, h * half : (h + 1) * half],
-                in_=late[:, (1 + a) * unit + h * half : (1 + a) * unit + (h + 1) * half],
-                func=ACT.Sqrt,
-            )
+        for t in range(1, PACK):
+            scalar_magnitude(1, 0, t, 4 + t)
+        plain_root(0, 1, 0)
+        interleaving_root(1, 0)
+        plain_root(0, 1, 1)
 
-        a, c, banks = scalar_units[0]
-        scalar_magnitude(a, c, 0, banks[0], magnitudes[0])
-        for k, (a, c, banks) in enumerate(scalar_units):
-            for t in range(1, PACK):
-                scalar_magnitude(a, c, t, banks[t], magnitudes[k])
-            if k + 1 < len(scalar_units):
-                a_next, c_next, banks_next = scalar_units[k + 1]
-                scalar_magnitude(a_next, c_next, 0, banks_next[0], magnitudes[k + 1])
-            else:
-                plain_root(0, 0)
-            z = interleaving_root(magnitudes[k])
-            if k == 0:
-                later_scales = held.tile([P, (CHUNKS - 1) * CHUNK], U8, name="first", align_bytes=64)
-                for later in range(1, CHUNKS):
-                    u_scales[later] = later_scales[:, (later - 1) * CHUNK : later * CHUNK]
-                    gather_image_scales(later)
-                grouped = [quantize_update(half_k) for half_k in range(PASSES)]
-                for half_k in range(PASSES):
-                    nc.vector.quantize_mx(
-                        out=wd_codes[:, half_k, :].bitcast(FP8X4), scales=wd_plane[:, half_k, :], in_=grouped[half_k][:]
-                    )
-            if k in (1, 2):
-                vector_unit(k - 1)
-            quantize_z(z, a, c)
-        plain_root(0, 1)
-        quantize_z(z_last[0], 0, last)
-        for h in range(2):
-            plain_root(1, h)
-        quantize_z(z_last[1], 1, last)
-        y = {}
-        for nb in range(NBLOCKS):
-            y[0, nb] = project(0, nb, 4 + nb)
-        for nb in range(NBLOCKS):
-            y[1, nb] = project(1, nb, nb)
+        signed[0] = vector_weighted(1, 1, 0)
+        quantize_z(0, 0)
+        vector_magnitude(1, 1, 0, signed[0])
+        grouped = round_update(0)
+        signed[1] = vector_weighted(1, 1, 1)
+        quantize_update(0, grouped)
+        quantize_z(1, 0)
+        vector_magnitude(1, 1, 1, signed[1])
+        grouped = round_update(1)
+        quantize_z(0, 1)
+        quantize_update(1, grouped)
 
-        staged = held.tile([P, CHUNKS * NBLOCKS * CHUNK], F32, name="late")
-        for c in range(CHUNKS):
-            for nb in range(NBLOCKS):
-                if c == CHUNKS - 1:
-                    y[c, nb] = project(c, nb, 4 + nb)
-                piece = staged[:, (c * NBLOCKS + nb) * CHUNK : (c * NBLOCKS + nb + 1) * CHUNK]
-                nc.scalar.activation(out=piece, in_=y[c, nb][:], func=ACT.Tanh, bias=bias[:, nb : nb + 1])
-                nc.sync.dma_start(out=out[nb * P : (nb + 1) * P, c * CHUNK : (c + 1) * CHUNK], in_=piece)
+        for a, banks in enumerate([[0, 1, 7, 6], [0, 1, 7, 2]]):
+            for t, number in enumerate(banks):
+                scalar_magnitude(a, 2, t, number)
+            plain_root(1, 1, a)
+            interleaving_root(a, 2)
+        quantize_z(1, 1)
+        for a in range(PASSES):
+            quantize_z(a, 2)
+
+        free_order = [4, 5, 6, 3, 0, 1, 7, 2]
+        pieces = [(c, nb) for c in range(CHUNKS) for nb in range(NBLOCKS)]
+        y = [project(c, nb, number) for (c, nb), number in zip(pieces, free_order)]
+
+        results = held.tile([P, len(pieces) * CHUNK], F32, name="late_then_results")
+        for k, (c, nb) in enumerate(pieces):
+            if k >= len(free_order):
+                y.append(project(c, nb, free_order[nb]))
+            result = results[:, k * CHUNK : (k + 1) * CHUNK]
+            nc.scalar.activation(out=result, in_=y[k][:], func=ACT.Tanh, bias=bias[:, nb : nb + 1])
+            nc.sync.dma_start(out=out[nb * P : (nb + 1) * P, c * CHUNK : (c + 1) * CHUNK], in_=result)

@@ -29,8 +29,8 @@ RUN = 4
 WORD_PLANE = 4
 UNIT = PACK * CHUNK
 HALF = UNIT // 2
-HALVES = [slice(0, HALF), slice(HALF, UNIT)]
-VECTOR_BANKS = [2, 3]
+BLOCK = PACK * P
+VECTOR_BLOCKS = 2
 
 
 def load_scale_rows(nc, plane, rows, start=0):
@@ -49,6 +49,7 @@ def tile_list_visual_word_hash_kernel(
     with ExitStack() as ctx:
         held = ctx.enter_context(tc.tile_pool(name="held", bufs=1))
         ring = ctx.enter_context(tc.tile_pool(name="ring", bufs=2))
+        reused = ctx.enter_context(tc.tile_pool(name="reused", bufs=1))
         psum = ctx.enter_context(tc.psum_pool(name="psum", bufs=1))
 
         def bank(number, shape):
@@ -62,7 +63,7 @@ def tile_list_visual_word_hash_kernel(
         word_table_plane = held.tile([P, T], U8, name="word_table_plane", align_bytes=64)
         image_table_plane = held.tile([P, T2], U8, name="image_table_plane", align_bytes=64)
         word_table = held.tile([P, T], U32, name="word_table", align_bytes=64)
-        image_table = held.tile([P, T2], U32, name="image_table", align_bytes=64)
+        image_table = reused.tile([P, T2], U32, name="image_table", align_bytes=64, offset=0)
         nc.vector.memset(word_table_plane[:].bitcast(I32), 0)
         load_scale_rows(nc, word_table_plane, tab_scales[0], WORD_PLANE)
         nc.sync.dma_start(out=word_table[:].bitcast(I32), in_=tab_words[0].rearrange("p c t -> p (c t)").bitcast(I32))
@@ -80,13 +81,13 @@ def tile_list_visual_word_hash_kernel(
         nc.vector.memset(zero[:], 0.0)
         nc.scalar.activation(out=no_bias[:], in_=zero[:], func=ACT.Sqrt)
 
-        word_codes = held.tile([P, S], U32, name="word_codes", align_bytes=64)
+        word_codes = {0: held.tile([P, PASS], U32, name="word_codes0", align_bytes=64)}
         listed_plane = [held.tile([P, PASS], U8, name="listed_plane%d" % a) for a in range(PASSES)]
         word_plane = held.tile([P, S], U8, name="word_plane", align_bytes=64)
-        image_codes = held.tile([P, S2], U32, name="image_codes", align_bytes=64)
+        image_codes = [held.tile([P, CHUNK], U32, name="image_codes%d" % c, align_bytes=64) for c in range(CHUNKS)]
         image_plane = {c: held.tile([P, CHUNK], U8, name="image_plane%d" % c, align_bytes=64) for c in range(CHUNKS - 1)}
-        wd_codes = held.tile([P, PASSES, N], U32, name="wd_codes", align_bytes=64)
-        wd_plane = held.tile([P, PASSES, N], U8, name="wd_plane", align_bytes=64)
+        wd_codes = [held.tile([P, PASSES, N // 2], U32, name="wd_codes%d" % h, align_bytes=64) for h in range(2)]
+        wd_plane = [held.tile([P, PASSES, N // 2], U8, name="wd_plane%d" % h, align_bytes=64) for h in range(2)]
         z_codes = held.tile([P, PASSES, S2], U32, name="z_codes", align_bytes=64)
         z_plane = held.tile([P, PASSES, S2], U8, name="z_plane", align_bytes=64)
 
@@ -101,7 +102,7 @@ def tile_list_visual_word_hash_kernel(
 
         def gather_word_codes(a):
             nc.vector.tensor_copy(
-                word_codes[:, a * PASS : (a + 1) * PASS].rearrange("p (t m) -> p m t", t=PACK),
+                word_codes[a][:].rearrange("p (t m) -> p m t", t=PACK),
                 word_table[:].indirect(entries(word_list, a * PASS, PASS)),
             )
 
@@ -109,97 +110,108 @@ def tile_list_visual_word_hash_kernel(
             nc.vector.tensor_copy(image_plane[c][:], image_table_plane[:].indirect(entries(image_list, c * CHUNK, CHUNK)))
 
         def gather_image_codes(c):
-            nc.vector.tensor_copy(
-                image_codes[:, c * CHUNK : (c + 1) * CHUNK], image_table[:].indirect(entries(image_list, c * CHUNK, CHUNK))
-            )
+            nc.vector.tensor_copy(image_codes[c][:], image_table[:].indirect(entries(image_list, c * CHUNK, CHUNK)))
 
         def response(acc, a, t, c, first, width):
             words = slice(a * PASS + t * P, a * PASS + (t + 1) * P)
             nc.tensor.matmul_mx(
                 out=acc,
-                lhsT=word_codes[:, words].bitcast(FP8X4),
+                lhsT=word_codes[a][:, t * P : (t + 1) * P].bitcast(FP8X4),
                 lhsT_scale=word_plane[WORD_PLANE:P, words],
-                rhs=image_codes[:, c * CHUNK + first : c * CHUNK + first + width].bitcast(FP8X4),
+                rhs=image_codes[c][:, first : first + width].bitcast(FP8X4),
                 rhs_scale=image_plane[c][:, first : first + width],
                 start=True,
                 stop=True,
             )
 
-        def scalar_magnitude(a, c, t, number):
+        def scalar_magnitude(a, c, t, number, width=CHUNK):
             acc = bank(number, [P, CHUNK])
-            response(acc[:], a, t, c, 0, CHUNK)
+            first = 0
+            for part in (CHUNK, CHUNK // 2, P):
+                if width - first >= part:
+                    response(acc[:, first : first + part], a, t, c, first, part)
+                    first = first + part
             nc.scalar.activation(
-                out=magnitude[a, c][:, t * CHUNK : (t + 1) * CHUNK],
-                in_=acc[:],
+                out=magnitude[a, c][:, t * width : (t + 1) * width],
+                in_=acc[:, 0:width],
                 func=ACT.Abs,
                 bias=no_bias[:],
                 scale=weight_sq[:, a, t : t + 1],
             )
 
-        def interleaving_root(a, c):
+        def interleaving_root(a, c, width=CHUNK):
             nc.scalar.activation(
-                out=z[a, c][:].rearrange("p (g i t) -> p g t i", i=RUN, t=PACK),
-                in_=magnitude[a, c].rearrange("p (t g i) -> p g t i", i=RUN, t=PACK),
+                out=z[a, c][:, 0 : PACK * width].rearrange("p (g i t) -> p g t i", i=RUN, t=PACK),
+                in_=magnitude[a, c][:, 0 : PACK * width].rearrange("p (t g i) -> p g t i", i=RUN, t=PACK),
                 func=ACT.Sqrt,
             )
 
-        def vector_weighted(a, c, h):
+        def vector_weighted(a, c, first, banks):
             signed = ring.tile([P, HALF], F32, name="signed", bufs=3)
-            for block, number in enumerate(VECTOR_BANKS):
+            for k, number in enumerate(banks):
                 acc = bank(number, [P, PACK, P])
                 for t in range(PACK):
-                    response(acc[:, t, :], a, t, c, h * CHUNK // 2 + block * P, P)
+                    response(acc[:, t, :], a, t, c, (first + k) * P, P)
                 nc.vector.tensor_tensor(
-                    out=signed[:, block * PACK * P : (block + 1) * PACK * P].rearrange("p (j t) -> p j t", t=PACK),
+                    out=signed[:, k * BLOCK : (k + 1) * BLOCK].rearrange("p (j t) -> p j t", t=PACK),
                     in0=acc[:].rearrange("p t j -> p j t"),
                     in1=weight_sq[:, a, :].unsqueeze(1).to_broadcast([P, P, PACK]),
                     op=ALU.mult,
                 )
-            return signed
+            return signed[:, 0 : len(banks) * BLOCK]
 
-        def vector_magnitude(a, c, h, signed):
+        def vector_magnitude(a, c, first, blocks, signed):
             nc.vector.scalar_tensor_tensor(
-                out=magnitude[a, c][:, HALVES[h]], in0=signed[:], scalar=-1.0, in1=signed[:], op0=ALU.mult, op1=ALU.max
+                out=halves[a, c, first][:],
+                in0=signed,
+                scalar=-1.0,
+                in1=signed,
+                op0=ALU.mult,
+                op1=ALU.max,
             )
 
-        def plain_root(a, c, h):
-            nc.scalar.activation(out=z[a, c][:, HALVES[h]], in_=magnitude[a, c][:, HALVES[h]], func=ACT.Sqrt)
+        def plain_root(a, c, first, blocks):
+            part = slice(first * BLOCK, (first + blocks) * BLOCK)
+            nc.scalar.activation(out=z[a, c][:, part], in_=halves[a, c, first][:], func=ACT.Sqrt)
 
         def quantize_z(a, c):
             images = slice(c * CHUNK, (c + 1) * CHUNK)
             nc.vector.quantize_mx(out=z_codes[:, a, images].bitcast(FP8X4), scales=z_plane[:, a, images], in_=z[a, c][:])
 
-        def round_update(a):
-            grouped = ring.tile([P, N, PACK], BF16, name="grouped", align_bytes=64)
+        def round_update(h, name):
+            grouped = held.tile([P, PASSES, N // 2, PACK], BF16, name=name, align_bytes=64)
             nc.vector.tensor_copy(
-                out=grouped[:].rearrange("p (g i) t -> p g t i", i=RUN),
-                in_=wd_raw[:, a].rearrange("p t (g i) -> p g t i", i=RUN),
+                out=grouped[:].rearrange("p a (g i) t -> p a g t i", i=RUN),
+                in_=wd_raw[:, :, :, h * N // 2 : (h + 1) * N // 2].rearrange("p a t (g i) -> p a g t i", i=RUN),
             )
             return grouped
 
-        def quantize_update(a, grouped):
+        def quantize_update(h, grouped):
             nc.vector.quantize_mx(
-                out=wd_codes[:, a, :].bitcast(FP8X4), scales=wd_plane[:, a, :], in_=grouped[:].rearrange("p n t -> p (n t)")
+                out=wd_codes[h][:].rearrange("p a n -> p (a n)").bitcast(FP8X4),
+                scales=wd_plane[h][:].rearrange("p a n -> p (a n)"),
+                in_=grouped[:].rearrange("p a n t -> p (a n t)"),
             )
 
         def project(c, nb, number):
             acc = bank(number, [P, CHUNK])
             images = slice(c * CHUNK, (c + 1) * CHUNK)
-            rows = slice(nb * P, (nb + 1) * P)
             for a in range(PASSES):
                 nc.tensor.matmul_mx(
                     out=acc[:],
                     lhsT=wb_codes[:, a, 2 * nb * P : 2 * (nb + 1) * P].bitcast(FP4X4),
-                    lhsT_scale=wb_plane[:, a, rows],
+                    lhsT_scale=wb_plane[:, a, nb * P : (nb + 1) * P],
                     rhs=z_codes[:, a, images].bitcast(FP8X4),
                     rhs_scale=z_plane[:, a, images],
                     start=(a == 0),
                     stop=False,
                 )
+            rows = slice(nb % 2 * P, (nb % 2 + 1) * P)
+            for a in range(PASSES):
                 nc.tensor.matmul_mx(
                     out=acc[:],
-                    lhsT=wd_codes[:, a, rows].bitcast(FP8X4),
-                    lhsT_scale=wd_plane[:, a, rows],
+                    lhsT=wd_codes[nb // 2][:, a, rows].bitcast(FP8X4),
+                    lhsT_scale=wd_plane[nb // 2][:, a, rows],
                     rhs=z_codes[:, a, images].bitcast(FP8X4),
                     rhs_scale=z_plane[:, a, images],
                     start=False,
@@ -213,7 +225,12 @@ def tile_list_visual_word_hash_kernel(
             reorder_word_scales(a)
         gather_word_codes(0)
         gather_image_scales(0)
-        gather_image_codes(0)
+        gather_image_scales(1)
+        for c in range(CHUNKS):
+            gather_image_codes(c)
+
+        word_codes[1] = reused.tile([P, PASS], U32, name="word_codes1", align_bytes=64, offset=0)
+        image_plane[2] = reused.tile([P, CHUNK], U8, name="image_plane2", align_bytes=64, offset=PACK * PASS)
         gather_word_codes(1)
 
         wd_raw = held.tile([P, PASSES, PACK, N], F32, name="wd_raw")
@@ -228,71 +245,79 @@ def tile_list_visual_word_hash_kernel(
         with nc.allow_non_contiguous_dma(reason="one bias value a partition and block of output rows"):
             nc.sync.dma_start(out=bias[:], in_=b.rearrange("(nb p) -> p nb", p=P))
 
-        gather_image_scales(1)
-        gather_image_codes(1)
-
-        late = held.tile([P, 3 * UNIT], F32, name="late_then_results")
-        first_unit = held.tile([P, UNIT], F32, name="first_unit_then_plane", align_bytes=64)
+        late = held.tile([P, 2 * UNIT], F32, name="late_then_results")
         z = {
             (a, c): held.tile([P, UNIT], BF16, name="z%d%d" % (a, c), align_bytes=64)
             for a in range(PASSES)
             for c in range(CHUNKS)
         }
         magnitude = {
-            (0, 0): first_unit[:],
-            (1, 0): held.tile([P, UNIT], F32, name="magnitude10")[:],
+            (0, 0): held.tile([P, UNIT], F32, name="magnitude00")[:],
             (0, 1): held.tile([P, UNIT], F32, name="magnitude01")[:],
-            (1, 1): late[:, 0:UNIT],
-            (0, 2): late[:, UNIT : 2 * UNIT],
-            (1, 2): late[:, 2 * UNIT : 3 * UNIT],
+            (0, 2): late[:, 0:UNIT],
+            (1, 2): late[:, UNIT : 2 * UNIT],
         }
 
+        halves = {
+            (1, 0, 0): held.tile([P, HALF], F32, name="half100"),
+            (1, 0, 2): held.tile([P, HALF], F32, name="half102"),
+            (1, 1, 0): held.tile([P, HALF], F32, name="half110"),
+            (1, 1, 2): held.tile([P, HALF], F32, name="half112", align_bytes=64),
+        }
+        shared = CHUNK - VECTOR_BLOCKS * P
         for t in range(PACK):
             scalar_magnitude(0, 0, t, 4 + t)
-        scalar_magnitude(1, 0, 0, 4)
+        scalar_magnitude(0, 1, 0, 0)
         interleaving_root(0, 0)
+        for t in range(1, PACK):
+            scalar_magnitude(0, 1, t, t)
 
-        image_plane[2] = held.tile([P, CHUNK], U8, name="first_unit_then_plane", align_bytes=64)
-        signed = [vector_weighted(0, 1, h) for h in range(2)]
-        vector_magnitude(0, 1, 0, signed[0])
-        gather_image_codes(2)
-        vector_magnitude(0, 1, 1, signed[1])
         gather_image_scales(2)
+        signed = [vector_weighted(1, 0, 0, [4, 5]), vector_weighted(1, 0, 2, [6, 7])]
+        vector_magnitude(1, 0, 0, 2, signed[0])
+        vector_magnitude(1, 0, 2, 2, signed[1])
+        quantize_z(0, 0)
+
+        scalar_magnitude(0, 2, 0, 0)
+        interleaving_root(0, 1)
+        plain_root(1, 0, 0, 2)
+        plain_root(1, 0, 2, 2)
+
+        signed = [vector_weighted(1, 1, 0, [6, 7]), vector_weighted(1, 1, 2, [6, 7])]
+        vector_magnitude(1, 1, 0, 2, signed[0])
+        vector_magnitude(1, 1, 2, 2, signed[1])
+        grouped = round_update(0, "update0")
+        quantize_z(1, 0)
+        quantize_update(0, grouped)
 
         for t in range(1, PACK):
-            scalar_magnitude(1, 0, t, 4 + t)
-        plain_root(0, 1, 0)
-        interleaving_root(1, 0)
-        plain_root(0, 1, 1)
-
-        signed[0] = vector_weighted(1, 1, 0)
-        quantize_z(0, 0)
-        vector_magnitude(1, 1, 0, signed[0])
-        grouped = round_update(0)
-        signed[1] = vector_weighted(1, 1, 1)
-        quantize_update(0, grouped)
-        quantize_z(1, 0)
-        vector_magnitude(1, 1, 1, signed[1])
-        grouped = round_update(1)
+            scalar_magnitude(0, 2, t, t)
+        for t in range(PACK):
+            scalar_magnitude(1, 2, t, t, shared)
+        plain_root(1, 1, 0, 2)
+        plain_root(1, 1, 2, 2)
+        interleaving_root(0, 2)
+        signed[0] = vector_weighted(1, 2, PACK - VECTOR_BLOCKS, [6, 7][:VECTOR_BLOCKS])
         quantize_z(0, 1)
-        quantize_update(1, grouped)
+        halves[1, 2, PACK - VECTOR_BLOCKS] = late[:, UNIT + PACK * shared : 2 * UNIT]
+        vector_magnitude(1, 2, PACK - VECTOR_BLOCKS, VECTOR_BLOCKS, signed[0])
+        plain_root(1, 2, PACK - VECTOR_BLOCKS, VECTOR_BLOCKS)
+        interleaving_root(1, 2, shared)
 
-        for a, banks in enumerate([[0, 1, 7, 6], [0, 1, 7, 2]]):
-            for t, number in enumerate(banks):
-                scalar_magnitude(a, 2, t, number)
-            plain_root(1, 1, a)
-            interleaving_root(a, 2)
+        grouped = round_update(1, "half112")
         quantize_z(1, 1)
-        for a in range(PASSES):
-            quantize_z(a, 2)
+        quantize_update(1, grouped)
+        quantize_z(0, 2)
+        quantize_z(1, 2)
 
-        free_order = [4, 5, 6, 3, 0, 1, 7, 2]
-        pieces = [(c, nb) for c in range(CHUNKS) for nb in range(NBLOCKS)]
-        y = [project(c, nb, number) for (c, nb), number in zip(pieces, free_order)]
+        pieces = [(c, nb) for c in range(2) for nb in range(NBLOCKS)]
+        free_order = [4, 5, 6, 7, 0, 1, 2, 3]
+        y = [project(c, nb, number) for number, (c, nb) in zip(free_order, pieces)]
+        pieces = pieces + [(2, nb) for nb in range(NBLOCKS)]
 
         results = held.tile([P, len(pieces) * CHUNK], F32, name="late_then_results")
         for k, (c, nb) in enumerate(pieces):
-            if k >= len(free_order):
+            if k >= len(y):
                 y.append(project(c, nb, free_order[nb]))
             result = results[:, k * CHUNK : (k + 1) * CHUNK]
             nc.scalar.activation(out=result, in_=y[k][:], func=ACT.Tanh, bias=bias[:, nb : nb + 1])

@@ -30,6 +30,7 @@ WORD_PLANE = 4
 UNIT = PACK * CHUNK
 HALF = UNIT // 2
 BLOCK = PACK * P
+UPDATE_PARTS = [(0, 2), (2, 1), (3, 1)]
 VECTOR_BLOCKS = 2
 
 
@@ -58,23 +59,25 @@ def tile_list_visual_word_hash_kernel(
         word_list = held.tile([P, S // LIST_ROWS], U16, name="word_list")
         image_list = held.tile([P, S2 // LIST_ROWS], U16, name="image_list")
         nc.sync.dma_start(word_list[:], offs)
-        nc.sync.dma_start(image_list[:], offs2)
 
         word_table_plane = held.tile([P, T], U8, name="word_table_plane", align_bytes=64)
         image_table_plane = held.tile([P, T2], U8, name="image_table_plane", align_bytes=64)
         word_table = held.tile([P, T], U32, name="word_table", align_bytes=64)
         image_table = reused.tile([P, T2], U32, name="image_table", align_bytes=64, offset=0)
         nc.vector.memset(word_table_plane[:].bitcast(I32), 0)
+        table_words = tab_words[0].rearrange("p c t -> p (c t)").bitcast(I32)
+        nc.sync.dma_start(out=word_table[:, 0 : T // 4].bitcast(I32), in_=table_words[:, 0 : T // 4])
         load_scale_rows(nc, word_table_plane, tab_scales[0], WORD_PLANE)
-        nc.sync.dma_start(out=word_table[:].bitcast(I32), in_=tab_words[0].rearrange("p c t -> p (c t)").bitcast(I32))
+        nc.sync.dma_start(out=word_table[:, T // 4 : T].bitcast(I32), in_=table_words[:, T // 4 : T])
+        nc.sync.dma_start(image_list[:], offs2)
         nc.vector.memset(image_table_plane[:].bitcast(I32), 0)
         load_scale_rows(nc, image_table_plane, tab2_scales[0])
         nc.sync.dma_start(out=image_table[:].bitcast(I32), in_=tab2_words[0].rearrange("p c t -> p (c t)").bitcast(I32))
 
         weight = held.tile([P, PASSES, PACK], F32, name="weight")
         weight_sq = held.tile([P, PASSES, PACK], F32, name="weight_sq")
-        nc.gpsimd.dma_start(out=weight[:], in_=wt.rearrange("(a p t) -> p a t", p=P, t=PACK))
-        nc.gpsimd.tensor_tensor(out=weight_sq[:], in0=weight[:], in1=weight[:], op=ALU.mult)
+        nc.sync.dma_start(out=weight[:], in_=wt.rearrange("(a p t) -> p a t", p=P, t=PACK))
+        nc.scalar.activation(out=weight_sq[:], in_=weight[:], func=ACT.Square)
 
         zero = held.tile([P, 1], F32, name="zero")
         no_bias = held.tile([P, 1], F32, name="no_bias")
@@ -82,22 +85,27 @@ def tile_list_visual_word_hash_kernel(
         nc.scalar.activation(out=no_bias[:], in_=zero[:], func=ACT.Sqrt)
 
         word_codes = {0: held.tile([P, PASS], U32, name="word_codes0", align_bytes=64)}
-        listed_plane = [held.tile([P, PASS], U8, name="listed_plane%d" % a) for a in range(PASSES)]
+        listed_plane = held.tile([P, S], U8, name="listed_plane")
         word_plane = held.tile([P, S], U8, name="word_plane", align_bytes=64)
         image_codes = [held.tile([P, CHUNK], U32, name="image_codes%d" % c, align_bytes=64) for c in range(CHUNKS)]
         image_plane = {c: held.tile([P, CHUNK], U8, name="image_plane%d" % c, align_bytes=64) for c in range(CHUNKS - 1)}
-        wd_codes = [held.tile([P, PASSES, N // 2], U32, name="wd_codes%d" % h, align_bytes=64) for h in range(2)]
-        wd_plane = [held.tile([P, PASSES, N // 2], U8, name="wd_plane%d" % h, align_bytes=64) for h in range(2)]
+        wd_codes, wd_plane = {}, {}
+        for first, blocks in UPDATE_PARTS:
+            codes = held.tile([P, PASSES, blocks, P], U32, name="wd_codes%d" % first, align_bytes=64)
+            plane = held.tile([P, PASSES, blocks, P], U8, name="wd_plane%d" % first, align_bytes=64)
+            wd_codes[first], wd_plane[first] = codes, plane
         z_codes = held.tile([P, PASSES, S2], U32, name="z_codes", align_bytes=64)
         z_plane = held.tile([P, PASSES, S2], U8, name="z_plane", align_bytes=64)
 
         def gather_word_scales(a):
-            nc.vector.tensor_copy(listed_plane[a][:], word_table_plane[:].indirect(entries(word_list, a * PASS, PASS)))
+            nc.vector.tensor_copy(
+                listed_plane[:, a * PASS : (a + 1) * PASS], word_table_plane[:].indirect(entries(word_list, a * PASS, PASS))
+            )
 
         def reorder_word_scales(a):
             nc.vector.tensor_copy(
                 out=word_plane[:, a * PASS : (a + 1) * PASS].rearrange("p (t m) -> p t m", t=PACK),
-                in_=listed_plane[a][:].rearrange("p (m t) -> p t m", t=PACK),
+                in_=listed_plane[:, a * PASS : (a + 1) * PASS].rearrange("p (m t) -> p t m", t=PACK),
             )
 
         def gather_word_codes(a):
@@ -147,7 +155,7 @@ def tile_list_visual_word_hash_kernel(
             )
 
         def vector_weighted(a, c, first, banks):
-            signed = ring.tile([P, HALF], F32, name="signed", bufs=3)
+            signed = ring.tile([P, len(banks) * BLOCK], F32, name="signed", bufs=3)
             for k, number in enumerate(banks):
                 acc = bank(number, [P, PACK, P])
                 for t in range(PACK):
@@ -178,18 +186,20 @@ def tile_list_visual_word_hash_kernel(
             images = slice(c * CHUNK, (c + 1) * CHUNK)
             nc.vector.quantize_mx(out=z_codes[:, a, images].bitcast(FP8X4), scales=z_plane[:, a, images], in_=z[a, c][:])
 
-        def round_update(h, name):
-            grouped = held.tile([P, PASSES, N // 2, PACK], BF16, name=name, align_bytes=64)
+        def round_update(part, name):
+            first, blocks = UPDATE_PARTS[part]
+            grouped = held.tile([P, PASSES, blocks * P, PACK], BF16, name=name, align_bytes=64)
             nc.vector.tensor_copy(
                 out=grouped[:].rearrange("p a (g i) t -> p a g t i", i=RUN),
-                in_=wd_raw[:, :, :, h * N // 2 : (h + 1) * N // 2].rearrange("p a t (g i) -> p a g t i", i=RUN),
+                in_=wd_raw[:, :, :, first * P : (first + blocks) * P].rearrange("p a t (g i) -> p a g t i", i=RUN),
             )
             return grouped
 
-        def quantize_update(h, grouped):
+        def quantize_update(part, grouped):
+            first = UPDATE_PARTS[part][0]
             nc.vector.quantize_mx(
-                out=wd_codes[h][:].rearrange("p a n -> p (a n)").bitcast(FP8X4),
-                scales=wd_plane[h][:].rearrange("p a n -> p (a n)"),
+                out=wd_codes[first][:].rearrange("p a b n -> p (a b n)").bitcast(FP8X4),
+                scales=wd_plane[first][:].rearrange("p a b n -> p (a b n)"),
                 in_=grouped[:].rearrange("p a n t -> p (a n t)"),
             )
 
@@ -206,12 +216,12 @@ def tile_list_visual_word_hash_kernel(
                     start=(a == 0),
                     stop=False,
                 )
-            rows = slice(nb % 2 * P, (nb % 2 + 1) * P)
+            first = max(f for f, blocks in UPDATE_PARTS if f <= nb)
             for a in range(PASSES):
                 nc.tensor.matmul_mx(
                     out=acc[:],
-                    lhsT=wd_codes[nb // 2][:, a, rows].bitcast(FP8X4),
-                    lhsT_scale=wd_plane[nb // 2][:, a, rows],
+                    lhsT=wd_codes[first][:, a, nb - first].bitcast(FP8X4),
+                    lhsT_scale=wd_plane[first][:, a, nb - first],
                     rhs=z_codes[:, a, images].bitcast(FP8X4),
                     rhs_scale=z_plane[:, a, images],
                     start=False,
@@ -261,7 +271,7 @@ def tile_list_visual_word_hash_kernel(
         halves = {
             (1, 0, 0): held.tile([P, HALF], F32, name="half100"),
             (1, 0, 2): held.tile([P, HALF], F32, name="half102"),
-            (1, 1, 0): held.tile([P, HALF], F32, name="half110"),
+            (1, 1, 0): held.tile([P, HALF], F32, name="half110", align_bytes=64),
             (1, 1, 2): held.tile([P, HALF], F32, name="half112", align_bytes=64),
         }
         shared = CHUNK - VECTOR_BLOCKS * P
@@ -297,16 +307,17 @@ def tile_list_visual_word_hash_kernel(
         plain_root(1, 1, 0, 2)
         plain_root(1, 1, 2, 2)
         interleaving_root(0, 2)
-        signed[0] = vector_weighted(1, 2, PACK - VECTOR_BLOCKS, [6, 7][:VECTOR_BLOCKS])
+        signed[0] = vector_weighted(1, 2, PACK - VECTOR_BLOCKS, [6, 7])
         quantize_z(0, 1)
         halves[1, 2, PACK - VECTOR_BLOCKS] = late[:, UNIT + PACK * shared : 2 * UNIT]
         vector_magnitude(1, 2, PACK - VECTOR_BLOCKS, VECTOR_BLOCKS, signed[0])
-        plain_root(1, 2, PACK - VECTOR_BLOCKS, VECTOR_BLOCKS)
         interleaving_root(1, 2, shared)
+        plain_root(1, 2, PACK - VECTOR_BLOCKS, VECTOR_BLOCKS)
 
-        grouped = round_update(1, "half112")
         quantize_z(1, 1)
-        quantize_update(1, grouped)
+        grouped = [round_update(1, "half110"), round_update(2, "half112")]
+        quantize_update(1, grouped[0])
+        quantize_update(2, grouped[1])
         quantize_z(0, 2)
         quantize_z(1, 2)
 

@@ -31,7 +31,7 @@ UNIT = PACK * CHUNK
 HALF = UNIT // 2
 BLOCK = PACK * P
 UPDATE_PARTS = [(0, 2), (2, 1), (3, 1)]
-VECTOR_BLOCKS = 2
+VECTOR_BLOCKS = 3
 
 
 def load_scale_rows(nc, plane, rows, start=0):
@@ -132,20 +132,20 @@ def tile_list_visual_word_hash_kernel(
                 stop=True,
             )
 
-        def scalar_magnitude(a, c, t, number, width=CHUNK):
-            acc = bank(number, [P, CHUNK])
-            first = 0
-            for part in (CHUNK, CHUNK // 2, P):
-                if width - first >= part:
-                    response(acc[:, first : first + part], a, t, c, first, part)
-                    first = first + part
+        def scalar_magnitude(a, c, t, acc):
+            width = acc.shape[1]
             nc.scalar.activation(
                 out=magnitude[a, c][:, t * width : (t + 1) * width],
-                in_=acc[:, 0:width],
+                in_=acc,
                 func=ACT.Abs,
                 bias=no_bias[:],
                 scale=weight_sq[:, a, t : t + 1],
             )
+
+        def scalar_slot(a, c, t, number):
+            acc = bank(number, [P, CHUNK])
+            response(acc[:], a, t, c, 0, CHUNK)
+            scalar_magnitude(a, c, t, acc[:])
 
         def interleaving_root(a, c, width=CHUNK):
             nc.scalar.activation(
@@ -170,7 +170,7 @@ def tile_list_visual_word_hash_kernel(
 
         def vector_magnitude(a, c, first, blocks, signed):
             nc.vector.scalar_tensor_tensor(
-                out=halves[a, c, first][:],
+                out=halves[a, c, first][:, 0 : blocks * BLOCK],
                 in0=signed,
                 scalar=-1.0,
                 in1=signed,
@@ -206,26 +206,19 @@ def tile_list_visual_word_hash_kernel(
         def project(c, nb, number):
             acc = bank(number, [P, CHUNK])
             images = slice(c * CHUNK, (c + 1) * CHUNK)
-            for a in range(PASSES):
-                nc.tensor.matmul_mx(
-                    out=acc[:],
-                    lhsT=wb_codes[:, a, 2 * nb * P : 2 * (nb + 1) * P].bitcast(FP4X4),
-                    lhsT_scale=wb_plane[:, a, nb * P : (nb + 1) * P],
-                    rhs=z_codes[:, a, images].bitcast(FP8X4),
-                    rhs_scale=z_plane[:, a, images],
-                    start=(a == 0),
-                    stop=False,
-                )
             first = max(f for f, blocks in UPDATE_PARTS if f <= nb)
-            for a in range(PASSES):
+            stored = [(wb_codes[:, a, 2 * nb * P : 2 * (nb + 1) * P].bitcast(FP4X4), wb_plane[:, a, nb * P : (nb + 1) * P], a) for a in range(PASSES)]
+            update = [(wd_codes[first][:, a, nb - first].bitcast(FP8X4), wd_plane[first][:, a, nb - first], a) for a in range(PASSES)]
+            passes = stored + update if first else [stored[0], update[0], stored[1], update[1]]
+            for k, (codes, plane, a) in enumerate(passes):
                 nc.tensor.matmul_mx(
                     out=acc[:],
-                    lhsT=wd_codes[first][:, a, nb - first].bitcast(FP8X4),
-                    lhsT_scale=wd_plane[first][:, a, nb - first],
+                    lhsT=codes,
+                    lhsT_scale=plane,
                     rhs=z_codes[:, a, images].bitcast(FP8X4),
                     rhs_scale=z_plane[:, a, images],
-                    start=False,
-                    stop=(a == PASSES - 1),
+                    start=(k == 0),
+                    stop=(k == len(passes) - 1),
                 )
             return acc
 
@@ -276,11 +269,11 @@ def tile_list_visual_word_hash_kernel(
         }
         shared = CHUNK - VECTOR_BLOCKS * P
         for t in range(PACK):
-            scalar_magnitude(0, 0, t, 4 + t)
-        scalar_magnitude(0, 1, 0, 0)
+            scalar_slot(0, 0, t, 4 + t)
+        scalar_slot(0, 1, 0, 0)
         interleaving_root(0, 0)
         for t in range(1, PACK):
-            scalar_magnitude(0, 1, t, t)
+            scalar_slot(0, 1, t, t)
 
         gather_image_scales(2)
         signed = [vector_weighted(1, 0, 0, [4, 5]), vector_weighted(1, 0, 2, [6, 7])]
@@ -288,48 +281,57 @@ def tile_list_visual_word_hash_kernel(
         vector_magnitude(1, 0, 2, 2, signed[1])
         quantize_z(0, 0)
 
-        scalar_magnitude(0, 2, 0, 0)
+        scalar_slot(0, 2, 0, 0)
         interleaving_root(0, 1)
         plain_root(1, 0, 0, 2)
         plain_root(1, 0, 2, 2)
 
-        signed = [vector_weighted(1, 1, 0, [6, 7]), vector_weighted(1, 1, 2, [6, 7])]
-        vector_magnitude(1, 1, 0, 2, signed[0])
-        vector_magnitude(1, 1, 2, 2, signed[1])
+
+        signed = [vector_weighted(1, 1, 0, [6, 7])]
+
         grouped = round_update(0, "update0")
-        quantize_z(1, 0)
+        signed.append(vector_weighted(1, 1, 2, [6, 7]))
+        vector_magnitude(1, 1, 0, 2, signed[0])
         quantize_update(0, grouped)
+        vector_magnitude(1, 1, 2, 2, signed[1])
+        quantize_z(1, 0)
+        quantize_z(0, 1)
 
         for t in range(1, PACK):
-            scalar_magnitude(0, 2, t, t)
+            scalar_slot(0, 2, t, t)
+        first_block = bank(0, [P, PACK, P])
         for t in range(PACK):
-            scalar_magnitude(1, 2, t, t, shared)
+            response(first_block[:, t, :], 1, t, 2, 0, P)
+        for t in range(PACK):
+            scalar_magnitude(1, 2, t, first_block[:, t, :])
         plain_root(1, 1, 0, 2)
         plain_root(1, 1, 2, 2)
         interleaving_root(0, 2)
-        signed[0] = vector_weighted(1, 2, PACK - VECTOR_BLOCKS, [6, 7])
-        quantize_z(0, 1)
-        halves[1, 2, PACK - VECTOR_BLOCKS] = late[:, UNIT + PACK * shared : 2 * UNIT]
-        vector_magnitude(1, 2, PACK - VECTOR_BLOCKS, VECTOR_BLOCKS, signed[0])
-        interleaving_root(1, 2, shared)
-        plain_root(1, 2, PACK - VECTOR_BLOCKS, VECTOR_BLOCKS)
-
+        signed = [vector_weighted(1, 2, 1, [6, 7]), vector_weighted(1, 2, 3, [2])]
+        halves[1, 2, 1] = late[:, UNIT + BLOCK : UNIT + 3 * BLOCK]
+        halves[1, 2, 3] = late[:, UNIT + 3 * BLOCK : 2 * UNIT]
+        vector_magnitude(1, 2, 1, 2, signed[0])
         quantize_z(1, 1)
-        grouped = [round_update(1, "half110"), round_update(2, "half112")]
-        quantize_update(1, grouped[0])
-        quantize_update(2, grouped[1])
-        quantize_z(0, 2)
-        quantize_z(1, 2)
+        vector_magnitude(1, 2, 3, 1, signed[1])
+        interleaving_root(1, 2, shared)
+        plain_root(1, 2, 1, 2)
+        plain_root(1, 2, 3, 1)
 
-        pieces = [(c, nb) for c in range(2) for nb in range(NBLOCKS)]
-        free_order = [4, 5, 6, 7, 0, 1, 2, 3]
+        quantize_z(0, 2)
+        grouped = [round_update(1, "z11")]
+        quantize_z(1, 2)
+        quantize_update(1, grouped[0])
+        grouped.append(round_update(2, "z12"))
+        quantize_update(2, grouped[1])
+
+        pieces = [(0, 0), (0, 1), (1, 0), (1, 1), (2, 0), (2, 1), (0, 2), (1, 2), (2, 2), (0, 3), (1, 3), (2, 3)]
+        free_order = [4, 5, 0, 1, 6, 7, 3, 2]
         y = [project(c, nb, number) for number, (c, nb) in zip(free_order, pieces)]
-        pieces = pieces + [(2, nb) for nb in range(NBLOCKS)]
 
         results = held.tile([P, len(pieces) * CHUNK], F32, name="late_then_results")
         for k, (c, nb) in enumerate(pieces):
             if k >= len(y):
-                y.append(project(c, nb, free_order[nb]))
+                y.append(project(c, nb, free_order[k - len(free_order)]))
             result = results[:, k * CHUNK : (k + 1) * CHUNK]
             nc.scalar.activation(out=result, in_=y[k][:], func=ACT.Tanh, bias=bias[:, nb : nb + 1])
             nc.sync.dma_start(out=out[nb * P : (nb + 1) * P, c * CHUNK : (c + 1) * CHUNK], in_=result)

@@ -80,9 +80,9 @@ def tile_list_visual_word_hash_kernel(
         nc.scalar.activation(out=weight_sq[:], in_=weight[:], func=ACT.Square)
 
         zero = held.tile([P, 1], F32, name="zero")
-        no_bias = held.tile([P, 1], F32, name="no_bias")
+        unread = held.tile([P, 1], F32, name="unread")
         nc.vector.memset(zero[:], 0.0)
-        nc.scalar.activation(out=no_bias[:], in_=zero[:], func=ACT.Sqrt)
+        nc.scalar.activation(out=unread[:], in_=zero[:], func=ACT.Sqrt)
 
         word_codes = {0: held.tile([P, PASS], U32, name="word_codes0", align_bytes=64)}
         listed_plane = held.tile([P, S], U8, name="listed_plane")
@@ -138,7 +138,6 @@ def tile_list_visual_word_hash_kernel(
                 out=magnitude[a, c][:, t * width : (t + 1) * width],
                 in_=acc,
                 func=ACT.Abs,
-                bias=no_bias[:],
                 scale=weight_sq[:, a, t : t + 1],
             )
 
@@ -332,6 +331,8 @@ def tile_list_visual_word_hash_kernel(
         for k, (c, nb) in enumerate(pieces):
             if k >= len(y):
                 y.append(project(c, nb, free_order[k - len(free_order)]))
-            result = results[:, k * CHUNK : (k + 1) * CHUNK]
-            nc.scalar.activation(out=result, in_=y[k][:], func=ACT.Tanh, bias=bias[:, nb : nb + 1])
-            nc.sync.dma_start(out=out[nb * P : (nb + 1) * P, c * CHUNK : (c + 1) * CHUNK], in_=result)
+            queue = nc.scalar if k % 2 == 1 else nc.sync
+            for first, last in [(0, P), (P, CHUNK)] if k == 0 else [(0, CHUNK)]:
+                result = results[:, k * CHUNK + first : k * CHUNK + last]
+                nc.scalar.activation(out=result, in_=y[k][:, first:last], func=ACT.Tanh, bias=bias[:, nb : nb + 1])
+                queue.dma_start(out=out[nb * P : (nb + 1) * P, c * CHUNK + first : c * CHUNK + last], in_=result)

@@ -26,7 +26,8 @@ NBLOCKS = N // P
 LIST_ROWS = 16
 QUAD = 32
 RUN = 4
-WORD_PLANE = 4
+SCALE_ROWS = 16
+ROWS_AT = P - SCALE_ROWS
 UNIT = PACK * CHUNK
 HALF = UNIT // 2
 BLOCK = PACK * P
@@ -34,9 +35,9 @@ UPDATE_PARTS = [(0, 2), (2, 1), (3, 1)]
 VECTOR_BLOCKS = 3
 
 
-def load_scale_rows(nc, plane, rows, start=0):
+def move_scale_rows(queue, plane, rows):
     for r in range(PACK):
-        nc.sync.dma_start(out=plane[start + r : P : QUAD].bitcast(I32), in_=rows[r::PACK].bitcast(I32))
+        queue.dma_start(out=plane[r:P:QUAD].bitcast(I32), in_=rows[ROWS_AT + r : P : PACK].bitcast(I32))
 
 
 def entries(list_tile, first, count):
@@ -58,20 +59,23 @@ def tile_list_visual_word_hash_kernel(
 
         word_list = held.tile([P, S // LIST_ROWS], U16, name="word_list")
         image_list = held.tile([P, S2 // LIST_ROWS], U16, name="image_list")
-        nc.sync.dma_start(word_list[:], offs)
+        nc.sync.dma_start(image_list[:], offs2)
 
-        word_table_plane = held.tile([P, T], U8, name="word_table_plane", align_bytes=64)
-        image_table_plane = held.tile([P, T2], U8, name="image_table_plane", align_bytes=64)
+        word_table_rows = held.tile([P, T], U8, name="word_table_rows", align_bytes=64)
+        image_table_rows = held.tile([P, T2], U8, name="image_table_rows", align_bytes=64)
         word_table = held.tile([P, T], U32, name="word_table", align_bytes=64)
         image_table = reused.tile([P, T2], U32, name="image_table", align_bytes=64, offset=0)
-        nc.vector.memset(word_table_plane[:].bitcast(I32), 0)
-        table_words = tab_words[0].rearrange("p c t -> p (c t)").bitcast(I32)
-        nc.sync.dma_start(out=word_table[:, 0 : T // 4].bitcast(I32), in_=table_words[:, 0 : T // 4])
-        load_scale_rows(nc, word_table_plane, tab_scales[0], WORD_PLANE)
-        nc.sync.dma_start(out=word_table[:, T // 4 : T].bitcast(I32), in_=table_words[:, T // 4 : T])
-        nc.sync.dma_start(image_list[:], offs2)
-        nc.vector.memset(image_table_plane[:].bitcast(I32), 0)
-        load_scale_rows(nc, image_table_plane, tab2_scales[0])
+        early_planes = held.tile([P, PASS + 2 * CHUNK], U8, name="early_planes", align_bytes=64)
+        middle_planes = held.tile([P, PASS + PASSES * N], U8, name="middle_planes", align_bytes=64)
+        late_plane = held.tile([P, CHUNK], U8, name="late_plane", align_bytes=64)
+        nc.vector.memset(image_table_rows[0:ROWS_AT].bitcast(I32), 0)
+        nc.vector.memset(word_table_rows[0:ROWS_AT].bitcast(I32), 0)
+        for plane in (early_planes, middle_planes, late_plane):
+            nc.gpsimd.memset(plane[:].bitcast(I32), 0)
+        nc.sync.dma_start(out=image_table_rows[ROWS_AT:P].bitcast(I32), in_=tab2_scales[0].bitcast(I32))
+        nc.sync.dma_start(word_list[:], offs)
+        nc.sync.dma_start(out=word_table_rows[ROWS_AT:P].bitcast(I32), in_=tab_scales[0].bitcast(I32))
+        nc.sync.dma_start(out=word_table[:].bitcast(I32), in_=tab_words[0].rearrange("p c t -> p (c t)").bitcast(I32))
         nc.sync.dma_start(out=image_table[:].bitcast(I32), in_=tab2_words[0].rearrange("p c t -> p (c t)").bitcast(I32))
 
         weight = held.tile([P, PASSES, PACK], F32, name="weight")
@@ -85,10 +89,14 @@ def tile_list_visual_word_hash_kernel(
         nc.scalar.activation(out=unread[:], in_=zero[:], func=ACT.Sqrt)
 
         word_codes = {0: held.tile([P, PASS], U32, name="word_codes0", align_bytes=64)}
-        listed_plane = held.tile([P, S], U8, name="listed_plane")
-        word_plane = held.tile([P, S], U8, name="word_plane", align_bytes=64)
+        listed_rows = [held.tile([P, PASS], U8, name="listed_rows%d" % a) for a in range(PASSES)]
+        early_image_rows = held.tile([P, 2 * CHUNK], U8, name="early_image_rows")
+        early_rows = reused.tile([P, PASS + 2 * CHUNK], U8, name="early_rows", align_bytes=64, offset=PACK * T2)
+        middle_rows = held.tile([P, PASS + PASSES * N], U8, name="middle_rows")
+        word_plane = [early_planes[:, 0:PASS], middle_planes[:, 0:PASS]]
+        image_plane = [early_planes[:, PASS : PASS + CHUNK], early_planes[:, PASS + CHUNK :], late_plane[:]]
+        wb_plane = middle_planes[:, PASS:].rearrange("p (a n) -> p a n", a=PASSES)
         image_codes = [held.tile([P, CHUNK], U32, name="image_codes%d" % c, align_bytes=64) for c in range(CHUNKS)]
-        image_plane = {c: held.tile([P, CHUNK], U8, name="image_plane%d" % c, align_bytes=64) for c in range(CHUNKS - 1)}
         wd_codes, wd_plane = {}, {}
         for first, blocks in UPDATE_PARTS:
             codes = held.tile([P, PASSES, blocks, P], U32, name="wd_codes%d" % first, align_bytes=64)
@@ -97,15 +105,13 @@ def tile_list_visual_word_hash_kernel(
         z_codes = held.tile([P, PASSES, S2], U32, name="z_codes", align_bytes=64)
         z_plane = held.tile([P, PASSES, S2], U8, name="z_plane", align_bytes=64)
 
-        def gather_word_scales(a):
-            nc.vector.tensor_copy(
-                listed_plane[:, a * PASS : (a + 1) * PASS], word_table_plane[:].indirect(entries(word_list, a * PASS, PASS))
-            )
+        def gather_word_rows(a):
+            nc.vector.tensor_copy(listed_rows[a][:], word_table_rows[:].indirect(entries(word_list, a * PASS, PASS)))
 
-        def reorder_word_scales(a):
+        def reorder_word_rows(a, rows):
             nc.vector.tensor_copy(
-                out=word_plane[:, a * PASS : (a + 1) * PASS].rearrange("p (t m) -> p t m", t=PACK),
-                in_=listed_plane[:, a * PASS : (a + 1) * PASS].rearrange("p (m t) -> p t m", t=PACK),
+                out=rows[:, 0:PASS].rearrange("p (t m) -> p t m", t=PACK),
+                in_=listed_rows[a][:].rearrange("p (m t) -> p t m", t=PACK),
             )
 
         def gather_word_codes(a):
@@ -114,18 +120,14 @@ def tile_list_visual_word_hash_kernel(
                 word_table[:].indirect(entries(word_list, a * PASS, PASS)),
             )
 
-        def gather_image_scales(c):
-            nc.vector.tensor_copy(image_plane[c][:], image_table_plane[:].indirect(entries(image_list, c * CHUNK, CHUNK)))
-
         def gather_image_codes(c):
             nc.vector.tensor_copy(image_codes[c][:], image_table[:].indirect(entries(image_list, c * CHUNK, CHUNK)))
 
         def response(acc, a, t, c, first, width):
-            words = slice(a * PASS + t * P, a * PASS + (t + 1) * P)
             nc.tensor.matmul_mx(
                 out=acc,
                 lhsT=word_codes[a][:, t * P : (t + 1) * P].bitcast(FP8X4),
-                lhsT_scale=word_plane[WORD_PLANE:P, words],
+                lhsT_scale=word_plane[a][:, t * P : (t + 1) * P],
                 rhs=image_codes[c][:, first : first + width].bitcast(FP8X4),
                 rhs_scale=image_plane[c][:, first : first + width],
                 start=True,
@@ -221,29 +223,35 @@ def tile_list_visual_word_hash_kernel(
                 )
             return acc
 
-        for a in range(PASSES):
-            gather_word_scales(a)
-        for a in range(PASSES):
-            reorder_word_scales(a)
+        nc.sync.dma_start(
+            out=middle_rows[ROWS_AT:P, PASS:].bitcast(I32).rearrange("q (a c) -> q a c", a=PASSES),
+            in_=wb_scales.rearrange("a q c -> q a c").bitcast(I32),
+        )
+        wb_codes = held.tile([P, PASSES, 2 * N], U8, name="wb_codes", align_bytes=64)
+        nc.sync.dma_start(out=wb_codes[:].bitcast(I32), in_=wb_words.rearrange("a p c -> p a c").bitcast(I32))
+
+        nc.vector.tensor_copy(early_image_rows[:], image_table_rows[:].indirect(entries(image_list, 0, 2 * CHUNK)))
+        gather_word_rows(0)
+        nc.vector.tensor_copy(out=early_rows[:, PASS:].bitcast(I32), in_=early_image_rows[:].bitcast(I32))
+        reorder_word_rows(0, early_rows)
+        move_scale_rows(nc.scalar, early_planes, early_rows)
+        gather_word_rows(1)
         gather_word_codes(0)
-        gather_image_scales(0)
-        gather_image_scales(1)
+        reorder_word_rows(1, middle_rows)
+        move_scale_rows(nc.scalar, middle_planes, middle_rows)
         for c in range(CHUNKS):
             gather_image_codes(c)
 
         word_codes[1] = reused.tile([P, PASS], U32, name="word_codes1", align_bytes=64, offset=0)
-        image_plane[2] = reused.tile([P, CHUNK], U8, name="image_plane2", align_bytes=64, offset=PACK * PASS)
+        late_image_rows = reused.tile([P, CHUNK], U8, name="late_image_rows", align_bytes=64, offset=PACK * PASS)
         gather_word_codes(1)
+        nc.vector.tensor_copy(late_image_rows[:], image_table_rows[:].indirect(entries(image_list, 2 * CHUNK, CHUNK)))
+        move_scale_rows(nc.sync, late_plane, late_image_rows)
 
-        wd_raw = held.tile([P, PASSES, PACK, N], F32, name="wd_raw")
+        bias = reused.tile([P, NBLOCKS], F32, name="bias", align_bytes=64, offset=PACK * T2)
+        wd_raw = reused.tile([P, PASSES, PACK, N], F32, name="wd_raw", align_bytes=64, offset=PACK * T2 + 64)
         for a in range(PASSES):
             nc.sync.dma_start(out=wd_raw[:, a], in_=wd[a * PASS : (a + 1) * PASS].rearrange("(p t) n -> p t n", t=PACK))
-        wb_codes = held.tile([P, PASSES, 2 * N], U8, name="wb_codes", align_bytes=64)
-        wb_plane = held.tile([P, PASSES, N], U8, name="wb_plane", align_bytes=64)
-        nc.sync.dma_start(out=wb_codes[:].bitcast(I32), in_=wb_words.rearrange("a p c -> p a c").bitcast(I32))
-        nc.vector.memset(wb_plane[:].bitcast(I32), 0)
-        load_scale_rows(nc, wb_plane, wb_scales.rearrange("a q c -> q a c"))
-        bias = held.tile([P, NBLOCKS], F32, name="bias")
         with nc.allow_non_contiguous_dma(reason="one bias value a partition and block of output rows"):
             nc.sync.dma_start(out=bias[:], in_=b.rearrange("(nb p) -> p nb", p=P))
 
@@ -274,7 +282,6 @@ def tile_list_visual_word_hash_kernel(
         for t in range(1, PACK):
             scalar_slot(0, 1, t, t)
 
-        gather_image_scales(2)
         signed = [vector_weighted(1, 0, 0, [4, 5]), vector_weighted(1, 0, 2, [6, 7])]
         vector_magnitude(1, 0, 0, 2, signed[0])
         vector_magnitude(1, 0, 2, 2, signed[1])

@@ -31,7 +31,7 @@ ROWS_AT = P - SCALE_ROWS
 UNIT = PACK * CHUNK
 HALF = UNIT // 2
 BLOCK = PACK * P
-UPDATE_PARTS = [(0, 2), (2, 1), (3, 1)]
+UPDATE_PARTS = [(0, 2), (2, 2)]
 VECTOR_BLOCKS = 3
 
 
@@ -60,27 +60,28 @@ def tile_list_visual_word_hash_kernel(
         word_list = held.tile([P, S // LIST_ROWS], U16, name="word_list")
         image_list = held.tile([P, S2 // LIST_ROWS], U16, name="image_list")
         nc.sync.dma_start(image_list[:], offs2)
+        nc.sync.dma_start(word_list[:], offs)
 
         word_table_rows = held.tile([P, T], U8, name="word_table_rows", align_bytes=64)
         image_table_rows = held.tile([P, T2], U8, name="image_table_rows", align_bytes=64)
         word_table = held.tile([P, T], U32, name="word_table", align_bytes=64)
         image_table = reused.tile([P, T2], U32, name="image_table", align_bytes=64, offset=0)
         early_planes = held.tile([P, PASS + 2 * CHUNK], U8, name="early_planes", align_bytes=64)
-        middle_planes = held.tile([P, PASS + PASSES * N], U8, name="middle_planes", align_bytes=64)
+        middle_plane = held.tile([P, PASS], U8, name="middle_plane", align_bytes=64)
+        wb_plane = held.tile([P, PASSES, N], U8, name="wb_plane", align_bytes=64)
         late_plane = held.tile([P, CHUNK], U8, name="late_plane", align_bytes=64)
         nc.vector.memset(image_table_rows[0:ROWS_AT].bitcast(I32), 0)
         nc.vector.memset(word_table_rows[0:ROWS_AT].bitcast(I32), 0)
-        for plane in (early_planes, middle_planes, late_plane):
+        for plane in (early_planes, middle_plane, late_plane, wb_plane):
             nc.gpsimd.memset(plane[:].bitcast(I32), 0)
         nc.sync.dma_start(out=image_table_rows[ROWS_AT:P].bitcast(I32), in_=tab2_scales[0].bitcast(I32))
-        nc.sync.dma_start(word_list[:], offs)
         nc.sync.dma_start(out=word_table_rows[ROWS_AT:P].bitcast(I32), in_=tab_scales[0].bitcast(I32))
-        nc.sync.dma_start(out=word_table[:].bitcast(I32), in_=tab_words[0].rearrange("p c t -> p (c t)").bitcast(I32))
-        nc.sync.dma_start(out=image_table[:].bitcast(I32), in_=tab2_words[0].rearrange("p c t -> p (c t)").bitcast(I32))
-
         weight = held.tile([P, PASSES, PACK], F32, name="weight")
         weight_sq = held.tile([P, PASSES, PACK], F32, name="weight_sq")
         nc.sync.dma_start(out=weight[:], in_=wt.rearrange("(a p t) -> p a t", p=P, t=PACK))
+        nc.sync.dma_start(out=word_table[:].bitcast(I32), in_=tab_words[0].rearrange("p c t -> p (c t)").bitcast(I32))
+        nc.sync.dma_start(out=image_table[:].bitcast(I32), in_=tab2_words[0].rearrange("p c t -> p (c t)").bitcast(I32))
+
         nc.scalar.activation(out=weight_sq[:], in_=weight[:], func=ACT.Square)
 
         zero = held.tile([P, 1], F32, name="zero")
@@ -91,11 +92,10 @@ def tile_list_visual_word_hash_kernel(
         word_codes = {0: held.tile([P, PASS], U32, name="word_codes0", align_bytes=64)}
         listed_rows = [held.tile([P, PASS], U8, name="listed_rows%d" % a) for a in range(PASSES)]
         early_image_rows = held.tile([P, 2 * CHUNK], U8, name="early_image_rows")
-        early_rows = reused.tile([P, PASS + 2 * CHUNK], U8, name="early_rows", align_bytes=64, offset=PACK * T2)
-        middle_rows = held.tile([P, PASS + PASSES * N], U8, name="middle_rows")
-        word_plane = [early_planes[:, 0:PASS], middle_planes[:, 0:PASS]]
+        early_rows = held.tile([P, PASS + 2 * CHUNK], U8, name="wd_raw")
+        middle_rows = held.tile([P, PASS], U8, name="middle_rows")
+        word_plane = [early_planes[:, 0:PASS], middle_plane[:]]
         image_plane = [early_planes[:, PASS : PASS + CHUNK], early_planes[:, PASS + CHUNK :], late_plane[:]]
-        wb_plane = middle_planes[:, PASS:].rearrange("p (a n) -> p a n", a=PASSES)
         image_codes = [held.tile([P, CHUNK], U32, name="image_codes%d" % c, align_bytes=64) for c in range(CHUNKS)]
         wd_codes, wd_plane = {}, {}
         for first, blocks in UPDATE_PARTS:
@@ -170,13 +170,12 @@ def tile_list_visual_word_hash_kernel(
             return signed[:, 0 : len(banks) * BLOCK]
 
         def vector_magnitude(a, c, first, blocks, signed):
-            nc.vector.scalar_tensor_tensor(
+            nc.vector.tensor_reduce(
                 out=halves[a, c, first][:, 0 : blocks * BLOCK],
-                in0=signed,
-                scalar=-1.0,
-                in1=signed,
-                op0=ALU.mult,
-                op1=ALU.max,
+                in_=signed.unsqueeze(2),
+                axis=mybir.AxisListType.X,
+                op=ALU.max,
+                apply_absolute_value=True,
             )
 
         def plain_root(a, c, first, blocks):
@@ -187,20 +186,25 @@ def tile_list_visual_word_hash_kernel(
             images = slice(c * CHUNK, (c + 1) * CHUNK)
             nc.vector.quantize_mx(out=z_codes[:, a, images].bitcast(FP8X4), scales=z_plane[:, a, images], in_=z[a, c][:])
 
-        def round_update(part, name):
+        def round_update(part, passes, name):
             first, blocks = UPDATE_PARTS[part]
             grouped = held.tile([P, PASSES, blocks * P, PACK], BF16, name=name, align_bytes=64)
-            nc.vector.tensor_copy(
-                out=grouped[:].rearrange("p a (g i) t -> p a g t i", i=RUN),
-                in_=wd_raw[:, :, :, first * P : (first + blocks) * P].rearrange("p a t (g i) -> p a g t i", i=RUN),
-            )
+            for a in range(PASSES):
+                nc.gpsimd.tensor_scalar(
+                    out=grouped[:, a],
+                    in0=wd_raw[:, a, :, first * P : (first + blocks) * P].rearrange("p t n -> p n t"),
+                    scalar1=1.0,
+                    scalar2=0.0,
+                    op0=ALU.mult,
+                    op1=ALU.add,
+                )
             return grouped
 
-        def quantize_update(part, grouped):
+        def quantize_update(part, passes, grouped):
             first = UPDATE_PARTS[part][0]
             nc.vector.quantize_mx(
-                out=wd_codes[first][:].rearrange("p a b n -> p (a b n)").bitcast(FP8X4),
-                scales=wd_plane[first][:].rearrange("p a b n -> p (a b n)"),
+                out=wd_codes[first][:, passes].rearrange("p a b n -> p (a b n)").bitcast(FP8X4),
+                scales=wd_plane[first][:, passes].rearrange("p a b n -> p (a b n)"),
                 in_=grouped[:].rearrange("p a n t -> p (a n t)"),
             )
 
@@ -223,13 +227,6 @@ def tile_list_visual_word_hash_kernel(
                 )
             return acc
 
-        nc.sync.dma_start(
-            out=middle_rows[ROWS_AT:P, PASS:].bitcast(I32).rearrange("q (a c) -> q a c", a=PASSES),
-            in_=wb_scales.rearrange("a q c -> q a c").bitcast(I32),
-        )
-        wb_codes = held.tile([P, PASSES, 2 * N], U8, name="wb_codes", align_bytes=64)
-        nc.sync.dma_start(out=wb_codes[:].bitcast(I32), in_=wb_words.rearrange("a p c -> p a c").bitcast(I32))
-
         nc.vector.tensor_copy(early_image_rows[:], image_table_rows[:].indirect(entries(image_list, 0, 2 * CHUNK)))
         gather_word_rows(0)
         nc.vector.tensor_copy(out=early_rows[:, PASS:].bitcast(I32), in_=early_image_rows[:].bitcast(I32))
@@ -238,7 +235,7 @@ def tile_list_visual_word_hash_kernel(
         gather_word_rows(1)
         gather_word_codes(0)
         reorder_word_rows(1, middle_rows)
-        move_scale_rows(nc.scalar, middle_planes, middle_rows)
+        move_scale_rows(nc.scalar, middle_plane, middle_rows)
         for c in range(CHUNKS):
             gather_image_codes(c)
 
@@ -248,10 +245,16 @@ def tile_list_visual_word_hash_kernel(
         nc.vector.tensor_copy(late_image_rows[:], image_table_rows[:].indirect(entries(image_list, 2 * CHUNK, CHUNK)))
         move_scale_rows(nc.sync, late_plane, late_image_rows)
 
-        bias = reused.tile([P, NBLOCKS], F32, name="bias", align_bytes=64, offset=PACK * T2)
-        wd_raw = reused.tile([P, PASSES, PACK, N], F32, name="wd_raw", align_bytes=64, offset=PACK * T2 + 64)
+        wd_raw = held.tile([P, PASSES, PACK, N], F32, name="wd_raw")
+        wd_rows = wd.rearrange("(a p t) n -> a p t n", p=P, t=PACK)
         for a in range(PASSES):
-            nc.sync.dma_start(out=wd_raw[:, a], in_=wd[a * PASS : (a + 1) * PASS].rearrange("(p t) n -> p t n", t=PACK))
+            nc.sync.dma_start(out=wd_raw[:, a], in_=wd_rows[a])
+        wb_codes = held.tile([P, PASSES, 2 * N], U8, name="wb_codes", align_bytes=64)
+        nc.sync.dma_start(out=wb_codes[:].bitcast(I32), in_=wb_words.rearrange("a p c -> p a c").bitcast(I32))
+        wb_rows = wb_scales.rearrange("a q c -> q a c")
+        for r in range(PACK):
+            nc.sync.dma_start(out=wb_plane[r:P:QUAD].bitcast(I32), in_=wb_rows[r::PACK].bitcast(I32))
+        bias = held.tile([P, NBLOCKS], F32, name="bias")
         with nc.allow_non_contiguous_dma(reason="one bias value a partition and block of output rows"):
             nc.sync.dma_start(out=bias[:], in_=b.rearrange("(nb p) -> p nb", p=P))
 
@@ -264,15 +267,15 @@ def tile_list_visual_word_hash_kernel(
         magnitude = {
             (0, 0): held.tile([P, UNIT], F32, name="magnitude00")[:],
             (0, 1): held.tile([P, UNIT], F32, name="magnitude01")[:],
-            (0, 2): late[:, 0:UNIT],
+            (1, 1): held.tile([P, UNIT], F32, name="magnitude11")[:],
             (1, 2): late[:, UNIT : 2 * UNIT],
         }
 
         halves = {
             (1, 0, 0): held.tile([P, HALF], F32, name="half100"),
             (1, 0, 2): held.tile([P, HALF], F32, name="half102"),
-            (1, 1, 0): held.tile([P, HALF], F32, name="half110", align_bytes=64),
-            (1, 1, 2): held.tile([P, HALF], F32, name="half112", align_bytes=64),
+            (0, 2, 0): late[:, 0:HALF],
+            (0, 2, 2): late[:, HALF:UNIT],
         }
         shared = CHUNK - VECTOR_BLOCKS * P
         for t in range(PACK):
@@ -282,56 +285,55 @@ def tile_list_visual_word_hash_kernel(
         for t in range(1, PACK):
             scalar_slot(0, 1, t, t)
 
-        signed = [vector_weighted(1, 0, 0, [4, 5]), vector_weighted(1, 0, 2, [6, 7])]
-        vector_magnitude(1, 0, 0, 2, signed[0])
-        vector_magnitude(1, 0, 2, 2, signed[1])
+        signed, grouped, both = {}, {}, slice(0, PASSES)
+        for k in range(1, PACK):
+            halves[1, 2, k] = late[:, UNIT + k * BLOCK : UNIT + (k + 1) * BLOCK]
+        grouped[0] = round_update(0, both, "image_table_rows")
+        signed[1, 0, 0] = vector_weighted(1, 0, 0, [4, 5])
+        signed[1, 0, 2] = vector_weighted(1, 0, 2, [6, 7])
+        vector_magnitude(1, 0, 0, 2, signed[1, 0, 0])
+        vector_magnitude(1, 0, 2, 2, signed[1, 0, 2])
         quantize_z(0, 0)
-
-        scalar_slot(0, 2, 0, 0)
+        quantize_update(0, both, grouped[0])
+        grouped[1] = round_update(1, both, "image_table_rows")
+        scalar_slot(1, 1, 0, 0)
         interleaving_root(0, 1)
+        scalar_slot(1, 1, 1, 1)
+        scalar_slot(1, 1, 2, 2)
+        scalar_slot(1, 1, 3, 3)
         plain_root(1, 0, 0, 2)
         plain_root(1, 0, 2, 2)
-
-
-        signed = [vector_weighted(1, 1, 0, [6, 7])]
-
-        grouped = round_update(0, "update0")
-        signed.append(vector_weighted(1, 1, 2, [6, 7]))
-        vector_magnitude(1, 1, 0, 2, signed[0])
-        quantize_update(0, grouped)
-        vector_magnitude(1, 1, 2, 2, signed[1])
-        quantize_z(1, 0)
+        signed[0, 2, 0] = vector_weighted(0, 2, 0, [6, 7])
+        signed[0, 2, 2] = vector_weighted(0, 2, 2, [4, 5])
+        vector_magnitude(0, 2, 0, 2, signed[0, 2, 0])
+        vector_magnitude(0, 2, 2, 2, signed[0, 2, 2])
         quantize_z(0, 1)
-
-        for t in range(1, PACK):
-            scalar_slot(0, 2, t, t)
+        quantize_z(1, 0)
         first_block = bank(0, [P, PACK, P])
         for t in range(PACK):
             response(first_block[:, t, :], 1, t, 2, 0, P)
         for t in range(PACK):
             scalar_magnitude(1, 2, t, first_block[:, t, :])
-        plain_root(1, 1, 0, 2)
-        plain_root(1, 1, 2, 2)
-        interleaving_root(0, 2)
-        signed = [vector_weighted(1, 2, 1, [6, 7]), vector_weighted(1, 2, 3, [2])]
-        halves[1, 2, 1] = late[:, UNIT + BLOCK : UNIT + 3 * BLOCK]
-        halves[1, 2, 3] = late[:, UNIT + 3 * BLOCK : 2 * UNIT]
-        vector_magnitude(1, 2, 1, 2, signed[0])
+        interleaving_root(1, 1)
+        plain_root(0, 2, 0, 2)
+        plain_root(0, 2, 2, 2)
+        signed[1, 2, 1] = vector_weighted(1, 2, 1, [6])
+        signed[1, 2, 2] = vector_weighted(1, 2, 2, [7])
+        signed[1, 2, 3] = vector_weighted(1, 2, 3, [2])
         quantize_z(1, 1)
-        vector_magnitude(1, 2, 3, 1, signed[1])
-        interleaving_root(1, 2, shared)
-        plain_root(1, 2, 1, 2)
-        plain_root(1, 2, 3, 1)
-
+        vector_magnitude(1, 2, 1, 1, signed[1, 2, 1])
+        vector_magnitude(1, 2, 2, 1, signed[1, 2, 2])
+        vector_magnitude(1, 2, 3, 1, signed[1, 2, 3])
+        quantize_update(1, both, grouped[1])
         quantize_z(0, 2)
-        grouped = [round_update(1, "z11")]
+        interleaving_root(1, 2, shared)
+        plain_root(1, 2, 1, 1)
+        plain_root(1, 2, 2, 1)
+        plain_root(1, 2, 3, 1)
         quantize_z(1, 2)
-        quantize_update(1, grouped[0])
-        grouped.append(round_update(2, "z12"))
-        quantize_update(2, grouped[1])
 
         pieces = [(0, 0), (0, 1), (1, 0), (1, 1), (2, 0), (2, 1), (0, 2), (1, 2), (2, 2), (0, 3), (1, 3), (2, 3)]
-        free_order = [4, 5, 0, 1, 6, 7, 3, 2]
+        free_order = [1, 4, 5, 0, 6, 7, 3, 2]
         y = [project(c, nb, number) for number, (c, nb) in zip(free_order, pieces)]
 
         results = held.tile([P, len(pieces) * CHUNK], F32, name="late_then_results")

@@ -28,10 +28,11 @@ QUAD = 32
 RUN = 4
 SCALE_ROWS = 16
 ROWS_AT = P - SCALE_ROWS
+LATE = PACK * T2 + PACK * PASS
 UNIT = PACK * CHUNK
 HALF = UNIT // 2
 BLOCK = PACK * P
-UPDATE_PARTS = [(0, 2), (2, 2)]
+UPDATE_PARTS = [(0, 2), (2, 1), (3, 1)]
 VECTOR_BLOCKS = 3
 
 
@@ -66,23 +67,23 @@ def tile_list_visual_word_hash_kernel(
         image_table_rows = held.tile([P, T2], U8, name="image_table_rows", align_bytes=64)
         word_table = held.tile([P, T], U32, name="word_table", align_bytes=64)
         image_table = reused.tile([P, T2], U32, name="image_table", align_bytes=64, offset=0)
-        early_planes = held.tile([P, PASS + 2 * CHUNK], U8, name="early_planes", align_bytes=64)
-        middle_plane = held.tile([P, PASS], U8, name="middle_plane", align_bytes=64)
+        early_planes = held.tile([P, S + 2 * CHUNK], U8, name="early_planes", align_bytes=64)
         wb_plane = held.tile([P, PASSES, N], U8, name="wb_plane", align_bytes=64)
         late_plane = held.tile([P, CHUNK], U8, name="late_plane", align_bytes=64)
         nc.vector.memset(image_table_rows[0:ROWS_AT].bitcast(I32), 0)
         nc.vector.memset(word_table_rows[0:ROWS_AT].bitcast(I32), 0)
-        for plane in (early_planes, middle_plane, late_plane, wb_plane):
+        for plane in (early_planes, late_plane, wb_plane):
             nc.gpsimd.memset(plane[:].bitcast(I32), 0)
         nc.sync.dma_start(out=image_table_rows[ROWS_AT:P].bitcast(I32), in_=tab2_scales[0].bitcast(I32))
         nc.sync.dma_start(out=word_table_rows[ROWS_AT:P].bitcast(I32), in_=tab_scales[0].bitcast(I32))
-        weight = held.tile([P, PASSES, PACK], F32, name="weight")
-        weight_sq = held.tile([P, PASSES, PACK], F32, name="weight_sq")
-        nc.sync.dma_start(out=weight[:], in_=wt.rearrange("(a p t) -> p a t", p=P, t=PACK))
         nc.sync.dma_start(out=word_table[:].bitcast(I32), in_=tab_words[0].rearrange("p c t -> p (c t)").bitcast(I32))
         nc.sync.dma_start(out=image_table[:].bitcast(I32), in_=tab2_words[0].rearrange("p c t -> p (c t)").bitcast(I32))
 
-        nc.scalar.activation(out=weight_sq[:], in_=weight[:], func=ACT.Square)
+        weight_line = reused.tile([P, 32], F32, name="weight", align_bytes=64, offset=LATE - 64)
+        weight = weight_line[:, 0 : PASSES * PACK].rearrange("p (a t) -> p a t", a=PASSES)
+        weight_sq = held.tile([P, PASSES, PACK], F32, name="weight_sq")
+        nc.sync.dma_start(out=weight, in_=wt.rearrange("(a p t) -> p a t", p=P, t=PACK))
+        nc.scalar.activation(out=weight_sq[:], in_=weight, func=ACT.Square)
 
         zero = held.tile([P, 1], F32, name="zero")
         unread = held.tile([P, 1], F32, name="unread")
@@ -90,12 +91,11 @@ def tile_list_visual_word_hash_kernel(
         nc.scalar.activation(out=unread[:], in_=zero[:], func=ACT.Sqrt)
 
         word_codes = {0: held.tile([P, PASS], U32, name="word_codes0", align_bytes=64)}
-        listed_rows = [held.tile([P, PASS], U8, name="listed_rows%d" % a) for a in range(PASSES)]
+        listed_rows = held.tile([P, S], U8, name="listed_rows")
         early_image_rows = held.tile([P, 2 * CHUNK], U8, name="early_image_rows")
-        early_rows = held.tile([P, PASS + 2 * CHUNK], U8, name="wd_raw")
-        middle_rows = held.tile([P, PASS], U8, name="middle_rows")
-        word_plane = [early_planes[:, 0:PASS], middle_plane[:]]
-        image_plane = [early_planes[:, PASS : PASS + CHUNK], early_planes[:, PASS + CHUNK :], late_plane[:]]
+        early_rows = held.tile([P, S + 2 * CHUNK], U8, name="wd_raw")
+        word_plane = [early_planes[:, a * PASS : (a + 1) * PASS] for a in range(PASSES)]
+        image_plane = [early_planes[:, S : S + CHUNK], early_planes[:, S + CHUNK :], late_plane[:]]
         image_codes = [held.tile([P, CHUNK], U32, name="image_codes%d" % c, align_bytes=64) for c in range(CHUNKS)]
         wd_codes, wd_plane = {}, {}
         for first, blocks in UPDATE_PARTS:
@@ -104,15 +104,6 @@ def tile_list_visual_word_hash_kernel(
             wd_codes[first], wd_plane[first] = codes, plane
         z_codes = held.tile([P, PASSES, S2], U32, name="z_codes", align_bytes=64)
         z_plane = held.tile([P, PASSES, S2], U8, name="z_plane", align_bytes=64)
-
-        def gather_word_rows(a):
-            nc.vector.tensor_copy(listed_rows[a][:], word_table_rows[:].indirect(entries(word_list, a * PASS, PASS)))
-
-        def reorder_word_rows(a, rows):
-            nc.vector.tensor_copy(
-                out=rows[:, 0:PASS].rearrange("p (t m) -> p t m", t=PACK),
-                in_=listed_rows[a][:].rearrange("p (m t) -> p t m", t=PACK),
-            )
 
         def gather_word_codes(a):
             nc.vector.tensor_copy(
@@ -170,12 +161,13 @@ def tile_list_visual_word_hash_kernel(
             return signed[:, 0 : len(banks) * BLOCK]
 
         def vector_magnitude(a, c, first, blocks, signed):
-            nc.vector.tensor_reduce(
+            nc.vector.scalar_tensor_tensor(
                 out=halves[a, c, first][:, 0 : blocks * BLOCK],
-                in_=signed.unsqueeze(2),
-                axis=mybir.AxisListType.X,
-                op=ALU.max,
-                apply_absolute_value=True,
+                in0=signed,
+                scalar=-1.0,
+                in1=signed,
+                op0=ALU.mult,
+                op1=ALU.max,
             )
 
         def plain_root(a, c, first, blocks):
@@ -188,16 +180,12 @@ def tile_list_visual_word_hash_kernel(
 
         def round_update(part, passes, name):
             first, blocks = UPDATE_PARTS[part]
-            grouped = held.tile([P, PASSES, blocks * P, PACK], BF16, name=name, align_bytes=64)
-            for a in range(PASSES):
-                nc.gpsimd.tensor_scalar(
-                    out=grouped[:, a],
-                    in0=wd_raw[:, a, :, first * P : (first + blocks) * P].rearrange("p t n -> p n t"),
-                    scalar1=1.0,
-                    scalar2=0.0,
-                    op0=ALU.mult,
-                    op1=ALU.add,
-                )
+            grouped = held.tile([P, passes.stop - passes.start, blocks * P, PACK], BF16, name=name, align_bytes=64)
+            raw = wd_raw[:, passes, :, first * P : (first + blocks) * P]
+            nc.vector.tensor_copy(
+                out=grouped[:].rearrange("p a (g i) t -> p a g t i", i=RUN),
+                in_=raw.rearrange("p a t (g i) -> p a g t i", i=RUN),
+            )
             return grouped
 
         def quantize_update(part, passes, grouped):
@@ -228,19 +216,19 @@ def tile_list_visual_word_hash_kernel(
             return acc
 
         nc.vector.tensor_copy(early_image_rows[:], image_table_rows[:].indirect(entries(image_list, 0, 2 * CHUNK)))
-        gather_word_rows(0)
-        nc.vector.tensor_copy(out=early_rows[:, PASS:].bitcast(I32), in_=early_image_rows[:].bitcast(I32))
-        reorder_word_rows(0, early_rows)
+        nc.vector.tensor_copy(listed_rows[:], word_table_rows[:].indirect(word_list[:]))
+        nc.vector.tensor_copy(out=early_rows[:, S:].bitcast(I32), in_=early_image_rows[:].bitcast(I32))
+        nc.vector.tensor_copy(
+            out=early_rows[:, 0:S].rearrange("p (a t m) -> p a t m", a=PASSES, t=PACK),
+            in_=listed_rows[:].rearrange("p (a m t) -> p a t m", a=PASSES, t=PACK),
+        )
         move_scale_rows(nc.scalar, early_planes, early_rows)
-        gather_word_rows(1)
         gather_word_codes(0)
-        reorder_word_rows(1, middle_rows)
-        move_scale_rows(nc.scalar, middle_plane, middle_rows)
         for c in range(CHUNKS):
             gather_image_codes(c)
 
-        word_codes[1] = reused.tile([P, PASS], U32, name="word_codes1", align_bytes=64, offset=0)
-        late_image_rows = reused.tile([P, CHUNK], U8, name="late_image_rows", align_bytes=64, offset=PACK * PASS)
+        word_codes[1] = reused.tile([P, PASS], U32, name="word_codes1", align_bytes=64, offset=LATE - PACK * PASS)
+        late_image_rows = reused.tile([P, CHUNK], U8, name="late_image_rows", align_bytes=64, offset=LATE)
         gather_word_codes(1)
         nc.vector.tensor_copy(late_image_rows[:], image_table_rows[:].indirect(entries(image_list, 2 * CHUNK, CHUNK)))
         move_scale_rows(nc.sync, late_plane, late_image_rows)
@@ -288,14 +276,12 @@ def tile_list_visual_word_hash_kernel(
         signed, grouped, both = {}, {}, slice(0, PASSES)
         for k in range(1, PACK):
             halves[1, 2, k] = late[:, UNIT + k * BLOCK : UNIT + (k + 1) * BLOCK]
-        grouped[0] = round_update(0, both, "image_table_rows")
         signed[1, 0, 0] = vector_weighted(1, 0, 0, [4, 5])
         signed[1, 0, 2] = vector_weighted(1, 0, 2, [6, 7])
         vector_magnitude(1, 0, 0, 2, signed[1, 0, 0])
         vector_magnitude(1, 0, 2, 2, signed[1, 0, 2])
         quantize_z(0, 0)
-        quantize_update(0, both, grouped[0])
-        grouped[1] = round_update(1, both, "image_table_rows")
+        grouped[0] = round_update(0, both, "update0")
         scalar_slot(1, 1, 0, 0)
         interleaving_root(0, 1)
         scalar_slot(1, 1, 1, 1)
@@ -304,10 +290,11 @@ def tile_list_visual_word_hash_kernel(
         plain_root(1, 0, 0, 2)
         plain_root(1, 0, 2, 2)
         signed[0, 2, 0] = vector_weighted(0, 2, 0, [6, 7])
+        quantize_update(0, both, grouped[0])
         signed[0, 2, 2] = vector_weighted(0, 2, 2, [4, 5])
+        quantize_z(0, 1)
         vector_magnitude(0, 2, 0, 2, signed[0, 2, 0])
         vector_magnitude(0, 2, 2, 2, signed[0, 2, 2])
-        quantize_z(0, 1)
         quantize_z(1, 0)
         first_block = bank(0, [P, PACK, P])
         for t in range(PACK):
@@ -320,20 +307,23 @@ def tile_list_visual_word_hash_kernel(
         signed[1, 2, 1] = vector_weighted(1, 2, 1, [6])
         signed[1, 2, 2] = vector_weighted(1, 2, 2, [7])
         signed[1, 2, 3] = vector_weighted(1, 2, 3, [2])
-        quantize_z(1, 1)
         vector_magnitude(1, 2, 1, 1, signed[1, 2, 1])
+        quantize_z(1, 1)
         vector_magnitude(1, 2, 2, 1, signed[1, 2, 2])
         vector_magnitude(1, 2, 3, 1, signed[1, 2, 3])
-        quantize_update(1, both, grouped[1])
         quantize_z(0, 2)
         interleaving_root(1, 2, shared)
         plain_root(1, 2, 1, 1)
         plain_root(1, 2, 2, 1)
         plain_root(1, 2, 3, 1)
+        grouped[1] = round_update(1, both, "z02")
         quantize_z(1, 2)
+        quantize_update(1, both, grouped[1])
+        grouped[2] = round_update(2, both, "z12")
+        quantize_update(2, both, grouped[2])
 
         pieces = [(0, 0), (0, 1), (1, 0), (1, 1), (2, 0), (2, 1), (0, 2), (1, 2), (2, 2), (0, 3), (1, 3), (2, 3)]
-        free_order = [1, 4, 5, 0, 6, 7, 3, 2]
+        free_order = [1, 3, 4, 5, 6, 7, 0, 2]
         y = [project(c, nb, number) for number, (c, nb) in zip(free_order, pieces)]
 
         results = held.tile([P, len(pieces) * CHUNK], F32, name="late_then_results")

@@ -67,15 +67,16 @@ def tile_list_visual_word_hash_kernel(
         image_table_rows = held.tile([P, T2], U8, name="image_table_rows", align_bytes=64)
         word_table = held.tile([P, T], U32, name="word_table", align_bytes=64)
         image_table = reused.tile([P, T2], U32, name="image_table", align_bytes=64, offset=0)
-        early_planes = held.tile([P, S + 2 * CHUNK], U8, name="early_planes", align_bytes=64)
+        early_planes = held.tile([P, PASS + 2 * CHUNK], U8, name="early_planes", align_bytes=64)
+        middle_plane = held.tile([P, PASS], U8, name="middle_plane", align_bytes=64)
         wb_plane = held.tile([P, PASSES, N], U8, name="wb_plane", align_bytes=64)
         late_plane = held.tile([P, CHUNK], U8, name="late_plane", align_bytes=64)
         nc.vector.memset(image_table_rows[0:ROWS_AT].bitcast(I32), 0)
         nc.vector.memset(word_table_rows[0:ROWS_AT].bitcast(I32), 0)
-        for plane in (early_planes, late_plane, wb_plane):
+        for plane in (early_planes, middle_plane, late_plane, wb_plane):
             nc.gpsimd.memset(plane[:].bitcast(I32), 0)
-        nc.sync.dma_start(out=image_table_rows[ROWS_AT:P].bitcast(I32), in_=tab2_scales[0].bitcast(I32))
-        nc.sync.dma_start(out=word_table_rows[ROWS_AT:P].bitcast(I32), in_=tab_scales[0].bitcast(I32))
+        nc.scalar.dma_start(out=image_table_rows[ROWS_AT:P].bitcast(I32), in_=tab2_scales[0].bitcast(I32))
+        nc.scalar.dma_start(out=word_table_rows[ROWS_AT:P].bitcast(I32), in_=tab_scales[0].bitcast(I32))
         nc.sync.dma_start(out=word_table[:].bitcast(I32), in_=tab_words[0].rearrange("p c t -> p (c t)").bitcast(I32))
         nc.sync.dma_start(out=image_table[:].bitcast(I32), in_=tab2_words[0].rearrange("p c t -> p (c t)").bitcast(I32))
 
@@ -91,11 +92,12 @@ def tile_list_visual_word_hash_kernel(
         nc.scalar.activation(out=unread[:], in_=zero[:], func=ACT.Sqrt)
 
         word_codes = {0: held.tile([P, PASS], U32, name="word_codes0", align_bytes=64)}
-        listed_rows = held.tile([P, S], U8, name="listed_rows")
+        listed_rows = [held.tile([P, PASS], U8, name="listed_rows%d" % a) for a in range(PASSES)]
         early_image_rows = held.tile([P, 2 * CHUNK], U8, name="early_image_rows")
-        early_rows = held.tile([P, S + 2 * CHUNK], U8, name="wd_raw")
-        word_plane = [early_planes[:, a * PASS : (a + 1) * PASS] for a in range(PASSES)]
-        image_plane = [early_planes[:, S : S + CHUNK], early_planes[:, S + CHUNK :], late_plane[:]]
+        early_rows = held.tile([P, PASS + 2 * CHUNK], U8, name="wd_raw")
+        middle_rows = held.tile([P, PASS], U8, name="middle_rows")
+        word_plane = [early_planes[:, 0:PASS], middle_plane[:]]
+        image_plane = [early_planes[:, PASS : PASS + CHUNK], early_planes[:, PASS + CHUNK :], late_plane[:]]
         image_codes = [held.tile([P, CHUNK], U32, name="image_codes%d" % c, align_bytes=64) for c in range(CHUNKS)]
         wd_codes, wd_plane = {}, {}
         for first, blocks in UPDATE_PARTS:
@@ -104,6 +106,15 @@ def tile_list_visual_word_hash_kernel(
             wd_codes[first], wd_plane[first] = codes, plane
         z_codes = held.tile([P, PASSES, S2], U32, name="z_codes", align_bytes=64)
         z_plane = held.tile([P, PASSES, S2], U8, name="z_plane", align_bytes=64)
+
+        def gather_word_rows(a):
+            nc.vector.tensor_copy(listed_rows[a][:], word_table_rows[:].indirect(entries(word_list, a * PASS, PASS)))
+
+        def reorder_word_rows(a, rows):
+            nc.vector.tensor_copy(
+                out=rows[:, 0:PASS].rearrange("p (t m) -> p t m", t=PACK),
+                in_=listed_rows[a][:].rearrange("p (m t) -> p t m", t=PACK),
+            )
 
         def gather_word_codes(a):
             nc.vector.tensor_copy(
@@ -216,14 +227,14 @@ def tile_list_visual_word_hash_kernel(
             return acc
 
         nc.vector.tensor_copy(early_image_rows[:], image_table_rows[:].indirect(entries(image_list, 0, 2 * CHUNK)))
-        nc.vector.tensor_copy(listed_rows[:], word_table_rows[:].indirect(word_list[:]))
-        nc.vector.tensor_copy(out=early_rows[:, S:].bitcast(I32), in_=early_image_rows[:].bitcast(I32))
-        nc.vector.tensor_copy(
-            out=early_rows[:, 0:S].rearrange("p (a t m) -> p a t m", a=PASSES, t=PACK),
-            in_=listed_rows[:].rearrange("p (a m t) -> p a t m", a=PASSES, t=PACK),
-        )
+        gather_word_rows(0)
+        nc.vector.tensor_copy(out=early_rows[:, PASS:].bitcast(I32), in_=early_image_rows[:].bitcast(I32))
+        reorder_word_rows(0, early_rows)
         move_scale_rows(nc.scalar, early_planes, early_rows)
+        gather_word_rows(1)
         gather_word_codes(0)
+        reorder_word_rows(1, middle_rows)
+        move_scale_rows(nc.sync, middle_plane, middle_rows)
         for c in range(CHUNKS):
             gather_image_codes(c)
 

@@ -22,18 +22,16 @@ PASS = P * PACK
 PASSES = S // PASS
 CHUNK = 512
 CHUNKS = S2 // CHUNK
-NBLOCKS = N // P
+ROW_BLOCKS = N // P
 LIST_ROWS = 16
 QUAD = 32
+ROWS_AT = P - K // 32
+ALIGN = 64
 RUN = 4
-SCALE_ROWS = 16
-ROWS_AT = P - SCALE_ROWS
-LATE = PACK * T2 + PACK * PASS
 UNIT = PACK * CHUNK
-HALF = UNIT // 2
 BLOCK = PACK * P
+SEAM = PACK * T2 + PACK * PASS
 UPDATE_PARTS = [(0, 2), (2, 1), (3, 1)]
-VECTOR_BLOCKS = 3
 
 
 def move_scale_rows(queue, plane, rows):
@@ -51,8 +49,8 @@ def tile_list_visual_word_hash_kernel(
     nc = tc.nc
     with ExitStack() as ctx:
         held = ctx.enter_context(tc.tile_pool(name="held", bufs=1))
-        ring = ctx.enter_context(tc.tile_pool(name="ring", bufs=2))
-        reused = ctx.enter_context(tc.tile_pool(name="reused", bufs=1))
+        ring = ctx.enter_context(tc.tile_pool(name="ring", bufs=3))
+        placed = ctx.enter_context(tc.tile_pool(name="placed", bufs=1))
         psum = ctx.enter_context(tc.psum_pool(name="psum", bufs=1))
 
         def bank(number, shape):
@@ -63,14 +61,14 @@ def tile_list_visual_word_hash_kernel(
         nc.sync.dma_start(image_list[:], offs2)
         nc.sync.dma_start(word_list[:], offs)
 
-        word_table_rows = held.tile([P, T], U8, name="word_table_rows", align_bytes=64)
-        image_table_rows = held.tile([P, T2], U8, name="image_table_rows", align_bytes=64)
-        word_table = held.tile([P, T], U32, name="word_table", align_bytes=64)
-        image_table = reused.tile([P, T2], U32, name="image_table", align_bytes=64, offset=0)
-        early_planes = held.tile([P, PASS + 2 * CHUNK], U8, name="early_planes", align_bytes=64)
-        middle_plane = held.tile([P, PASS], U8, name="middle_plane", align_bytes=64)
-        wb_plane = held.tile([P, PASSES, N], U8, name="wb_plane", align_bytes=64)
-        late_plane = held.tile([P, CHUNK], U8, name="late_plane", align_bytes=64)
+        word_table_rows = held.tile([P, T], U8, name="word_table_rows", align_bytes=ALIGN)
+        image_table_rows = held.tile([P, T2], U8, name="image_table_rows", align_bytes=ALIGN)
+        word_table = held.tile([P, T], U32, name="word_table", align_bytes=ALIGN)
+        image_table = placed.tile([P, T2], U32, name="image_table", align_bytes=ALIGN, offset=0)
+        early_planes = held.tile([P, PASS + 2 * CHUNK], U8, name="early_planes", align_bytes=ALIGN)
+        middle_plane = held.tile([P, PASS], U8, name="middle_plane", align_bytes=ALIGN)
+        wb_plane = held.tile([P, PASSES, N], U8, name="wb_plane", align_bytes=ALIGN)
+        late_plane = held.tile([P, CHUNK], U8, name="late_plane", align_bytes=ALIGN)
         nc.vector.memset(image_table_rows[0:ROWS_AT].bitcast(I32), 0)
         nc.vector.memset(word_table_rows[0:ROWS_AT].bitcast(I32), 0)
         for plane in (early_planes, middle_plane, late_plane, wb_plane):
@@ -80,32 +78,30 @@ def tile_list_visual_word_hash_kernel(
         nc.sync.dma_start(out=word_table[:].bitcast(I32), in_=tab_words[0].rearrange("p c t -> p (c t)").bitcast(I32))
         nc.sync.dma_start(out=image_table[:].bitcast(I32), in_=tab2_words[0].rearrange("p c t -> p (c t)").bitcast(I32))
 
-        weight_line = reused.tile([P, 32], F32, name="weight", align_bytes=64, offset=LATE - 64)
-        weight = weight_line[:, 0 : PASSES * PACK].rearrange("p (a t) -> p a t", a=PASSES)
+        weight_tile = placed.tile([P, 2 * ALIGN // 4], F32, name="weight", align_bytes=ALIGN, offset=SEAM - ALIGN)
+        weight = weight_tile[:, 0 : PASSES * PACK].rearrange("p (a t) -> p a t", a=PASSES)
         weight_sq = held.tile([P, PASSES, PACK], F32, name="weight_sq")
         nc.sync.dma_start(out=weight, in_=wt.rearrange("(a p t) -> p a t", p=P, t=PACK))
-        nc.scalar.activation(out=weight_sq[:], in_=weight, func=ACT.Square)
-
         zero = held.tile([P, 1], F32, name="zero")
-        unread = held.tile([P, 1], F32, name="unread")
+        zero_root = held.tile([P, 1], F32, name="zero_root")
         nc.vector.memset(zero[:], 0.0)
-        nc.scalar.activation(out=unread[:], in_=zero[:], func=ACT.Sqrt)
+        nc.scalar.activation(out=zero_root[:], in_=zero[:], func=ACT.Sqrt)
+        nc.scalar.activation(out=weight_sq[:], in_=weight, func=ACT.Square, bias=zero_root[:])
 
-        word_codes = {0: held.tile([P, PASS], U32, name="word_codes0", align_bytes=64)}
+        word_codes = {0: held.tile([P, PASS], U32, name="word_codes0", align_bytes=ALIGN)}
         listed_rows = [held.tile([P, PASS], U8, name="listed_rows%d" % a) for a in range(PASSES)]
         early_image_rows = held.tile([P, 2 * CHUNK], U8, name="early_image_rows")
-        early_rows = held.tile([P, PASS + 2 * CHUNK], U8, name="wd_raw")
+        early_rows = held.tile([P, PASS + 2 * CHUNK], U8, name="early_rows_then_wd")
         middle_rows = held.tile([P, PASS], U8, name="middle_rows")
         word_plane = [early_planes[:, 0:PASS], middle_plane[:]]
         image_plane = [early_planes[:, PASS : PASS + CHUNK], early_planes[:, PASS + CHUNK :], late_plane[:]]
-        image_codes = [held.tile([P, CHUNK], U32, name="image_codes%d" % c, align_bytes=64) for c in range(CHUNKS)]
+        image_codes = [held.tile([P, CHUNK], U32, name="image_codes%d" % c, align_bytes=ALIGN) for c in range(CHUNKS)]
         wd_codes, wd_plane = {}, {}
-        for first, blocks in UPDATE_PARTS:
-            codes = held.tile([P, PASSES, blocks, P], U32, name="wd_codes%d" % first, align_bytes=64)
-            plane = held.tile([P, PASSES, blocks, P], U8, name="wd_plane%d" % first, align_bytes=64)
-            wd_codes[first], wd_plane[first] = codes, plane
-        z_codes = held.tile([P, PASSES, S2], U32, name="z_codes", align_bytes=64)
-        z_plane = held.tile([P, PASSES, S2], U8, name="z_plane", align_bytes=64)
+        for first, count in UPDATE_PARTS:
+            wd_codes[first] = held.tile([P, PASSES, count, P], U32, name="wd_codes%d" % first, align_bytes=ALIGN)
+            wd_plane[first] = held.tile([P, PASSES, count, P], U8, name="wd_plane%d" % first, align_bytes=ALIGN)
+        z_codes = held.tile([P, PASSES, S2], U32, name="z_codes", align_bytes=ALIGN)
+        z_plane = held.tile([P, PASSES, S2], U8, name="z_plane", align_bytes=ALIGN)
 
         def gather_word_rows(a):
             nc.vector.tensor_copy(listed_rows[a][:], word_table_rows[:].indirect(entries(word_list, a * PASS, PASS)))
@@ -121,6 +117,10 @@ def tile_list_visual_word_hash_kernel(
                 word_codes[a][:].rearrange("p (t m) -> p m t", t=PACK),
                 word_table[:].indirect(entries(word_list, a * PASS, PASS)),
             )
+
+        def gather_image_rows(rows, c, chunks):
+            offsets = entries(image_list, c * CHUNK, chunks * CHUNK)
+            nc.vector.tensor_copy(rows[:], image_table_rows[:].indirect(offsets))
 
         def gather_image_codes(c):
             nc.vector.tensor_copy(image_codes[c][:], image_table[:].indirect(entries(image_list, c * CHUNK, CHUNK)))
@@ -139,7 +139,7 @@ def tile_list_visual_word_hash_kernel(
         def scalar_magnitude(a, c, t, acc):
             width = acc.shape[1]
             nc.scalar.activation(
-                out=magnitude[a, c][:, t * width : (t + 1) * width],
+                out=by_slot[a, c][:, t * width : (t + 1) * width],
                 in_=acc,
                 func=ACT.Abs,
                 scale=weight_sq[:, a, t : t + 1],
@@ -150,69 +150,67 @@ def tile_list_visual_word_hash_kernel(
             response(acc[:], a, t, c, 0, CHUNK)
             scalar_magnitude(a, c, t, acc[:])
 
-        def interleaving_root(a, c, width=CHUNK):
+        def interleaving_root(a, c, width):
             nc.scalar.activation(
                 out=z[a, c][:, 0 : PACK * width].rearrange("p (g i t) -> p g t i", i=RUN, t=PACK),
-                in_=magnitude[a, c][:, 0 : PACK * width].rearrange("p (t g i) -> p g t i", i=RUN, t=PACK),
+                in_=by_slot[a, c][:, 0 : PACK * width].rearrange("p (t g i) -> p g t i", i=RUN, t=PACK),
                 func=ACT.Sqrt,
             )
 
         def vector_weighted(a, c, first, banks):
-            signed = ring.tile([P, len(banks) * BLOCK], F32, name="signed", bufs=3)
+            product = ring.tile([P, len(banks) * BLOCK], F32, name="signed")
             for k, number in enumerate(banks):
                 acc = bank(number, [P, PACK, P])
                 for t in range(PACK):
                     response(acc[:, t, :], a, t, c, (first + k) * P, P)
                 nc.vector.tensor_tensor(
-                    out=signed[:, k * BLOCK : (k + 1) * BLOCK].rearrange("p (j t) -> p j t", t=PACK),
+                    out=product[:, k * BLOCK : (k + 1) * BLOCK].rearrange("p (j t) -> p j t", t=PACK),
                     in0=acc[:].rearrange("p t j -> p j t"),
                     in1=weight_sq[:, a, :].unsqueeze(1).to_broadcast([P, P, PACK]),
                     op=ALU.mult,
                 )
-            return signed[:, 0 : len(banks) * BLOCK]
+            signed[a, c, first] = product[:]
 
-        def vector_magnitude(a, c, first, blocks, signed):
+        def vector_magnitude(a, c, first):
+            x = signed[a, c, first]
             nc.vector.scalar_tensor_tensor(
-                out=halves[a, c, first][:, 0 : blocks * BLOCK],
-                in0=signed,
-                scalar=-1.0,
-                in1=signed,
-                op0=ALU.mult,
-                op1=ALU.max,
+                out=by_image[a, c, first], in0=x, scalar=-1.0, in1=x, op0=ALU.mult, op1=ALU.max
             )
 
-        def plain_root(a, c, first, blocks):
-            part = slice(first * BLOCK, (first + blocks) * BLOCK)
-            nc.scalar.activation(out=z[a, c][:, part], in_=halves[a, c, first][:], func=ACT.Sqrt)
+        def plain_root(a, c, first):
+            x = by_image[a, c, first]
+            nc.scalar.activation(out=z[a, c][:, first * BLOCK : first * BLOCK + x.shape[1]], in_=x, func=ACT.Sqrt)
 
         def quantize_z(a, c):
             images = slice(c * CHUNK, (c + 1) * CHUNK)
             nc.vector.quantize_mx(out=z_codes[:, a, images].bitcast(FP8X4), scales=z_plane[:, a, images], in_=z[a, c][:])
 
-        def round_update(part, passes, name):
-            first, blocks = UPDATE_PARTS[part]
-            grouped = held.tile([P, passes.stop - passes.start, blocks * P, PACK], BF16, name=name, align_bytes=64)
-            raw = wd_raw[:, passes, :, first * P : (first + blocks) * P]
+        def round_update(part, name):
+            first, count = UPDATE_PARTS[part]
+            grouped = held.tile([P, PASSES, count * P, PACK], BF16, name=name, align_bytes=ALIGN)
             nc.vector.tensor_copy(
                 out=grouped[:].rearrange("p a (g i) t -> p a g t i", i=RUN),
-                in_=raw.rearrange("p a t (g i) -> p a g t i", i=RUN),
+                in_=wd_raw[:, :, :, first * P : (first + count) * P].rearrange("p a t (g i) -> p a g t i", i=RUN),
             )
             return grouped
 
-        def quantize_update(part, passes, grouped):
+        def quantize_update(part, grouped):
             first = UPDATE_PARTS[part][0]
             nc.vector.quantize_mx(
-                out=wd_codes[first][:, passes].rearrange("p a b n -> p (a b n)").bitcast(FP8X4),
-                scales=wd_plane[first][:, passes].rearrange("p a b n -> p (a b n)"),
+                out=wd_codes[first][:].rearrange("p a b n -> p (a b n)").bitcast(FP8X4),
+                scales=wd_plane[first][:].rearrange("p a b n -> p (a b n)"),
                 in_=grouped[:].rearrange("p a n t -> p (a n t)"),
             )
 
         def project(c, nb, number):
             acc = bank(number, [P, CHUNK])
             images = slice(c * CHUNK, (c + 1) * CHUNK)
-            first = max(f for f, blocks in UPDATE_PARTS if f <= nb)
-            stored = [(wb_codes[:, a, 2 * nb * P : 2 * (nb + 1) * P].bitcast(FP4X4), wb_plane[:, a, nb * P : (nb + 1) * P], a) for a in range(PASSES)]
-            update = [(wd_codes[first][:, a, nb - first].bitcast(FP8X4), wd_plane[first][:, a, nb - first], a) for a in range(PASSES)]
+            first = max(f for f, count in UPDATE_PARTS if f <= nb)
+            stored, update = [], []
+            for a in range(PASSES):
+                wb_operand = wb_codes[:, a, 2 * nb * P : 2 * (nb + 1) * P].bitcast(FP4X4)
+                stored.append((wb_operand, wb_plane[:, a, nb * P : (nb + 1) * P], a))
+                update.append((wd_codes[first][:, a, nb - first].bitcast(FP8X4), wd_plane[first][:, a, nb - first], a))
             passes = stored + update if first else [stored[0], update[0], stored[1], update[1]]
             for k, (codes, plane, a) in enumerate(passes):
                 nc.tensor.matmul_mx(
@@ -226,7 +224,7 @@ def tile_list_visual_word_hash_kernel(
                 )
             return acc
 
-        nc.vector.tensor_copy(early_image_rows[:], image_table_rows[:].indirect(entries(image_list, 0, 2 * CHUNK)))
+        gather_image_rows(early_image_rows, 0, 2)
         gather_word_rows(0)
         nc.vector.tensor_copy(out=early_rows[:, PASS:].bitcast(I32), in_=early_image_rows[:].bitcast(I32))
         reorder_word_rows(0, early_rows)
@@ -238,111 +236,114 @@ def tile_list_visual_word_hash_kernel(
         for c in range(CHUNKS):
             gather_image_codes(c)
 
-        word_codes[1] = reused.tile([P, PASS], U32, name="word_codes1", align_bytes=64, offset=LATE - PACK * PASS)
-        late_image_rows = reused.tile([P, CHUNK], U8, name="late_image_rows", align_bytes=64, offset=LATE)
+        word_codes[1] = placed.tile([P, PASS], U32, name="word_codes1", align_bytes=ALIGN, offset=SEAM - PACK * PASS)
+        late_image_rows = placed.tile([P, CHUNK], U8, name="late_image_rows", align_bytes=ALIGN, offset=SEAM)
         gather_word_codes(1)
-        nc.vector.tensor_copy(late_image_rows[:], image_table_rows[:].indirect(entries(image_list, 2 * CHUNK, CHUNK)))
+        gather_image_rows(late_image_rows, 2, 1)
         move_scale_rows(nc.sync, late_plane, late_image_rows)
 
-        wd_raw = held.tile([P, PASSES, PACK, N], F32, name="wd_raw")
+        wd_raw = held.tile([P, PASSES, PACK, N], F32, name="early_rows_then_wd")
         wd_rows = wd.rearrange("(a p t) n -> a p t n", p=P, t=PACK)
         for a in range(PASSES):
             nc.sync.dma_start(out=wd_raw[:, a], in_=wd_rows[a])
-        wb_codes = held.tile([P, PASSES, 2 * N], U8, name="wb_codes", align_bytes=64)
+        wb_codes = held.tile([P, PASSES, 2 * N], U8, name="wb_codes", align_bytes=ALIGN)
         nc.sync.dma_start(out=wb_codes[:].bitcast(I32), in_=wb_words.rearrange("a p c -> p a c").bitcast(I32))
         wb_rows = wb_scales.rearrange("a q c -> q a c")
         for r in range(PACK):
             nc.sync.dma_start(out=wb_plane[r:P:QUAD].bitcast(I32), in_=wb_rows[r::PACK].bitcast(I32))
-        bias = held.tile([P, NBLOCKS], F32, name="bias")
+        bias = held.tile([P, ROW_BLOCKS], F32, name="bias")
         with nc.allow_non_contiguous_dma(reason="one bias value a partition and block of output rows"):
             nc.sync.dma_start(out=bias[:], in_=b.rearrange("(nb p) -> p nb", p=P))
 
-        late = held.tile([P, 2 * UNIT], F32, name="late_then_results")
+        late = held.tile([P, PASSES * UNIT], F32, name="late_then_results")
         z = {
-            (a, c): held.tile([P, UNIT], BF16, name="z%d%d" % (a, c), align_bytes=64)
+            (a, c): held.tile([P, UNIT], BF16, name="z%d%d" % (a, c), align_bytes=ALIGN)
             for a in range(PASSES)
             for c in range(CHUNKS)
         }
-        magnitude = {
+        by_slot = {
             (0, 0): held.tile([P, UNIT], F32, name="magnitude00")[:],
             (0, 1): held.tile([P, UNIT], F32, name="magnitude01")[:],
             (1, 1): held.tile([P, UNIT], F32, name="magnitude11")[:],
-            (1, 2): late[:, UNIT : 2 * UNIT],
+            (1, 2): late[:, UNIT : UNIT + BLOCK],
         }
+        by_image = {
+            (1, 0, 0): held.tile([P, 2 * BLOCK], F32, name="magnitude100")[:],
+            (1, 0, 2): held.tile([P, 2 * BLOCK], F32, name="magnitude102")[:],
+            (0, 2, 0): late[:, 0 : 2 * BLOCK],
+            (0, 2, 2): late[:, 2 * BLOCK : UNIT],
+        }
+        for k in range(1, PACK):
+            by_image[1, 2, k] = late[:, UNIT + k * BLOCK : UNIT + (k + 1) * BLOCK]
+        signed = {}
 
-        halves = {
-            (1, 0, 0): held.tile([P, HALF], F32, name="half100"),
-            (1, 0, 2): held.tile([P, HALF], F32, name="half102"),
-            (0, 2, 0): late[:, 0:HALF],
-            (0, 2, 2): late[:, HALF:UNIT],
-        }
-        shared = CHUNK - VECTOR_BLOCKS * P
         for t in range(PACK):
             scalar_slot(0, 0, t, 4 + t)
         scalar_slot(0, 1, 0, 0)
-        interleaving_root(0, 0)
+        interleaving_root(0, 0, CHUNK)
         for t in range(1, PACK):
             scalar_slot(0, 1, t, t)
 
-        signed, grouped, both = {}, {}, slice(0, PASSES)
-        for k in range(1, PACK):
-            halves[1, 2, k] = late[:, UNIT + k * BLOCK : UNIT + (k + 1) * BLOCK]
-        signed[1, 0, 0] = vector_weighted(1, 0, 0, [4, 5])
-        signed[1, 0, 2] = vector_weighted(1, 0, 2, [6, 7])
-        vector_magnitude(1, 0, 0, 2, signed[1, 0, 0])
-        vector_magnitude(1, 0, 2, 2, signed[1, 0, 2])
+        vector_weighted(1, 0, 0, [4, 5])
+        vector_weighted(1, 0, 2, [6, 7])
+        vector_magnitude(1, 0, 0)
+        vector_magnitude(1, 0, 2)
         quantize_z(0, 0)
-        grouped[0] = round_update(0, both, "update0")
+        grouped = [round_update(0, "update0")]
+
         scalar_slot(1, 1, 0, 0)
-        interleaving_root(0, 1)
-        scalar_slot(1, 1, 1, 1)
-        scalar_slot(1, 1, 2, 2)
-        scalar_slot(1, 1, 3, 3)
-        plain_root(1, 0, 0, 2)
-        plain_root(1, 0, 2, 2)
-        signed[0, 2, 0] = vector_weighted(0, 2, 0, [6, 7])
-        quantize_update(0, both, grouped[0])
-        signed[0, 2, 2] = vector_weighted(0, 2, 2, [4, 5])
+        interleaving_root(0, 1, CHUNK)
+        for t in range(1, PACK):
+            scalar_slot(1, 1, t, t)
+        plain_root(1, 0, 0)
+        plain_root(1, 0, 2)
+
+        vector_weighted(0, 2, 0, [6, 7])
+        quantize_update(0, grouped[0])
+        vector_weighted(0, 2, 2, [4, 5])
         quantize_z(0, 1)
-        vector_magnitude(0, 2, 0, 2, signed[0, 2, 0])
-        vector_magnitude(0, 2, 2, 2, signed[0, 2, 2])
+        vector_magnitude(0, 2, 0)
+        vector_magnitude(0, 2, 2)
         quantize_z(1, 0)
+
         first_block = bank(0, [P, PACK, P])
         for t in range(PACK):
             response(first_block[:, t, :], 1, t, 2, 0, P)
         for t in range(PACK):
             scalar_magnitude(1, 2, t, first_block[:, t, :])
-        interleaving_root(1, 1)
-        plain_root(0, 2, 0, 2)
-        plain_root(0, 2, 2, 2)
-        signed[1, 2, 1] = vector_weighted(1, 2, 1, [6])
-        signed[1, 2, 2] = vector_weighted(1, 2, 2, [7])
-        signed[1, 2, 3] = vector_weighted(1, 2, 3, [2])
-        vector_magnitude(1, 2, 1, 1, signed[1, 2, 1])
-        quantize_z(1, 1)
-        vector_magnitude(1, 2, 2, 1, signed[1, 2, 2])
-        vector_magnitude(1, 2, 3, 1, signed[1, 2, 3])
-        quantize_z(0, 2)
-        interleaving_root(1, 2, shared)
-        plain_root(1, 2, 1, 1)
-        plain_root(1, 2, 2, 1)
-        plain_root(1, 2, 3, 1)
-        grouped[1] = round_update(1, both, "z02")
-        quantize_z(1, 2)
-        quantize_update(1, both, grouped[1])
-        grouped[2] = round_update(2, both, "z12")
-        quantize_update(2, both, grouped[2])
+        interleaving_root(1, 1, CHUNK)
+        plain_root(0, 2, 0)
+        plain_root(0, 2, 2)
 
-        pieces = [(0, 0), (0, 1), (1, 0), (1, 1), (2, 0), (2, 1), (0, 2), (1, 2), (2, 2), (0, 3), (1, 3), (2, 3)]
-        free_order = [1, 3, 4, 5, 6, 7, 0, 2]
-        y = [project(c, nb, number) for number, (c, nb) in zip(free_order, pieces)]
+        for k, number in [(1, 6), (2, 7), (3, 2)]:
+            vector_weighted(1, 2, k, [number])
+        vector_magnitude(1, 2, 1)
+        quantize_z(1, 1)
+        vector_magnitude(1, 2, 2)
+        vector_magnitude(1, 2, 3)
+        quantize_z(0, 2)
+        interleaving_root(1, 2, P)
+        for k in range(1, PACK):
+            plain_root(1, 2, k)
+
+        grouped.append(round_update(1, "z02"))
+        quantize_z(1, 2)
+        quantize_update(1, grouped[1])
+        grouped.append(round_update(2, "z12"))
+        quantize_update(2, grouped[2])
+
+        pieces = [(c, nb) for first, count in UPDATE_PARTS for c in range(CHUNKS) for nb in range(first, first + count)]
+        sum_banks = [1, 3, 4, 5, 6, 7, 0, 2]
+        y = [project(c, nb, number) for number, (c, nb) in zip(sum_banks, pieces)]
 
         results = held.tile([P, len(pieces) * CHUNK], F32, name="late_then_results")
+        cuts = {0: [0, P, CHUNK], len(pieces) - 1: [0, CHUNK // 2, CHUNK]}
         for k, (c, nb) in enumerate(pieces):
             if k >= len(y):
-                y.append(project(c, nb, free_order[k - len(free_order)]))
-            queue = nc.scalar if k % 2 == 1 else nc.sync
-            for first, last in [(0, P), (P, CHUNK)] if k == 0 else [(0, CHUNK)]:
+                y.append(project(c, nb, sum_banks[k - len(sum_banks)]))
+            edges = cuts.get(k, [0, CHUNK])
+            for first, last in zip(edges, edges[1:]):
+                queue = nc.scalar if k % 2 == 1 and last == CHUNK else nc.sync
                 result = results[:, k * CHUNK + first : k * CHUNK + last]
                 nc.scalar.activation(out=result, in_=y[k][:, first:last], func=ACT.Tanh, bias=bias[:, nb : nb + 1])
                 queue.dma_start(out=out[nb * P : (nb + 1) * P, c * CHUNK + first : c * CHUNK + last], in_=result)

@@ -100,8 +100,7 @@ def tile_list_visual_word_hash_kernel(
         for first, count in UPDATE_PARTS:
             wd_codes[first] = held.tile([P, PASSES, count, P], U32, name="wd_codes%d" % first, align_bytes=ALIGN)
             wd_plane[first] = held.tile([P, PASSES, count, P], U8, name="wd_plane%d" % first, align_bytes=ALIGN)
-        z_codes = held.tile([P, PASSES, S2], U32, name="z_codes", align_bytes=ALIGN)
-        z_plane = held.tile([P, PASSES, S2], U8, name="z_plane", align_bytes=ALIGN)
+        z_codes, z_plane = {}, {}
 
         def gather_word_rows(a):
             nc.vector.tensor_copy(listed_rows[a][:], word_table_rows[:].indirect(entries(word_list, a * PASS, PASS)))
@@ -157,8 +156,7 @@ def tile_list_visual_word_hash_kernel(
                 func=ACT.Sqrt,
             )
 
-        def vector_weighted(a, c, first, banks):
-            product = ring.tile([P, len(banks) * BLOCK], F32, name="signed")
+        def vector_weighted(a, c, first, banks, product):
             for k, number in enumerate(banks):
                 acc = bank(number, [P, PACK, P])
                 for t in range(PACK):
@@ -181,9 +179,10 @@ def tile_list_visual_word_hash_kernel(
             x = by_image[a, c, first]
             nc.scalar.activation(out=z[a, c][:, first * BLOCK : first * BLOCK + x.shape[1]], in_=x, func=ACT.Sqrt)
 
-        def quantize_z(a, c):
-            images = slice(c * CHUNK, (c + 1) * CHUNK)
-            nc.vector.quantize_mx(out=z_codes[:, a, images].bitcast(FP8X4), scales=z_plane[:, a, images], in_=z[a, c][:])
+        def quantize_z(a, c, name):
+            z_codes[a, c] = held.tile([P, CHUNK], U32, name=name, align_bytes=ALIGN)
+            z_plane[a, c] = held.tile([P, CHUNK], U8, name="z_plane%d%d" % (a, c), align_bytes=ALIGN)
+            nc.vector.quantize_mx(out=z_codes[a, c][:].bitcast(FP8X4), scales=z_plane[a, c][:], in_=z[a, c][:])
 
         def round_update(part, name):
             first, count = UPDATE_PARTS[part]
@@ -204,21 +203,20 @@ def tile_list_visual_word_hash_kernel(
 
         def project(c, nb, number):
             acc = bank(number, [P, CHUNK])
-            images = slice(c * CHUNK, (c + 1) * CHUNK)
             first = max(f for f, count in UPDATE_PARTS if f <= nb)
             stored, update = [], []
             for a in range(PASSES):
                 wb_operand = wb_codes[:, a, 2 * nb * P : 2 * (nb + 1) * P].bitcast(FP4X4)
                 stored.append((wb_operand, wb_plane[:, a, nb * P : (nb + 1) * P], a))
                 update.append((wd_codes[first][:, a, nb - first].bitcast(FP8X4), wd_plane[first][:, a, nb - first], a))
-            passes = stored + update if first else [stored[0], update[0], stored[1], update[1]]
+            passes = stored + update if first and c < 2 else [stored[0], update[0], stored[1], update[1]]
             for k, (codes, plane, a) in enumerate(passes):
                 nc.tensor.matmul_mx(
                     out=acc[:],
                     lhsT=codes,
                     lhsT_scale=plane,
-                    rhs=z_codes[:, a, images].bitcast(FP8X4),
-                    rhs_scale=z_plane[:, a, images],
+                    rhs=z_codes[a, c][:].bitcast(FP8X4),
+                    rhs_scale=z_plane[a, c][:],
                     start=(k == 0),
                     stop=(k == len(passes) - 1),
                 )
@@ -277,6 +275,9 @@ def tile_list_visual_word_hash_kernel(
             by_image[1, 2, k] = late[:, UNIT + k * BLOCK : UNIT + (k + 1) * BLOCK]
         signed = {}
 
+        def pair():
+            return ring.tile([P, 2 * BLOCK], F32, name="signed")
+
         for t in range(PACK):
             scalar_slot(0, 0, t, 4 + t)
         scalar_slot(0, 1, 0, 0)
@@ -284,11 +285,11 @@ def tile_list_visual_word_hash_kernel(
         for t in range(1, PACK):
             scalar_slot(0, 1, t, t)
 
-        vector_weighted(1, 0, 0, [4, 5])
-        vector_weighted(1, 0, 2, [6, 7])
+        vector_weighted(1, 0, 0, [4, 5], pair())
+        vector_weighted(1, 0, 2, [6, 7], pair())
         vector_magnitude(1, 0, 0)
         vector_magnitude(1, 0, 2)
-        quantize_z(0, 0)
+        quantize_z(0, 0, "z_codes00")
         grouped = [round_update(0, "update0")]
 
         scalar_slot(1, 1, 0, 0)
@@ -298,13 +299,13 @@ def tile_list_visual_word_hash_kernel(
         plain_root(1, 0, 0)
         plain_root(1, 0, 2)
 
-        vector_weighted(0, 2, 0, [6, 7])
+        vector_weighted(0, 2, 0, [6, 7], pair())
         quantize_update(0, grouped[0])
-        vector_weighted(0, 2, 2, [4, 5])
-        quantize_z(0, 1)
+        vector_weighted(0, 2, 2, [4, 5], pair())
+        quantize_z(0, 1, "z_codes01")
         vector_magnitude(0, 2, 0)
         vector_magnitude(0, 2, 2)
-        quantize_z(1, 0)
+        quantize_z(1, 0, "z_codes10")
 
         first_block = bank(0, [P, PACK, P])
         for t in range(PACK):
@@ -316,24 +317,35 @@ def tile_list_visual_word_hash_kernel(
         plain_root(0, 2, 2)
 
         for k, number in [(1, 6), (2, 7), (3, 2)]:
-            vector_weighted(1, 2, k, [number])
+            vector_weighted(1, 2, k, [number], held.tile([P, BLOCK], F32, name="last%d" % k, align_bytes=ALIGN))
         vector_magnitude(1, 2, 1)
-        quantize_z(1, 1)
+        quantize_z(1, 1, "z_codes11")
         vector_magnitude(1, 2, 2)
         vector_magnitude(1, 2, 3)
-        quantize_z(0, 2)
         interleaving_root(1, 2, P)
         for k in range(1, PACK):
             plain_root(1, 2, k)
 
-        grouped.append(round_update(1, "z02"))
-        quantize_z(1, 2)
-        quantize_update(1, grouped[1])
-        grouped.append(round_update(2, "z12"))
-        quantize_update(2, grouped[2])
+        for part, name in ((1, "last2"), (2, "last3")):
+            first = UPDATE_PARTS[part][0]
+            rounded = held.tile([P, PASSES, P, PACK], BF16, name=name, align_bytes=ALIGN)
+            for a in range(PASSES):
+                nc.vector.tensor_copy(
+                    out=rounded[:, a].rearrange("p (g i) t -> p g t i", i=RUN),
+                    in_=wd_raw[:, a, :, first * P : (first + 1) * P].rearrange("p t (g i) -> p g t i", i=RUN),
+                )
+            for a in range(PASSES):
+                nc.vector.quantize_mx(
+                    out=wd_codes[first][:, a, 0].bitcast(FP8X4),
+                    scales=wd_plane[first][:, a, 0],
+                    in_=rounded[:, a].rearrange("p n t -> p (n t)"),
+                )
+        quantize_z(0, 2, "last2")
+        quantize_z(1, 2, "last3")
 
-        pieces = [(c, nb) for first, count in UPDATE_PARTS for c in range(CHUNKS) for nb in range(first, first + count)]
-        sum_banks = [1, 3, 4, 5, 6, 7, 0, 2]
+        pieces = [(c, nb) for first, count in UPDATE_PARTS for c in range(2) for nb in range(first, first + count)]
+        pieces = pieces + [(2, nb) for nb in range(ROW_BLOCKS)]
+        sum_banks = [1, 3, 4, 5, 0, 6, 7, 2]
         y = [project(c, nb, number) for number, (c, nb) in zip(sum_banks, pieces)]
 
         results = held.tile([P, len(pieces) * CHUNK], F32, name="late_then_results")

@@ -349,7 +349,7 @@ def tile_list_visual_word_hash_kernel(
         y = [project(c, nb, number) for number, (c, nb) in zip(sum_banks, pieces)]
 
         results = held.tile([P, len(pieces) * CHUNK], F32, name="late_then_results")
-        cuts = {0: [0, P, CHUNK], len(pieces) - 1: [0, CHUNK // 2, CHUNK]}
+        cuts = {0: [0, P, CHUNK]}
         for k, (c, nb) in enumerate(pieces):
             if k >= len(y):
                 y.append(project(c, nb, sum_banks[k - len(sum_banks)]))

@@ -269,7 +269,6 @@ def tile_list_visual_word_hash_kernel(
             (1, 0, 0): held.tile([P, 2 * BLOCK], F32, name="magnitude100")[:],
             (1, 0, 2): held.tile([P, 2 * BLOCK], F32, name="magnitude102")[:],
             (0, 2, 0): late[:, 0 : 2 * BLOCK],
-            (0, 2, 2): late[:, 2 * BLOCK : UNIT],
         }
         for k in range(1, PACK):
             by_image[1, 2, k] = late[:, UNIT + k * BLOCK : UNIT + (k + 1) * BLOCK]
@@ -304,8 +303,9 @@ def tile_list_visual_word_hash_kernel(
         vector_weighted(0, 2, 2, [4, 5], pair())
         quantize_z(0, 1, "z_codes01")
         vector_magnitude(0, 2, 0)
-        vector_magnitude(0, 2, 2)
         quantize_z(1, 0, "z_codes10")
+        by_image[0, 2, 2] = held.tile([P, 2 * BLOCK], F32, name="z10", align_bytes=ALIGN)[:]
+        vector_magnitude(0, 2, 2)
 
         first_block = bank(0, [P, PACK, P])
         for t in range(PACK):

@@ -30,8 +30,14 @@ ALIGN = 64
 RUN = 4
 UNIT = PACK * CHUNK
 BLOCK = PACK * P
+HALF = UNIT // 2
+HALF_BYTES = 4 * HALF
 SEAM = PACK * T2 + PACK * PASS
-UPDATE_PARTS = [(0, 2), (2, 1), (3, 1)]
+RESULTS_AT = 24 * 1024
+RESULTS_END = RESULTS_AT + 4 * ROW_BLOCKS * S2
+RING_AT = RESULTS_END - 4 * HALF_BYTES
+SLOT_BANKS = [[0, 1, 2, 3], [4, 5, 6, 7], [5, 6, 7, 4]]
+PRODUCT_BANKS = [[5, 6, 7, 0], [1, 2, 3, 4], [0, 1, 2, 3]]
 
 
 def move_scale_rows(queue, plane, rows):
@@ -49,12 +55,14 @@ def tile_list_visual_word_hash_kernel(
     nc = tc.nc
     with ExitStack() as ctx:
         held = ctx.enter_context(tc.tile_pool(name="held", bufs=1))
-        ring = ctx.enter_context(tc.tile_pool(name="ring", bufs=3))
         placed = ctx.enter_context(tc.tile_pool(name="placed", bufs=1))
         psum = ctx.enter_context(tc.psum_pool(name="psum", bufs=1))
 
         def bank(number, shape):
             return psum.tile(shape, F32, name="bank%d" % number)
+
+        def place(shape, dtype, name, offset):
+            return placed.tile(shape, dtype, name=name, align_bytes=ALIGN, offset=offset)
 
         word_list = held.tile([P, S // LIST_ROWS], U16, name="word_list")
         image_list = held.tile([P, S2 // LIST_ROWS], U16, name="image_list")
@@ -64,21 +72,21 @@ def tile_list_visual_word_hash_kernel(
         word_table_rows = held.tile([P, T], U8, name="word_table_rows", align_bytes=ALIGN)
         image_table_rows = held.tile([P, T2], U8, name="image_table_rows", align_bytes=ALIGN)
         word_table = held.tile([P, T], U32, name="word_table", align_bytes=ALIGN)
-        image_table = placed.tile([P, T2], U32, name="image_table", align_bytes=ALIGN, offset=0)
-        early_planes = held.tile([P, PASS + 2 * CHUNK], U8, name="early_planes", align_bytes=ALIGN)
-        middle_plane = held.tile([P, PASS], U8, name="middle_plane", align_bytes=ALIGN)
+        image_table = place([P, T2], U32, "image_table", 0)
+        planes = [
+            held.tile([P, PASS + (2 - a) * CHUNK], U8, name="planes%d" % a, align_bytes=ALIGN) for a in range(PASSES)
+        ]
         wb_plane = held.tile([P, PASSES, N], U8, name="wb_plane", align_bytes=ALIGN)
-        late_plane = held.tile([P, CHUNK], U8, name="late_plane", align_bytes=ALIGN)
         nc.vector.memset(image_table_rows[0:ROWS_AT].bitcast(I32), 0)
         nc.vector.memset(word_table_rows[0:ROWS_AT].bitcast(I32), 0)
-        for plane in (early_planes, middle_plane, late_plane, wb_plane):
+        for plane in planes + [wb_plane]:
             nc.gpsimd.memset(plane[:].bitcast(I32), 0)
         nc.scalar.dma_start(out=image_table_rows[ROWS_AT:P].bitcast(I32), in_=tab2_scales[0].bitcast(I32))
         nc.scalar.dma_start(out=word_table_rows[ROWS_AT:P].bitcast(I32), in_=tab_scales[0].bitcast(I32))
         nc.sync.dma_start(out=word_table[:].bitcast(I32), in_=tab_words[0].rearrange("p c t -> p (c t)").bitcast(I32))
         nc.sync.dma_start(out=image_table[:].bitcast(I32), in_=tab2_words[0].rearrange("p c t -> p (c t)").bitcast(I32))
 
-        weight_tile = placed.tile([P, 2 * ALIGN // 4], F32, name="weight", align_bytes=ALIGN, offset=SEAM - ALIGN)
+        weight_tile = place([P, 2 * ALIGN // 4], F32, "weight", SEAM - ALIGN)
         weight = weight_tile[:, 0 : PASSES * PACK].rearrange("p (a t) -> p a t", a=PASSES)
         weight_sq = held.tile([P, PASSES, PACK], F32, name="weight_sq")
         nc.sync.dma_start(out=weight, in_=wt.rearrange("(a p t) -> p a t", p=P, t=PACK))
@@ -88,27 +96,19 @@ def tile_list_visual_word_hash_kernel(
         nc.scalar.activation(out=zero_root[:], in_=zero[:], func=ACT.Sqrt)
         nc.scalar.activation(out=weight_sq[:], in_=weight, func=ACT.Square, bias=zero_root[:])
 
+        rows = [
+            held.tile([P, PASS + 2 * CHUNK], U8, name="rows0", align_bytes=ALIGN),
+            held.tile([P, PASS + CHUNK], U8, name="rows1", align_bytes=ALIGN),
+        ]
+        word_plane = [planes[a][:, 0:PASS] for a in range(PASSES)]
+        image_plane = [planes[0][:, PASS : PASS + CHUNK], planes[0][:, PASS + CHUNK :], planes[1][:, PASS:]]
         word_codes = {0: held.tile([P, PASS], U32, name="word_codes0", align_bytes=ALIGN)}
-        listed_rows = [held.tile([P, PASS], U8, name="listed_rows%d" % a) for a in range(PASSES)]
-        early_image_rows = held.tile([P, 2 * CHUNK], U8, name="early_image_rows")
-        early_rows = held.tile([P, PASS + 2 * CHUNK], U8, name="early_rows_then_wd")
-        middle_rows = held.tile([P, PASS], U8, name="middle_rows")
-        word_plane = [early_planes[:, 0:PASS], middle_plane[:]]
-        image_plane = [early_planes[:, PASS : PASS + CHUNK], early_planes[:, PASS + CHUNK :], late_plane[:]]
-        image_codes = [held.tile([P, CHUNK], U32, name="image_codes%d" % c, align_bytes=ALIGN) for c in range(CHUNKS)]
-        wd_codes, wd_plane = {}, {}
-        for first, count in UPDATE_PARTS:
-            wd_codes[first] = held.tile([P, PASSES, count, P], U32, name="wd_codes%d" % first, align_bytes=ALIGN)
-            wd_plane[first] = held.tile([P, PASSES, count, P], U8, name="wd_plane%d" % first, align_bytes=ALIGN)
-        z_codes, z_plane = {}, {}
+        image_codes = {c: held.tile([P, CHUNK], U32, name="image_codes%d" % c, align_bytes=ALIGN) for c in range(2)}
 
         def gather_word_rows(a):
-            nc.vector.tensor_copy(listed_rows[a][:], word_table_rows[:].indirect(entries(word_list, a * PASS, PASS)))
-
-        def reorder_word_rows(a, rows):
             nc.vector.tensor_copy(
-                out=rows[:, 0:PASS].rearrange("p (t m) -> p t m", t=PACK),
-                in_=listed_rows[a][:].rearrange("p (m t) -> p t m", t=PACK),
+                rows[a][:, 0:PASS].rearrange("p (t m) -> p m t", t=PACK),
+                word_table_rows[:].indirect(entries(word_list, a * PASS, PASS)),
             )
 
         def gather_word_codes(a):
@@ -117,12 +117,52 @@ def tile_list_visual_word_hash_kernel(
                 word_table[:].indirect(entries(word_list, a * PASS, PASS)),
             )
 
-        def gather_image_rows(rows, c, chunks):
-            offsets = entries(image_list, c * CHUNK, chunks * CHUNK)
-            nc.vector.tensor_copy(rows[:], image_table_rows[:].indirect(offsets))
+        def gather_image_rows(dst, c):
+            nc.vector.tensor_copy(dst, image_table_rows[:].indirect(entries(image_list, c * CHUNK, dst.shape[1])))
 
         def gather_image_codes(c):
             nc.vector.tensor_copy(image_codes[c][:], image_table[:].indirect(entries(image_list, c * CHUNK, CHUNK)))
+
+        for a, queue in enumerate((nc.scalar, nc.sync)):
+            gather_image_rows(rows[a][:, PASS:], 2 * a)
+            gather_word_rows(a)
+            move_scale_rows(queue, planes[a], rows[a])
+        gather_word_codes(0)
+        for h in range(2):
+            nc.vector.tensor_copy(
+                image_codes[0][:, h * 2 * P : (h + 1) * 2 * P],
+                image_table[:].indirect(entries(image_list, h * 2 * P, 2 * P)),
+            )
+        gather_image_codes(1)
+        word_codes[1] = place([P, PASS], U32, "word_codes1", SEAM - PACK * PASS)
+        image_codes[2] = place([P, CHUNK], U32, "image_codes2", SEAM)
+        gather_word_codes(1)
+        gather_image_codes(2)
+
+        wd_rows = wd.rearrange("(a p t) n -> a p t n", p=P, t=PACK)
+        wd_tile = place([P, (4 * HALF_BYTES + PACK * CHUNK + ALIGN) // 4], F32, "wd_raw", RING_AT)
+        wd_raw = wd_tile[:, 0 : 2 * UNIT].rearrange("p (a t n) -> p a t n", a=PASSES, t=PACK)
+        for a in range(PASSES):
+            nc.sync.dma_start(out=wd_raw[:, a], in_=wd_rows[a])
+        wb_codes = held.tile([P, PASSES, 2 * N], U8, name="wb_codes", align_bytes=ALIGN)
+        nc.sync.dma_start(out=wb_codes[:].bitcast(I32), in_=wb_words.rearrange("a p c -> p a c").bitcast(I32))
+        wb_rows = wb_scales.rearrange("a q c -> q a c")
+        for r in range(PACK):
+            nc.sync.dma_start(out=wb_plane[r:P:QUAD].bitcast(I32), in_=wb_rows[r::PACK].bitcast(I32))
+        bias = held.tile([P, ROW_BLOCKS], F32, name="bias")
+        with nc.allow_non_contiguous_dma(reason="one bias value a partition and block of output rows"):
+            nc.sync.dma_start(out=bias[:], in_=b.rearrange("(nb p) -> p nb", p=P))
+
+        z = {
+            (a, c): held.tile([P, UNIT], BF16, name="z%d%d" % (a, c), align_bytes=ALIGN)
+            for a in range(PASSES)
+            for c in range(CHUNKS)
+        }
+        by_slot = [held.tile([P, UNIT], F32, name="magnitude%d" % c) for c in range(CHUNKS)]
+        signed = [held.tile([P, UNIT], F32, name="signed%d" % c, align_bytes=ALIGN) for c in range(2)]
+        signed_last = [held.tile([P, HALF], F32, name="signed2", align_bytes=ALIGN)]
+        signed_last += [held.tile([P, BLOCK], F32, name="last%d" % k, align_bytes=ALIGN) for k in (2, 3)]
+        wd_codes, wd_plane, z_codes, z_plane = {}, {}, {}, {}
 
         def response(acc, a, t, c, first, width):
             nc.tensor.matmul_mx(
@@ -135,81 +175,62 @@ def tile_list_visual_word_hash_kernel(
                 stop=True,
             )
 
-        def scalar_magnitude(a, c, t, acc):
-            width = acc.shape[1]
+        def scalar_slot(c, t):
+            acc = bank(SLOT_BANKS[c][t], [P, CHUNK])
+            response(acc[:], 0, t, c, 0, CHUNK)
             nc.scalar.activation(
-                out=by_slot[a, c][:, t * width : (t + 1) * width],
-                in_=acc,
-                func=ACT.Abs,
-                scale=weight_sq[:, a, t : t + 1],
+                out=by_slot[c][:, t * CHUNK : (t + 1) * CHUNK], in_=acc[:], func=ACT.Abs, scale=weight_sq[:, 0, t : t + 1]
             )
 
-        def scalar_slot(a, c, t, number):
-            acc = bank(number, [P, CHUNK])
-            response(acc[:], a, t, c, 0, CHUNK)
-            scalar_magnitude(a, c, t, acc[:])
-
-        def interleaving_root(a, c, width):
+        def interleaving_root(c):
             nc.scalar.activation(
-                out=z[a, c][:, 0 : PACK * width].rearrange("p (g i t) -> p g t i", i=RUN, t=PACK),
-                in_=by_slot[a, c][:, 0 : PACK * width].rearrange("p (t g i) -> p g t i", i=RUN, t=PACK),
+                out=z[0, c][:].rearrange("p (g i t) -> p g t i", i=RUN, t=PACK),
+                in_=by_slot[c][:].rearrange("p (t g i) -> p g t i", i=RUN, t=PACK),
                 func=ACT.Sqrt,
             )
 
-        def vector_weighted(a, c, first, banks, product):
-            for k, number in enumerate(banks):
-                acc = bank(number, [P, PACK, P])
-                for t in range(PACK):
-                    response(acc[:, t, :], a, t, c, (first + k) * P, P)
-                nc.vector.tensor_tensor(
-                    out=product[:, k * BLOCK : (k + 1) * BLOCK].rearrange("p (j t) -> p j t", t=PACK),
-                    in0=acc[:].rearrange("p t j -> p j t"),
-                    in1=weight_sq[:, a, :].unsqueeze(1).to_broadcast([P, P, PACK]),
-                    op=ALU.mult,
-                )
-            signed[a, c, first] = product[:]
-
-        def vector_magnitude(a, c, first):
-            x = signed[a, c, first]
-            nc.vector.scalar_tensor_tensor(
-                out=by_image[a, c, first], in0=x, scalar=-1.0, in1=x, op0=ALU.mult, op1=ALU.max
+        def vector_product(c, k, product):
+            acc = bank(PRODUCT_BANKS[c][k], [P, PACK, P])
+            for t in range(PACK):
+                response(acc[:, t, :], 1, t, c, k * P, P)
+            nc.vector.tensor_tensor(
+                out=product.rearrange("p (j t) -> p j t", t=PACK),
+                in0=acc[:].rearrange("p t j -> p j t"),
+                in1=weight_sq[:, 1, :].unsqueeze(1).to_broadcast([P, P, PACK]),
+                op=ALU.mult,
             )
 
-        def plain_root(a, c, first):
-            x = by_image[a, c, first]
-            nc.scalar.activation(out=z[a, c][:, first * BLOCK : first * BLOCK + x.shape[1]], in_=x, func=ACT.Sqrt)
+        def vector_magnitude(x, name, offset):
+            m = place([P, x.shape[1]], F32, name, offset)
+            nc.vector.scalar_tensor_tensor(out=m[:], in0=x, scalar=-1.0, in1=x, op0=ALU.mult, op1=ALU.max)
+            return m
 
-        def quantize_z(a, c, name):
-            z_codes[a, c] = held.tile([P, CHUNK], U32, name=name, align_bytes=ALIGN)
+        def plain_root(c, first, m):
+            nc.scalar.activation(out=z[1, c][:, first : first + m.shape[1]], in_=m[:], func=ACT.Sqrt)
+
+        def quantize_z(a, c, codes):
+            z_codes[a, c] = codes
             z_plane[a, c] = held.tile([P, CHUNK], U8, name="z_plane%d%d" % (a, c), align_bytes=ALIGN)
-            nc.vector.quantize_mx(out=z_codes[a, c][:].bitcast(FP8X4), scales=z_plane[a, c][:], in_=z[a, c][:])
+            nc.vector.quantize_mx(out=codes[:].bitcast(FP8X4), scales=z_plane[a, c][:], in_=z[a, c][:])
 
-        def round_update(part, name):
-            first, count = UPDATE_PARTS[part]
-            grouped = held.tile([P, PASSES, count * P, PACK], BF16, name=name, align_bytes=ALIGN)
-            nc.vector.tensor_copy(
-                out=grouped[:].rearrange("p a (g i) t -> p a g t i", i=RUN),
-                in_=wd_raw[:, :, :, first * P : (first + count) * P].rearrange("p a t (g i) -> p a g t i", i=RUN),
-            )
-            return grouped
-
-        def quantize_update(part, grouped):
-            first = UPDATE_PARTS[part][0]
+        def quantize_update(a, codes):
+            wd_codes[a] = codes
+            wd_plane[a] = held.tile([P, N], U8, name="wd_plane%d" % a, align_bytes=ALIGN)
             nc.vector.quantize_mx(
-                out=wd_codes[first][:].rearrange("p a b n -> p (a b n)").bitcast(FP8X4),
-                scales=wd_plane[first][:].rearrange("p a b n -> p (a b n)"),
-                in_=grouped[:].rearrange("p a n t -> p (a n t)"),
+                out=codes[:].bitcast(FP8X4), scales=wd_plane[a][:], in_=grouped[:, a].rearrange("p n t -> p (n t)")
             )
+
+        def codes_tile(name):
+            return held.tile([P, CHUNK], U32, name=name, align_bytes=ALIGN)
 
         def project(c, nb, number):
             acc = bank(number, [P, CHUNK])
-            first = max(f for f, count in UPDATE_PARTS if f <= nb)
-            stored, update = [], []
+            columns = slice(nb * P, (nb + 1) * P)
+            passes = []
             for a in range(PASSES):
                 wb_operand = wb_codes[:, a, 2 * nb * P : 2 * (nb + 1) * P].bitcast(FP4X4)
-                stored.append((wb_operand, wb_plane[:, a, nb * P : (nb + 1) * P], a))
-                update.append((wd_codes[first][:, a, nb - first].bitcast(FP8X4), wd_plane[first][:, a, nb - first], a))
-            passes = stored + update if first and c < 2 else [stored[0], update[0], stored[1], update[1]]
+                passes.append((wb_operand, wb_plane[:, a, columns], a))
+                passes.append((wd_codes[a][:, columns].bitcast(FP8X4), wd_plane[a][:, columns], a))
             for k, (codes, plane, a) in enumerate(passes):
                 nc.tensor.matmul_mx(
                     out=acc[:],
@@ -222,133 +243,74 @@ def tile_list_visual_word_hash_kernel(
                 )
             return acc
 
-        gather_image_rows(early_image_rows, 0, 2)
-        gather_word_rows(0)
-        nc.vector.tensor_copy(out=early_rows[:, PASS:].bitcast(I32), in_=early_image_rows[:].bitcast(I32))
-        reorder_word_rows(0, early_rows)
-        move_scale_rows(nc.scalar, early_planes, early_rows)
-        gather_word_rows(1)
-        gather_word_codes(0)
-        reorder_word_rows(1, middle_rows)
-        move_scale_rows(nc.sync, middle_plane, middle_rows)
-        for c in range(CHUNKS):
-            gather_image_codes(c)
+        for h in range(2):
+            for pair in range(2):
+                acc = bank(SLOT_BANKS[0][2 * h + pair], [P, 2, 2 * P])
+                for u in range(2):
+                    response(acc[:, u], 0, 2 * pair + u, 0, h * 2 * P, 2 * P)
+                for u in range(2):
+                    t = 2 * pair + u
+                    first = t * CHUNK + h * 2 * P
+                    nc.scalar.activation(
+                        out=by_slot[0][:, first : first + 2 * P],
+                        in_=acc[:, u],
+                        func=ACT.Abs,
+                        scale=weight_sq[:, 0, t : t + 1],
+                    )
+        scalar_slot(1, 0)
+        interleaving_root(0)
+        for k in range(PACK):
+            vector_product(0, k, signed[0][:, k * BLOCK : (k + 1) * BLOCK])
+        for t in range(1, PACK):
+            scalar_slot(1, t)
+        for k in range(PACK):
+            vector_product(1, k, signed[1][:, k * BLOCK : (k + 1) * BLOCK])
+        for t in range(PACK):
+            scalar_slot(2, t)
+        interleaving_root(1)
+        vector_product(2, 0, signed_last[0][:, 0:BLOCK])
+        vector_product(2, 1, signed_last[0][:, BLOCK:])
+        vector_product(2, 2, signed_last[1][:])
+        vector_product(2, 3, signed_last[2][:])
+        interleaving_root(2)
 
-        word_codes[1] = placed.tile([P, PASS], U32, name="word_codes1", align_bytes=ALIGN, offset=SEAM - PACK * PASS)
-        late_image_rows = placed.tile([P, CHUNK], U8, name="late_image_rows", align_bytes=ALIGN, offset=SEAM)
-        gather_word_codes(1)
-        gather_image_rows(late_image_rows, 2, 1)
-        move_scale_rows(nc.sync, late_plane, late_image_rows)
-
-        wd_raw = held.tile([P, PASSES, PACK, N], F32, name="early_rows_then_wd")
-        wd_rows = wd.rearrange("(a p t) n -> a p t n", p=P, t=PACK)
+        grouped = place([P, PASSES, N, PACK], BF16, "grouped", 0)
         for a in range(PASSES):
-            nc.sync.dma_start(out=wd_raw[:, a], in_=wd_rows[a])
-        wb_codes = held.tile([P, PASSES, 2 * N], U8, name="wb_codes", align_bytes=ALIGN)
-        nc.sync.dma_start(out=wb_codes[:].bitcast(I32), in_=wb_words.rearrange("a p c -> p a c").bitcast(I32))
-        wb_rows = wb_scales.rearrange("a q c -> q a c")
-        for r in range(PACK):
-            nc.sync.dma_start(out=wb_plane[r:P:QUAD].bitcast(I32), in_=wb_rows[r::PACK].bitcast(I32))
-        bias = held.tile([P, ROW_BLOCKS], F32, name="bias")
-        with nc.allow_non_contiguous_dma(reason="one bias value a partition and block of output rows"):
-            nc.sync.dma_start(out=bias[:], in_=b.rearrange("(nb p) -> p nb", p=P))
-
-        late = held.tile([P, PASSES * UNIT], F32, name="late_then_results")
-        z = {
-            (a, c): held.tile([P, UNIT], BF16, name="z%d%d" % (a, c), align_bytes=ALIGN)
-            for a in range(PASSES)
-            for c in range(CHUNKS)
-        }
-        by_slot = {
-            (0, 0): held.tile([P, UNIT], F32, name="magnitude00")[:],
-            (0, 1): held.tile([P, UNIT], F32, name="magnitude01")[:],
-            (1, 1): held.tile([P, UNIT], F32, name="magnitude11")[:],
-            (1, 2): late[:, UNIT : UNIT + BLOCK],
-        }
-        by_image = {
-            (1, 0, 0): held.tile([P, 2 * BLOCK], F32, name="magnitude100")[:],
-            (1, 0, 2): held.tile([P, 2 * BLOCK], F32, name="magnitude102")[:],
-            (0, 2, 0): late[:, 0 : 2 * BLOCK],
-        }
-        for k in range(1, PACK):
-            by_image[1, 2, k] = late[:, UNIT + k * BLOCK : UNIT + (k + 1) * BLOCK]
-        signed = {}
-
-        def pair():
-            return ring.tile([P, 2 * BLOCK], F32, name="signed")
-
-        for t in range(PACK):
-            scalar_slot(0, 0, t, 4 + t)
-        scalar_slot(0, 1, 0, 0)
-        interleaving_root(0, 0, CHUNK)
-        for t in range(1, PACK):
-            scalar_slot(0, 1, t, t)
-
-        vector_weighted(1, 0, 0, [4, 5], pair())
-        vector_weighted(1, 0, 2, [6, 7], pair())
-        vector_magnitude(1, 0, 0)
-        vector_magnitude(1, 0, 2)
-        quantize_z(0, 0, "z_codes00")
-        grouped = [round_update(0, "update0")]
-
-        scalar_slot(1, 1, 0, 0)
-        interleaving_root(0, 1, CHUNK)
-        for t in range(1, PACK):
-            scalar_slot(1, 1, t, t)
-        plain_root(1, 0, 0)
-        plain_root(1, 0, 2)
-
-        vector_weighted(0, 2, 0, [6, 7], pair())
-        quantize_update(0, grouped[0])
-        vector_weighted(0, 2, 2, [4, 5], pair())
-        quantize_z(0, 1, "z_codes01")
-        vector_magnitude(0, 2, 0)
-        quantize_z(1, 0, "z_codes10")
-        by_image[0, 2, 2] = held.tile([P, 2 * BLOCK], F32, name="z10", align_bytes=ALIGN)[:]
-        vector_magnitude(0, 2, 2)
-
-        first_block = bank(0, [P, PACK, P])
-        for t in range(PACK):
-            response(first_block[:, t, :], 1, t, 2, 0, P)
-        for t in range(PACK):
-            scalar_magnitude(1, 2, t, first_block[:, t, :])
-        interleaving_root(1, 1, CHUNK)
-        plain_root(0, 2, 0)
-        plain_root(0, 2, 2)
-
-        for k, number in [(1, 6), (2, 7), (3, 2)]:
-            vector_weighted(1, 2, k, [number], held.tile([P, BLOCK], F32, name="last%d" % k, align_bytes=ALIGN))
-        vector_magnitude(1, 2, 1)
-        quantize_z(1, 1, "z_codes11")
-        vector_magnitude(1, 2, 2)
-        vector_magnitude(1, 2, 3)
-        interleaving_root(1, 2, P)
-        for k in range(1, PACK):
-            plain_root(1, 2, k)
-
-        for part, name in ((1, "last2"), (2, "last3")):
-            first = UPDATE_PARTS[part][0]
-            rounded = held.tile([P, PASSES, P, PACK], BF16, name=name, align_bytes=ALIGN)
-            for a in range(PASSES):
-                nc.vector.tensor_copy(
-                    out=rounded[:, a].rearrange("p (g i) t -> p g t i", i=RUN),
-                    in_=wd_raw[:, a, :, first * P : (first + 1) * P].rearrange("p t (g i) -> p g t i", i=RUN),
+            for h in range(2):
+                nc.gpsimd.tensor_scalar(
+                    out=grouped[:, a, h * 2 * P : (h + 1) * 2 * P],
+                    in0=wd_raw[:, a, :, h * 2 * P : (h + 1) * 2 * P].rearrange("p t n -> p n t"),
+                    scalar1=1.0,
+                    scalar2=0.0,
+                    op0=ALU.mult,
+                    op1=ALU.add,
                 )
-            for a in range(PASSES):
-                nc.vector.quantize_mx(
-                    out=wd_codes[first][:, a, 0].bitcast(FP8X4),
-                    scales=wd_plane[first][:, a, 0],
-                    in_=rounded[:, a].rearrange("p n t -> p (n t)"),
-                )
-        quantize_z(0, 2, "last2")
-        quantize_z(1, 2, "last3")
 
-        pieces = [(c, nb) for first, count in UPDATE_PARTS for c in range(2) for nb in range(first, first + count)]
-        pieces = pieces + [(2, nb) for nb in range(ROW_BLOCKS)]
-        sum_banks = [1, 3, 4, 5, 0, 6, 7, 2]
+        quantize_z(0, 0, place([P, CHUNK], U32, "z_codes00", RESULTS_END))
+        quantize_update(0, place([P, N], U32, "wd_codes0", RESULTS_END + PACK * CHUNK))
+        quantize_z(0, 1, codes_tile("z_codes01"))
+        for c in range(2):
+            for h in range(2):
+                m = vector_magnitude(
+                    signed[c][:, h * HALF : (h + 1) * HALF], "ring%d%d" % (c, h), RING_AT + (2 * c + h) * HALF_BYTES
+                )
+                plain_root(c, h * HALF, m)
+        quantize_z(1, 0, codes_tile("z_codes10"))
+        plain_root(2, 0, vector_magnitude(signed_last[0][:], "ring20", RING_AT + HALF_BYTES))
+        for k in (2, 3):
+            m = vector_magnitude(signed_last[k - 1][:], "ring2%d" % k, RING_AT + 2 * HALF_BYTES + (k - 2) * 4 * BLOCK)
+            plain_root(2, k * BLOCK, m)
+        quantize_update(1, codes_tile("last2"))
+        quantize_z(1, 1, codes_tile("z_codes11"))
+
+        quantize_z(0, 2, codes_tile("last3"))
+        quantize_z(1, 2, codes_tile("z_codes12"))
+
+        pieces = [(c, nb) for c in range(CHUNKS) for nb in range(ROW_BLOCKS)]
+        sum_banks = [number for pair in zip(SLOT_BANKS[2], PRODUCT_BANKS[2]) for number in pair]
         y = [project(c, nb, number) for number, (c, nb) in zip(sum_banks, pieces)]
 
-        results = held.tile([P, len(pieces) * CHUNK], F32, name="late_then_results")
+        results = place([P, len(pieces) * CHUNK], F32, "results", RESULTS_AT)
         cuts = {0: [0, P, CHUNK]}
         for k, (c, nb) in enumerate(pieces):
             if k >= len(y):

@@ -141,9 +141,12 @@ def tile_list_visual_word_hash_kernel(
 
         wd_rows = wd.rearrange("(a p t) n -> a p t n", p=P, t=PACK)
         wd_tile = place([P, (4 * HALF_BYTES + PACK * CHUNK + ALIGN) // 4], F32, "wd_raw", RING_AT)
-        wd_raw = wd_tile[:, 0 : 2 * UNIT].rearrange("p (a t n) -> p a t n", a=PASSES, t=PACK)
-        for a in range(PASSES):
-            nc.sync.dma_start(out=wd_raw[:, a], in_=wd_rows[a])
+        wd_raw = [
+            wd_tile[:, 0:UNIT].rearrange("p (t n) -> p t n", t=PACK),
+            held.tile([P, PACK, N], F32, name="wd_raw1")[:],
+        ]
+        for a in (1, 0):
+            nc.sync.dma_start(out=wd_raw[a], in_=wd_rows[a])
         wb_codes = held.tile([P, PASSES, 2 * N], U8, name="wb_codes", align_bytes=ALIGN)
         nc.sync.dma_start(out=wb_codes[:].bitcast(I32), in_=wb_words.rearrange("a p c -> p a c").bitcast(I32))
         wb_rows = wb_scales.rearrange("a q c -> q a c")
@@ -213,12 +216,14 @@ def tile_list_visual_word_hash_kernel(
             z_plane[a, c] = held.tile([P, CHUNK], U8, name="z_plane%d%d" % (a, c), align_bytes=ALIGN)
             nc.vector.quantize_mx(out=codes[:].bitcast(FP8X4), scales=z_plane[a, c][:], in_=z[a, c][:])
 
-        def quantize_update(a, codes):
-            wd_codes[a] = codes
-            wd_plane[a] = held.tile([P, N], U8, name="wd_plane%d" % a, align_bytes=ALIGN)
+        def quantize_update(a, first, rounded, codes):
+            plane = held.tile([P, codes.shape[1]], U8, name="wd_plane%d%d" % (a, first), align_bytes=ALIGN)
             nc.vector.quantize_mx(
-                out=codes[:].bitcast(FP8X4), scales=wd_plane[a][:], in_=grouped[:, a].rearrange("p n t -> p (n t)")
+                out=codes[:].bitcast(FP8X4), scales=plane[:], in_=rounded.rearrange("p n t -> p (n t)")
             )
+            for k in range(codes.shape[1] // P):
+                wd_codes[a, first + k] = codes[:, k * P : (k + 1) * P]
+                wd_plane[a, first + k] = plane[:, k * P : (k + 1) * P]
 
         def codes_tile(name):
             return held.tile([P, CHUNK], U32, name=name, align_bytes=ALIGN)
@@ -230,7 +235,7 @@ def tile_list_visual_word_hash_kernel(
             for a in range(PASSES):
                 wb_operand = wb_codes[:, a, 2 * nb * P : 2 * (nb + 1) * P].bitcast(FP4X4)
                 passes.append((wb_operand, wb_plane[:, a, columns], a))
-                passes.append((wd_codes[a][:, columns].bitcast(FP8X4), wd_plane[a][:, columns], a))
+                passes.append((wd_codes[a, nb].bitcast(FP8X4), wd_plane[a, nb], a))
             for k, (codes, plane, a) in enumerate(passes):
                 nc.tensor.matmul_mx(
                     out=acc[:],
@@ -275,19 +280,18 @@ def tile_list_visual_word_hash_kernel(
         interleaving_root(2)
 
         grouped = place([P, PASSES, N, PACK], BF16, "grouped", 0)
-        for a in range(PASSES):
-            for h in range(2):
-                nc.gpsimd.tensor_scalar(
-                    out=grouped[:, a, h * 2 * P : (h + 1) * 2 * P],
-                    in0=wd_raw[:, a, :, h * 2 * P : (h + 1) * 2 * P].rearrange("p t n -> p n t"),
-                    scalar1=1.0,
-                    scalar2=0.0,
-                    op0=ALU.mult,
-                    op1=ALU.add,
-                )
+        for a, h in ((1, 0), (0, 0), (0, 1)):
+            nc.gpsimd.tensor_scalar(
+                out=grouped[:, a, h * 2 * P : (h + 1) * 2 * P],
+                in0=wd_raw[a][:, :, h * 2 * P : (h + 1) * 2 * P].rearrange("p t n -> p n t"),
+                scalar1=1.0,
+                scalar2=0.0,
+                op0=ALU.mult,
+                op1=ALU.add,
+            )
 
         quantize_z(0, 0, place([P, CHUNK], U32, "z_codes00", RESULTS_END))
-        quantize_update(0, place([P, N], U32, "wd_codes0", RESULTS_END + PACK * CHUNK))
+        quantize_update(0, 0, grouped[:, 0], place([P, N], U32, "wd_codes0", RESULTS_END + PACK * CHUNK))
         quantize_z(0, 1, codes_tile("z_codes01"))
         for c in range(2):
             for h in range(2):
@@ -300,13 +304,19 @@ def tile_list_visual_word_hash_kernel(
         for k in (2, 3):
             m = vector_magnitude(signed_last[k - 1][:], "ring2%d" % k, RING_AT + 2 * HALF_BYTES + (k - 2) * 4 * BLOCK)
             plain_root(2, k * BLOCK, m)
-        quantize_update(1, codes_tile("last2"))
+        quantize_update(1, 0, grouped[:, 1, 0 : 2 * P], held.tile([P, 2 * P], U32, name="last2", align_bytes=ALIGN))
         quantize_z(1, 1, codes_tile("z_codes11"))
-
-        quantize_z(0, 2, codes_tile("last3"))
+        rounded = held.tile([P, 2 * P, PACK], BF16, name="last3", align_bytes=ALIGN)
+        nc.vector.tensor_copy(
+            out=rounded[:].rearrange("p (g i) t -> p g t i", i=RUN),
+            in_=wd_raw[1][:, :, 2 * P :].rearrange("p t (g i) -> p g t i", i=RUN),
+        )
+        quantize_z(0, 2, codes_tile("z11"))
+        quantize_update(1, 2, rounded[:], held.tile([P, 2 * P], U32, name="wd_codes12", align_bytes=ALIGN))
         quantize_z(1, 2, codes_tile("z_codes12"))
 
-        pieces = [(c, nb) for c in range(CHUNKS) for nb in range(ROW_BLOCKS)]
+        pieces = [(c, nb) for first in (0, 2) for c in range(2) for nb in (first, first + 1)]
+        pieces = pieces + [(2, nb) for nb in range(ROW_BLOCKS)]
         sum_banks = [number for pair in zip(SLOT_BANKS[2], PRODUCT_BANKS[2]) for number in pair]
         y = [project(c, nb, number) for number, (c, nb) in zip(sum_banks, pieces)]
 

@@ -36,8 +36,9 @@ SEAM = PACK * T2 + PACK * PASS
 RESULTS_AT = 24 * 1024
 RESULTS_END = RESULTS_AT + 4 * ROW_BLOCKS * S2
 RING_AT = RESULTS_END - 4 * HALF_BYTES
-SLOT_BANKS = [[0, 1, 2, 3], [4, 5, 6, 7], [5, 6, 7, 4]]
-PRODUCT_BANKS = [[5, 6, 7, 0], [1, 2, 3, 4], [0, 1, 2, 3]]
+SLOT_BANKS = [None, [2, 5, 6, 7], [3, 4, 0, 1]]
+PRODUCT_BANKS = [[5, 6, 7, 3], [4, 0, 1, 2], [5, 6, 7, 2]]
+SUM_BANKS = [3, 4, 5, 0, 6, 1, 7, 2]
 
 
 def move_scale_rows(queue, plane, rows):
@@ -185,10 +186,11 @@ def tile_list_visual_word_hash_kernel(
                 out=by_slot[c][:, t * CHUNK : (t + 1) * CHUNK], in_=acc[:], func=ACT.Abs, scale=weight_sq[:, 0, t : t + 1]
             )
 
-        def interleaving_root(c):
+        def interleaving_root(c, first=0, count=CHUNK):
+            groups = slice(first // RUN, (first + count) // RUN)
             nc.scalar.activation(
-                out=z[0, c][:].rearrange("p (g i t) -> p g t i", i=RUN, t=PACK),
-                in_=by_slot[c][:].rearrange("p (t g i) -> p g t i", i=RUN, t=PACK),
+                out=z[0, c][:].rearrange("p (g i t) -> p g t i", i=RUN, t=PACK)[:, groups],
+                in_=by_slot[c][:].rearrange("p (t g i) -> p g t i", i=RUN, t=PACK)[:, groups],
                 func=ACT.Sqrt,
             )
 
@@ -248,35 +250,42 @@ def tile_list_visual_word_hash_kernel(
                 )
             return acc
 
-        for h in range(2):
-            for pair in range(2):
-                acc = bank(SLOT_BANKS[0][2 * h + pair], [P, 2, 2 * P])
-                for u in range(2):
-                    response(acc[:, u], 0, 2 * pair + u, 0, h * 2 * P, 2 * P)
-                for u in range(2):
-                    t = 2 * pair + u
-                    first = t * CHUNK + h * 2 * P
-                    nc.scalar.activation(
-                        out=by_slot[0][:, first : first + 2 * P],
-                        in_=acc[:, u],
-                        func=ACT.Abs,
-                        scale=weight_sq[:, 0, t : t + 1],
-                    )
+        def half_slots(h, slots, number):
+            acc = bank(number, [P, len(slots), 2 * P])
+            for u, t in enumerate(slots):
+                response(acc[:, u], 0, t, 0, h * 2 * P, 2 * P)
+            for u, t in enumerate(slots):
+                first = t * CHUNK + h * 2 * P
+                nc.scalar.activation(
+                    out=by_slot[0][:, first : first + 2 * P],
+                    in_=acc[:, u],
+                    func=ACT.Abs,
+                    scale=weight_sq[:, 0, t : t + 1],
+                )
+
+        for t in range(PACK):
+            half_slots(0, [t], t)
+        half_slots(1, [0], 4)
+        interleaving_root(0, 0, 2 * P)
+        half_slots(1, [1], 0)
+        half_slots(1, [2, 3], 1)
         scalar_slot(1, 0)
-        interleaving_root(0)
+        interleaving_root(0, 2 * P, 2 * P)
         for k in range(PACK):
             vector_product(0, k, signed[0][:, k * BLOCK : (k + 1) * BLOCK])
         for t in range(1, PACK):
             scalar_slot(1, t)
         for k in range(PACK):
             vector_product(1, k, signed[1][:, k * BLOCK : (k + 1) * BLOCK])
-        for t in range(PACK):
-            scalar_slot(2, t)
-        interleaving_root(1)
+        scalar_slot(2, 0)
+        scalar_slot(2, 1)
         vector_product(2, 0, signed_last[0][:, 0:BLOCK])
+        scalar_slot(2, 2)
         vector_product(2, 1, signed_last[0][:, BLOCK:])
+        scalar_slot(2, 3)
         vector_product(2, 2, signed_last[1][:])
         vector_product(2, 3, signed_last[2][:])
+        interleaving_root(1)
         interleaving_root(2)
 
         grouped = place([P, PASSES, N, PACK], BF16, "grouped", 0)
@@ -300,7 +309,9 @@ def tile_list_visual_word_hash_kernel(
                 )
                 plain_root(c, h * HALF, m)
         quantize_z(1, 0, codes_tile("z_codes10"))
-        plain_root(2, 0, vector_magnitude(signed_last[0][:], "ring20", RING_AT + HALF_BYTES))
+        for k in range(2):
+            x = signed_last[0][:, k * BLOCK : (k + 1) * BLOCK]
+            plain_root(2, k * BLOCK, vector_magnitude(x, "ring2%d" % k, RING_AT + HALF_BYTES + k * 4 * BLOCK))
         for k in (2, 3):
             m = vector_magnitude(signed_last[k - 1][:], "ring2%d" % k, RING_AT + 2 * HALF_BYTES + (k - 2) * 4 * BLOCK)
             plain_root(2, k * BLOCK, m)
@@ -317,7 +328,7 @@ def tile_list_visual_word_hash_kernel(
 
         pieces = [(c, nb) for first in (0, 2) for c in range(2) for nb in (first, first + 1)]
         pieces = pieces + [(2, nb) for nb in range(ROW_BLOCKS)]
-        sum_banks = [number for pair in zip(SLOT_BANKS[2], PRODUCT_BANKS[2]) for number in pair]
+        sum_banks = SUM_BANKS
         y = [project(c, nb, number) for number, (c, nb) in zip(sum_banks, pieces)]
 
         results = place([P, len(pieces) * CHUNK], F32, "results", RESULTS_AT)

@@ -299,14 +299,22 @@ def tile_list_visual_word_hash_kernel(
                 op1=ALU.add,
             )
 
+        first_magnitude = held.tile([P, HALF], F32, name="first_magnitude")
+        nc.vector.tensor_reduce(
+            out=first_magnitude[:],
+            in_=signed[0][:, 0:HALF].unsqueeze(2),
+            axis=mybir.AxisListType.X,
+            op=ALU.max,
+            apply_absolute_value=True,
+        )
         quantize_z(0, 0, place([P, CHUNK], U32, "z_codes00", RESULTS_END))
         quantize_update(0, 0, grouped[:, 0], place([P, N], U32, "wd_codes0", RESULTS_END + PACK * CHUNK))
         quantize_z(0, 1, codes_tile("z_codes01"))
         for c in range(2):
             for h in range(2):
-                m = vector_magnitude(
-                    signed[c][:, h * HALF : (h + 1) * HALF], "ring%d%d" % (c, h), RING_AT + (2 * c + h) * HALF_BYTES
-                )
+                x = signed[c][:, h * HALF : (h + 1) * HALF]
+                at = RING_AT + (2 * c + h) * HALF_BYTES
+                m = vector_magnitude(x, "ring%d%d" % (c, h), at) if c or h else first_magnitude
                 plain_root(c, h * HALF, m)
         quantize_z(1, 0, codes_tile("z_codes10"))
         for k in range(2):

@@ -36,9 +36,9 @@ SEAM = PACK * T2 + PACK * PASS
 RESULTS_AT = 24 * 1024
 RESULTS_END = RESULTS_AT + 4 * ROW_BLOCKS * S2
 RING_AT = RESULTS_END - 4 * HALF_BYTES
-SLOT_BANKS = [None, [2, 5, 6, 7], [3, 4, 0, 1]]
-PRODUCT_BANKS = [[5, 6, 7, 3], [4, 0, 1, 2], [5, 6, 7, 2]]
-SUM_BANKS = [3, 4, 5, 0, 6, 1, 7, 2]
+SLOT_BANKS = [None, [7, 0, 1, 2], [3, 4, 5, 6]]
+PRODUCT_BANKS = [[0, 1, 2, 3], [4, 5, 6, 7], [0, 1, 2, 7]]
+SUM_BANKS = [3, 4, 0, 5, 1, 6, 2, 7]
 
 
 def move_scale_rows(queue, plane, rows):
@@ -67,23 +67,24 @@ def tile_list_visual_word_hash_kernel(
 
         word_list = held.tile([P, S // LIST_ROWS], U16, name="word_list")
         image_list = held.tile([P, S2 // LIST_ROWS], U16, name="image_list")
-        nc.sync.dma_start(image_list[:], offs2)
         nc.sync.dma_start(word_list[:], offs)
+        nc.sync.dma_start(image_list[:], offs2)
 
         word_table_rows = held.tile([P, T], U8, name="word_table_rows", align_bytes=ALIGN)
         image_table_rows = held.tile([P, T2], U8, name="image_table_rows", align_bytes=ALIGN)
         word_table = held.tile([P, T], U32, name="word_table", align_bytes=ALIGN)
         image_table = place([P, T2], U32, "image_table", 0)
         planes = [
-            held.tile([P, PASS + (2 - a) * CHUNK], U8, name="planes%d" % a, align_bytes=ALIGN) for a in range(PASSES)
+            held.tile([P, width], U8, name="planes%d" % k, align_bytes=ALIGN)
+            for k, width in enumerate((S + 2 * CHUNK, CHUNK))
         ]
         wb_plane = held.tile([P, PASSES, N], U8, name="wb_plane", align_bytes=ALIGN)
-        nc.vector.memset(image_table_rows[0:ROWS_AT].bitcast(I32), 0)
         nc.vector.memset(word_table_rows[0:ROWS_AT].bitcast(I32), 0)
+        nc.vector.memset(image_table_rows[0:ROWS_AT].bitcast(I32), 0)
         for plane in planes + [wb_plane]:
             nc.gpsimd.memset(plane[:].bitcast(I32), 0)
-        nc.scalar.dma_start(out=image_table_rows[ROWS_AT:P].bitcast(I32), in_=tab2_scales[0].bitcast(I32))
         nc.scalar.dma_start(out=word_table_rows[ROWS_AT:P].bitcast(I32), in_=tab_scales[0].bitcast(I32))
+        nc.scalar.dma_start(out=image_table_rows[ROWS_AT:P].bitcast(I32), in_=tab2_scales[0].bitcast(I32))
         nc.sync.dma_start(out=word_table[:].bitcast(I32), in_=tab_words[0].rearrange("p c t -> p (c t)").bitcast(I32))
         nc.sync.dma_start(out=image_table[:].bitcast(I32), in_=tab2_words[0].rearrange("p c t -> p (c t)").bitcast(I32))
 
@@ -98,18 +99,18 @@ def tile_list_visual_word_hash_kernel(
         nc.scalar.activation(out=weight_sq[:], in_=weight, func=ACT.Square, bias=zero_root[:])
 
         rows = [
-            held.tile([P, PASS + 2 * CHUNK], U8, name="rows0", align_bytes=ALIGN),
-            held.tile([P, PASS + CHUNK], U8, name="rows1", align_bytes=ALIGN),
+            held.tile([P, S + 2 * CHUNK], U8, name="rows0", align_bytes=ALIGN),
+            held.tile([P, CHUNK], U8, name="rows1", align_bytes=ALIGN),
         ]
-        word_plane = [planes[a][:, 0:PASS] for a in range(PASSES)]
-        image_plane = [planes[0][:, PASS : PASS + CHUNK], planes[0][:, PASS + CHUNK :], planes[1][:, PASS:]]
+        word_plane = [planes[0][:, a * PASS : (a + 1) * PASS] for a in range(PASSES)]
+        image_plane = [planes[0][:, S : S + CHUNK], planes[0][:, S + CHUNK :], planes[1][:]]
         word_codes = {0: held.tile([P, PASS], U32, name="word_codes0", align_bytes=ALIGN)}
         image_codes = {c: held.tile([P, CHUNK], U32, name="image_codes%d" % c, align_bytes=ALIGN) for c in range(2)}
 
-        def gather_word_rows(a):
+        def gather_word_rows():
             nc.vector.tensor_copy(
-                rows[a][:, 0:PASS].rearrange("p (t m) -> p m t", t=PACK),
-                word_table_rows[:].indirect(entries(word_list, a * PASS, PASS)),
+                rows[0][:, 0:S].rearrange("p (a t m) -> p a m t", a=PASSES, t=PACK),
+                word_table_rows[:].indirect(word_list[:]),
             )
 
         def gather_word_codes(a):
@@ -124,10 +125,11 @@ def tile_list_visual_word_hash_kernel(
         def gather_image_codes(c):
             nc.vector.tensor_copy(image_codes[c][:], image_table[:].indirect(entries(image_list, c * CHUNK, CHUNK)))
 
-        for a, queue in enumerate((nc.scalar, nc.sync)):
-            gather_image_rows(rows[a][:, PASS:], 2 * a)
-            gather_word_rows(a)
-            move_scale_rows(queue, planes[a], rows[a])
+        gather_word_rows()
+        gather_image_rows(rows[0][:, S:], 0)
+        move_scale_rows(nc.scalar, planes[0], rows[0])
+        gather_image_rows(rows[1][:], 2)
+        move_scale_rows(nc.sync, planes[1], rows[1])
         gather_word_codes(0)
         for h in range(2):
             nc.vector.tensor_copy(
@@ -267,8 +269,8 @@ def tile_list_visual_word_hash_kernel(
             half_slots(0, [t], t)
         half_slots(1, [0], 4)
         interleaving_root(0, 0, 2 * P)
-        half_slots(1, [1], 0)
-        half_slots(1, [2, 3], 1)
+        half_slots(1, [1], 5)
+        half_slots(1, [2, 3], 6)
         scalar_slot(1, 0)
         interleaving_root(0, 2 * P, 2 * P)
         for k in range(PACK):

@@ -82,7 +82,7 @@ def tile_list_visual_word_hash_kernel(
         nc.vector.memset(word_table_rows[0:ROWS_AT].bitcast(I32), 0)
         nc.vector.memset(image_table_rows[0:ROWS_AT].bitcast(I32), 0)
         for plane in planes + [wb_plane]:
-            nc.gpsimd.memset(plane[:].bitcast(I32), 0)
+            nc.vector.memset(plane[:].bitcast(I32), 0)
         nc.scalar.dma_start(out=word_table_rows[ROWS_AT:P].bitcast(I32), in_=tab_scales[0].bitcast(I32))
         nc.scalar.dma_start(out=image_table_rows[ROWS_AT:P].bitcast(I32), in_=tab2_scales[0].bitcast(I32))
         nc.sync.dma_start(out=word_table[:].bitcast(I32), in_=tab_words[0].rearrange("p c t -> p (c t)").bitcast(I32))

from contextlib import ExitStack

import concourse.mybir as mybir

K, T, T2, S, S2, N = 512, 2048, 4096, 1024, 1536, 512
FLOPS = 2 * K * S * S2 + 2 * 2 * S * N * S2

F32 = mybir.dt.float32
BF16 = mybir.dt.bfloat16
I32 = mybir.dt.int32
U32 = mybir.dt.uint32
U16 = mybir.dt.uint16
U8 = mybir.dt.uint8
FP8X4 = mybir.dt.float8_e4m3fn_x4
FP4X4 = mybir.dt.float4_e2m1fn_x4
ACT = mybir.ActivationFunctionType
ALU = mybir.AluOpType

P = 128
PACK = 4
PASS = P * PACK
PASSES = S // PASS
CHUNK = 512
CHUNKS = S2 // CHUNK
ROW_BLOCKS = N // P
LIST_ROWS = 16
QUAD = 32
ROWS_AT = P - K // 32
ALIGN = 64
RUN = 4
UNIT = PACK * CHUNK
BLOCK = PACK * P
HALF = UNIT // 2
HALF_BYTES = 4 * HALF
SEAM = PACK * T2 + PACK * PASS
RESULTS_AT = 24 * 1024
RESULTS_END = RESULTS_AT + 4 * ROW_BLOCKS * S2
RING_AT = RESULTS_END - 4 * HALF_BYTES
SLOT_BANKS = [None, [7, 0, 1, 2], [3, 4, 5, 6]]
PRODUCT_BANKS = [[0, 1, 2, 3], [4, 5, 6, 7], [0, 1, 2, 7]]
SUM_BANKS = [3, 4, 0, 5, 1, 6, 2, 7]


def move_scale_rows(queue, plane, rows):
    for r in range(PACK):
        queue.dma_start(out=plane[r:P:QUAD].bitcast(I32), in_=rows[ROWS_AT + r : P : PACK].bitcast(I32))


def entries(list_tile, first, count):
    return list_tile[:, first // LIST_ROWS : (first + count) // LIST_ROWS]


def tile_list_visual_word_hash_kernel(
    tc, tab_words, tab_scales, tab2_words, tab2_scales, offs, offs2, wt, wb_words, wb_scales, wd, b, out
):
    nc = tc.nc
    with ExitStack() as ctx:
        held = ctx.enter_context(tc.tile_pool(name="held", bufs=1))
        placed = ctx.enter_context(tc.tile_pool(name="placed", bufs=1))
        psum = ctx.enter_context(tc.psum_pool(name="psum", bufs=1))

        def bank(number, shape):
            return psum.tile(shape, F32, name="bank%d" % number)

        def place(shape, dtype, name, offset):
            return placed.tile(shape, dtype, name=name, align_bytes=ALIGN, offset=offset)

        word_list = held.tile([P, S // LIST_ROWS], U16, name="word_list")
        image_list = held.tile([P, S2 // LIST_ROWS], U16, name="image_list")
        nc.sync.dma_start(word_list[:], offs)
        nc.sync.dma_start(image_list[:], offs2)

        word_table_rows = held.tile([P, T], U8, name="word_table_rows", align_bytes=ALIGN)
        image_table_rows = held.tile([P, T2], U8, name="image_table_rows", align_bytes=ALIGN)
        word_table = held.tile([P, T], U32, name="word_table", align_bytes=ALIGN)
        image_table = place([P, T2], U32, "image_table", 0)
        planes = [
            held.tile([P, width], U8, name="planes%d" % k, align_bytes=ALIGN)
            for k, width in enumerate((S + 2 * CHUNK, CHUNK))
        ]
        wb_plane = held.tile([P, PASSES, N], U8, name="wb_plane", align_bytes=ALIGN)
        nc.vector.memset(word_table_rows[0:ROWS_AT].bitcast(I32), 0)
        nc.vector.memset(image_table_rows[0:ROWS_AT].bitcast(I32), 0)
        for plane in planes + [wb_plane]:
            nc.vector.memset(plane[:].bitcast(I32), 0)
        nc.scalar.dma_start(out=word_table_rows[ROWS_AT:P].bitcast(I32), in_=tab_scales[0].bitcast(I32))
        nc.scalar.dma_start(out=image_table_rows[ROWS_AT:P].bitcast(I32), in_=tab2_scales[0].bitcast(I32))
        nc.sync.dma_start(out=word_table[:].bitcast(I32), in_=tab_words[0].rearrange("p c t -> p (c t)").bitcast(I32))
        nc.sync.dma_start(out=image_table[:].bitcast(I32), in_=tab2_words[0].rearrange("p c t -> p (c t)").bitcast(I32))

        weight_tile = place([P, 2 * ALIGN // 4], F32, "weight", SEAM - ALIGN)
        weight = weight_tile[:, 0 : PASSES * PACK].rearrange("p (a t) -> p a t", a=PASSES)
        weight_sq = held.tile([P, PASSES, PACK], F32, name="weight_sq")
        nc.sync.dma_start(out=weight, in_=wt.rearrange("(a p t) -> p a t", p=P, t=PACK))
        zero = held.tile([P, 1], F32, name="zero")
        zero_root = held.tile([P, 1], F32, name="zero_root")
        nc.vector.memset(zero[:], 0.0)
        nc.scalar.activation(out=zero_root[:], in_=zero[:], func=ACT.Sqrt)
        nc.scalar.activation(out=weight_sq[:], in_=weight, func=ACT.Square, bias=zero_root[:])

        rows = [
            held.tile([P, S + 2 * CHUNK], U8, name="rows0", align_bytes=ALIGN),
            held.tile([P, CHUNK], U8, name="rows1", align_bytes=ALIGN),
        ]
        word_plane = [planes[0][:, a * PASS : (a + 1) * PASS] for a in range(PASSES)]
        image_plane = [planes[0][:, S : S + CHUNK], planes[0][:, S + CHUNK :], planes[1][:]]
        word_codes = {0: held.tile([P, PASS], U32, name="word_codes0", align_bytes=ALIGN)}
        image_codes = {c: held.tile([P, CHUNK], U32, name="image_codes%d" % c, align_bytes=ALIGN) for c in range(2)}

        def gather_word_rows():
            nc.vector.tensor_copy(
                rows[0][:, 0:S].rearrange("p (a t m) -> p a m t", a=PASSES, t=PACK),
                word_table_rows[:].indirect(word_list[:]),
            )

        def gather_word_codes(a):
            nc.vector.tensor_copy(
                word_codes[a][:].rearrange("p (t m) -> p m t", t=PACK),
                word_table[:].indirect(entries(word_list, a * PASS, PASS)),
            )

        def gather_image_rows(dst, c):
            nc.vector.tensor_copy(dst, image_table_rows[:].indirect(entries(image_list, c * CHUNK, dst.shape[1])))

        def gather_image_codes(c):
            nc.vector.tensor_copy(image_codes[c][:], image_table[:].indirect(entries(image_list, c * CHUNK, CHUNK)))

        gather_word_rows()
        gather_image_rows(rows[0][:, S:], 0)
        move_scale_rows(nc.scalar, planes[0], rows[0])
        gather_image_rows(rows[1][:], 2)
        move_scale_rows(nc.sync, planes[1], rows[1])
        gather_word_codes(0)
        for h in range(2):
            nc.vector.tensor_copy(
                image_codes[0][:, h * 2 * P : (h + 1) * 2 * P],
                image_table[:].indirect(entries(image_list, h * 2 * P, 2 * P)),
            )
        gather_image_codes(1)
        word_codes[1] = place([P, PASS], U32, "word_codes1", SEAM - PACK * PASS)
        image_codes[2] = place([P, CHUNK], U32, "image_codes2", SEAM)
        gather_word_codes(1)
        gather_image_codes(2)

        wd_rows = wd.rearrange("(a p t) n -> a p t n", p=P, t=PACK)
        wd_tile = place([P, (4 * HALF_BYTES + PACK * CHUNK + ALIGN) // 4], F32, "wd_raw", RING_AT)
        wd_raw = [
            wd_tile[:, 0:UNIT].rearrange("p (t n) -> p t n", t=PACK),
            held.tile([P, PACK, N], F32, name="wd_raw1")[:],
        ]
        for a in (1, 0):
            nc.sync.dma_start(out=wd_raw[a], in_=wd_rows[a])
        wb_codes = held.tile([P, PASSES, 2 * N], U8, name="wb_codes", align_bytes=ALIGN)
        nc.sync.dma_start(out=wb_codes[:].bitcast(I32), in_=wb_words.rearrange("a p c -> p a c").bitcast(I32))
        wb_rows = wb_scales.rearrange("a q c -> q a c")
        for r in range(PACK):
            nc.sync.dma_start(out=wb_plane[r:P:QUAD].bitcast(I32), in_=wb_rows[r::PACK].bitcast(I32))
        bias = held.tile([P, ROW_BLOCKS], F32, name="bias")
        with nc.allow_non_contiguous_dma(reason="one bias value a partition and block of output rows"):
            nc.sync.dma_start(out=bias[:], in_=b.rearrange("(nb p) -> p nb", p=P))

        z = {
            (a, c): held.tile([P, UNIT], BF16, name="z%d%d" % (a, c), align_bytes=ALIGN)
            for a in range(PASSES)
            for c in range(CHUNKS)
        }
        by_slot = [held.tile([P, UNIT], F32, name="magnitude%d" % c) for c in range(CHUNKS)]
        signed = [held.tile([P, UNIT], F32, name="signed%d" % c, align_bytes=ALIGN) for c in range(2)]
        signed_last = [held.tile([P, HALF], F32, name="signed2", align_bytes=ALIGN)]
        signed_last += [held.tile([P, BLOCK], F32, name="last%d" % k, align_bytes=ALIGN) for k in (2, 3)]
        wd_codes, wd_plane, z_codes, z_plane = {}, {}, {}, {}

        def response(acc, a, t, c, first, width):
            nc.tensor.matmul_mx(
                out=acc,
                lhsT=word_codes[a][:, t * P : (t + 1) * P].bitcast(FP8X4),
                lhsT_scale=word_plane[a][:, t * P : (t + 1) * P],
                rhs=image_codes[c][:, first : first + width].bitcast(FP8X4),
                rhs_scale=image_plane[c][:, first : first + width],
                start=True,
                stop=True,
            )

        def scalar_slot(c, t):
            acc = bank(SLOT_BANKS[c][t], [P, CHUNK])
            response(acc[:], 0, t, c, 0, CHUNK)
            nc.scalar.activation(
                out=by_slot[c][:, t * CHUNK : (t + 1) * CHUNK], in_=acc[:], func=ACT.Abs, scale=weight_sq[:, 0, t : t + 1]
            )

        def interleaving_root(c, first=0, count=CHUNK):
            groups = slice(first // RUN, (first + count) // RUN)
            nc.scalar.activation(
                out=z[0, c][:].rearrange("p (g i t) -> p g t i", i=RUN, t=PACK)[:, groups],
                in_=by_slot[c][:].rearrange("p (t g i) -> p g t i", i=RUN, t=PACK)[:, groups],
                func=ACT.Sqrt,
            )

        def vector_product(c, k, product):
            acc = bank(PRODUCT_BANKS[c][k], [P, PACK, P])
            for t in range(PACK):
                response(acc[:, t, :], 1, t, c, k * P, P)
            nc.vector.tensor_tensor(
                out=product.rearrange("p (j t) -> p j t", t=PACK),
                in0=acc[:].rearrange("p t j -> p j t"),
                in1=weight_sq[:, 1, :].unsqueeze(1).to_broadcast([P, P, PACK]),
                op=ALU.mult,
            )

        def vector_magnitude(x, name, offset):
            m = place([P, x.shape[1]], F32, name, offset)
            nc.vector.scalar_tensor_tensor(out=m[:], in0=x, scalar=-1.0, in1=x, op0=ALU.mult, op1=ALU.max)
            return m

        def plain_root(c, first, m):
            nc.scalar.activation(out=z[1, c][:, first : first + m.shape[1]], in_=m[:], func=ACT.Sqrt)

        def quantize_z(a, c, codes):
            z_codes[a, c] = codes
            z_plane[a, c] = held.tile([P, CHUNK], U8, name="z_plane%d%d" % (a, c), align_bytes=ALIGN)
            nc.vector.quantize_mx(out=codes[:].bitcast(FP8X4), scales=z_plane[a, c][:], in_=z[a, c][:])

        def quantize_update(a, first, rounded, codes):
            plane = held.tile([P, codes.shape[1]], U8, name="wd_plane%d%d" % (a, first), align_bytes=ALIGN)
            nc.vector.quantize_mx(
                out=codes[:].bitcast(FP8X4), scales=plane[:], in_=rounded.rearrange("p n t -> p (n t)")
            )
            for k in range(codes.shape[1] // P):
                wd_codes[a, first + k] = codes[:, k * P : (k + 1) * P]
                wd_plane[a, first + k] = plane[:, k * P : (k + 1) * P]

        def codes_tile(name):
            return held.tile([P, CHUNK], U32, name=name, align_bytes=ALIGN)

        def project(c, nb, number):
            acc = bank(number, [P, CHUNK])
            columns = slice(nb * P, (nb + 1) * P)
            passes = []
            for a in range(PASSES):
                wb_operand = wb_codes[:, a, 2 * nb * P : 2 * (nb + 1) * P].bitcast(FP4X4)
                passes.append((wb_operand, wb_plane[:, a, columns], a))
                passes.append((wd_codes[a, nb].bitcast(FP8X4), wd_plane[a, nb], a))
            for k, (codes, plane, a) in enumerate(passes):
                nc.tensor.matmul_mx(
                    out=acc[:],
                    lhsT=codes,
                    lhsT_scale=plane,
                    rhs=z_codes[a, c][:].bitcast(FP8X4),
                    rhs_scale=z_plane[a, c][:],
                    start=(k == 0),
                    stop=(k == len(passes) - 1),
                )
            return acc

        def half_slots(h, slots, number):
            acc = bank(number, [P, len(slots), 2 * P])
            for u, t in enumerate(slots):
                response(acc[:, u], 0, t, 0, h * 2 * P, 2 * P)
            for u, t in enumerate(slots):
                first = t * CHUNK + h * 2 * P
                nc.scalar.activation(
                    out=by_slot[0][:, first : first + 2 * P],
                    in_=acc[:, u],
                    func=ACT.Abs,
                    scale=weight_sq[:, 0, t : t + 1],
                )

        for t in range(PACK):
            half_slots(0, [t], t)
        half_slots(1, [0], 4)
        interleaving_root(0, 0, 2 * P)
        half_slots(1, [1], 5)
        half_slots(1, [2, 3], 6)
        scalar_slot(1, 0)
        interleaving_root(0, 2 * P, 2 * P)
        for k in range(PACK):
            vector_product(0, k, signed[0][:, k * BLOCK : (k + 1) * BLOCK])
        for t in range(1, PACK):
            scalar_slot(1, t)
        for k in range(PACK):
            vector_product(1, k, signed[1][:, k * BLOCK : (k + 1) * BLOCK])
        scalar_slot(2, 0)
        scalar_slot(2, 1)
        vector_product(2, 0, signed_last[0][:, 0:BLOCK])
        scalar_slot(2, 2)
        vector_product(2, 1, signed_last[0][:, BLOCK:])
        scalar_slot(2, 3)
        vector_product(2, 2, signed_last[1][:])
        vector_product(2, 3, signed_last[2][:])
        interleaving_root(1)
        interleaving_root(2)

        grouped = place([P, PASSES, N, PACK], BF16, "grouped", 0)
        for a, h in ((1, 0), (0, 0), (0, 1)):
            nc.gpsimd.tensor_scalar(
                out=grouped[:, a, h * 2 * P : (h + 1) * 2 * P],
                in0=wd_raw[a][:, :, h * 2 * P : (h + 1) * 2 * P].rearrange("p t n -> p n t"),
                scalar1=1.0,
                scalar2=0.0,
                op0=ALU.mult,
                op1=ALU.add,
            )

        first_magnitude = held.tile([P, HALF], F32, name="first_magnitude")
        nc.vector.tensor_reduce(
            out=first_magnitude[:],
            in_=signed[0][:, 0:HALF].unsqueeze(2),
            axis=mybir.AxisListType.X,
            op=ALU.max,
            apply_absolute_value=True,
        )
        quantize_z(0, 0, place([P, CHUNK], U32, "z_codes00", RESULTS_END))
        quantize_update(0, 0, grouped[:, 0], place([P, N], U32, "wd_codes0", RESULTS_END + PACK * CHUNK))
        quantize_z(0, 1, codes_tile("z_codes01"))
        for c in range(2):
            for h in range(2):
                x = signed[c][:, h * HALF : (h + 1) * HALF]
                at = RING_AT + (2 * c + h) * HALF_BYTES
                m = vector_magnitude(x, "ring%d%d" % (c, h), at) if c or h else first_magnitude
                plain_root(c, h * HALF, m)
        quantize_z(1, 0, codes_tile("z_codes10"))
        for k in range(2):
            x = signed_last[0][:, k * BLOCK : (k + 1) * BLOCK]
            plain_root(2, k * BLOCK, vector_magnitude(x, "ring2%d" % k, RING_AT + HALF_BYTES + k * 4 * BLOCK))
        for k in (2, 3):
            m = vector_magnitude(signed_last[k - 1][:], "ring2%d" % k, RING_AT + 2 * HALF_BYTES + (k - 2) * 4 * BLOCK)
            plain_root(2, k * BLOCK, m)
        quantize_update(1, 0, grouped[:, 1, 0 : 2 * P], held.tile([P, 2 * P], U32, name="last2", align_bytes=ALIGN))
        quantize_z(1, 1, codes_tile("z_codes11"))
        rounded = held.tile([P, 2 * P, PACK], BF16, name="last3", align_bytes=ALIGN)
        nc.vector.tensor_copy(
            out=rounded[:].rearrange("p (g i) t -> p g t i", i=RUN),
            in_=wd_raw[1][:, :, 2 * P :].rearrange("p t (g i) -> p g t i", i=RUN),
        )
        quantize_z(0, 2, codes_tile("z11"))
        quantize_update(1, 2, rounded[:], held.tile([P, 2 * P], U32, name="wd_codes12", align_bytes=ALIGN))
        quantize_z(1, 2, codes_tile("z_codes12"))

        pieces = [(c, nb) for first in (0, 2) for c in range(2) for nb in (first, first + 1)]
        pieces = pieces + [(2, nb) for nb in range(ROW_BLOCKS)]
        sum_banks = SUM_BANKS
        y = [project(c, nb, number) for number, (c, nb) in zip(sum_banks, pieces)]

        results = place([P, len(pieces) * CHUNK], F32, "results", RESULTS_AT)
        cuts = {0: [0, P, CHUNK]}
        for k, (c, nb) in enumerate(pieces):
            if k >= len(y):
                y.append(project(c, nb, sum_banks[k - len(sum_banks)]))
            edges = cuts.get(k, [0, CHUNK])
            for first, last in zip(edges, edges[1:]):
                queue = nc.scalar if k % 2 == 1 and last == CHUNK else nc.sync
                result = results[:, k * CHUNK + first : k * CHUNK + last]
                nc.scalar.activation(out=result, in_=y[k][:, first:last], func=ACT.Tanh, bias=bias[:, nb : nb + 1])
                queue.dma_start(out=out[nb * P : (nb + 1) * P, c * CHUNK + first : c * CHUNK + last], in_=result)
